import numpy as np
import ml_dtypes


def mxq(x, axis, fmt="e4m3"):
    dtype, down = {"e4m3": (ml_dtypes.float8_e4m3fn, 7), "e5m2": (ml_dtypes.float8_e5m2, 14)}[fmt]
    v = np.moveaxis(np.asarray(x, np.float32).astype(ml_dtypes.bfloat16).astype(np.float64), axis, -1)
    blocks = v.reshape(v.shape[:-1] + (-1, 32))
    amax = np.abs(blocks).max(-1, keepdims=True)
    byte = np.maximum(np.where(amax > 0, np.frexp(amax)[1] - 1 + 127, 0) - down, 1)
    scale = np.exp2(byte - 127.0)
    codes = (blocks / scale).astype(np.float32).astype(dtype).astype(np.float64)
    return np.moveaxis((codes * scale).reshape(v.shape), -1, axis)


WIDE = False


def mx_kscale(k):
    if not WIDE:
        return np.ones(k)
    levels = np.array([10, -10, 5, -5, 0])
    if k % 512:
        return np.exp2(np.random.permutation(np.resize(levels, k // 32))).repeat(32)
    a = np.empty((k // 512, 16))
    for p in range(k // 512):
        a[p, :8] = np.random.permutation(np.resize(levels, 8))
        for g in range(8):
            far = levels[np.abs(levels - a[p, g]) >= 10]
            a[p, g + 8] = far[np.random.randint(len(far))]
    return np.exp2(a.ravel()).repeat(32)


def f64(x):
    return np.asarray(x).astype(np.float64)


def striped(idx):
    return np.tile(idx.reshape(-1, 16).T, (8, 1)).astype(np.uint16)


def unstriped(offs):
    return offs[:16].T.reshape(-1).astype(np.int64)


def striped8(idx):
    return np.concatenate([x.reshape(-1, 16).T for x in idx]).astype(np.uint16)


def runs(offs, k):
    lists = np.stack([offs[16 * r : 16 * r + 16].T.reshape(-1) for r in range(8)]).astype(np.int64)
    return lists[np.arange(k) % 512 // 64]


def pack_weight(w):
    k, n = w.shape
    w = f64(np.asarray(w, np.float32).astype(ml_dtypes.bfloat16)).reshape(k // 32, 32, n)
    amax = np.abs(w).max(1)
    byte = np.clip(np.where(amax > 0, np.frexp(amax)[1] - 1 + 127 - 7, 1), 1, 254)
    scaled = (w * np.exp2(127.0 - byte)[:, None, :]).reshape(k, n).astype(np.float32)
    words = np.ascontiguousarray(scaled.reshape(k // 512, 128, 4, n).transpose(0, 1, 3, 2)).astype(ml_dtypes.float8_e4m3fn).view(np.uint8)
    return words, np.ascontiguousarray(byte.astype(np.uint8).reshape(k // 512, 16, n))


def unpack_weight(words, scales):
    g, p, n, _ = words.shape
    vals = np.ascontiguousarray(words).view(ml_dtypes.float8_e4m3fn).astype(np.float64) * np.repeat(np.exp2(scales.astype(np.float64) - 127.0), 8, axis=1)[..., None]
    return vals.transpose(0, 1, 3, 2).reshape(g * 512, n)


def gelu(v):
    return 0.5 * v * (1.0 + np.tanh(np.sqrt(2.0 / np.pi) * (v + 0.044715 * v**3)))

def planes(y):
    n, m = y.shape
    v = y.astype(np.float32).astype(ml_dtypes.bfloat16).astype(np.float64).reshape(n // 32, 32, m)
    top = np.abs(v).max(1)
    byte = np.clip(np.where(top > 0, np.frexp(top)[1] - 1 + 127 - 7, 1), 1, 254)
    codes = (v * np.exp2(127.0 - byte)[:, None, :]).reshape(n, m).astype(np.float32).astype(ml_dtypes.float8_e4m3fn).view(np.uint8)
    words = codes.reshape(n // 512, 128, 4, m).transpose(0, 1, 3, 2)
    return np.ascontiguousarray(words), np.ascontiguousarray(byte.astype(np.uint8).reshape(n // 512, 16, m))


K, T, S, V, N, H = 512, 2048, 512, 256, 512, 512


def setup_inputs():
    n = np.random.standard_normal
    s = mx_kscale(K)[:, None]
    u = mx_kscale(H)
    packed_xT = pack_weight(n((K, T)) * s)
    packed_w2 = pack_weight(n((H, N)) / np.sqrt(H) / u[:, None])
    perm = np.stack([np.random.permutation(S) for _ in range(8)])
    return {
        "x_words": packed_xT[0],
        "x_scales": packed_xT[1],
        "w1": (n((K, H)) / np.sqrt(K) / s * u).astype(np.float32),
        "wa": np.repeat(np.random.uniform(0.3, 1.2, (8, V)), 64, axis=0).astype(np.float32),
        "wb": np.repeat(np.random.uniform(0.3, 1.2, (8, V)), 64, axis=0).astype(np.float32),
        "w2_words": packed_w2[0],
        "w2_scales": packed_w2[1],
        "offs": striped(np.random.permutation(T)[:S]),
        "la": striped8(perm[:, :V]),
        "lb": striped8(perm[:, V:]),
    }


def reference(x_words, x_scales, w1, wa, wb, w2_words, w2_scales, offs, la, lb):
    xq = unpack_weight(x_words, x_scales)[:, unstriped(offs)]
    y = mxq(f64(w1), 0, "e4m3").T @ xq
    b = (y[np.arange(H)[:, None], runs(lb, H)]) * f64(wb)
    a = (gelu(y[np.arange(H)[:, None], runs(la, H)])) * f64(wa)
    p = np.zeros((H, S))
    p[np.arange(H)[:, None], runs(la, H)] = a
    z = p.copy()
    z[np.arange(H)[:, None], runs(lb, H)] = b
    out_0 = unpack_weight(w2_words, w2_scales).T @ mxq(z, 0, "e4m3")
    return (out_0,) + planes(out_0)

@@ -1,0 +1,236 @@
+from contextlib import ExitStack
+
+import concourse.mybir as mybir
+
+K, T, S, V, N, H = 512, 2048, 512, 256, 512, 512
+FLOPS = 2 * K * H * S + 2 * H * N * S
+
+F32 = mybir.dt.float32
+BF16 = mybir.dt.bfloat16
+I32 = mybir.dt.int32
+U32 = mybir.dt.uint32
+U16 = mybir.dt.uint16
+U8 = mybir.dt.uint8
+FP8X4 = mybir.dt.float8_e4m3fn_x4
+GELU = mybir.ActivationFunctionType.Gelu_apprx_tanh
+MULT = mybir.AluOpType.mult
+
+P = 128
+PACK = 4
+QUADS = 4
+CHUNK = 128
+CHUNKS = S // CHUNK
+
+
+def tile_picked_tworoute_gelu_po_kernel(
+    tc, x_words, x_scales, w1, wa, wb, w2_words, w2_scales, offs, la, lb, out_0, out_1, out_2
+):
+    nc = tc.nc
+    with ExitStack() as ctx:
+        keep = ctx.enter_context(tc.tile_pool(name="keep", bufs=1))
+        shared = ctx.enter_context(tc.tile_pool(name="shared", bufs=1))
+        psum = ctx.enter_context(tc.psum_pool(name="psum", bufs=8))
+
+        def mx(out, w_codes, w_scales, w_cols, a_codes, a_scales, a_cols):
+            nc.tensor.matmul_mx(
+                out=out,
+                lhsT=w_codes[:, w_cols].bitcast(FP8X4),
+                lhsT_scale=w_scales[:, w_cols],
+                rhs=a_codes[:, a_cols].bitcast(FP8X4),
+                rhs_scale=a_scales[:, a_cols],
+                start=True,
+                stop=True,
+            )
+
+        x_scale_table = shared.tile([P, T], U8, align_bytes=64, offset=4 * T)
+        nc.vector.memset(x_scale_table[:, 0 : T // 2].bitcast(I32), 0)
+        nc.gpsimd.memset(x_scale_table[:, T // 2 : T].bitcast(I32), 0)
+        w2_scale_raw = keep.tile([P, N], U8, align_bytes=64)
+        nc.gpsimd.memset(w2_scale_raw[:].bitcast(I32), 0)
+        warm = keep.tile([P, 8], F32)
+        nc.gpsimd.memset(warm[:, 0:1], 0.0)
+        nc.scalar.activation(out=warm[:, 1:2], in_=warm[:, 0:1], func=GELU)
+
+        w1_rows = w1.rearrange("(p j) c -> p j c", j=PACK)
+        half = H // 2
+        w1_raw = [keep.tile([P, PACK, half], F32, name=f"w1_raw{h}") for h in range(2)]
+        offs_t = keep.tile([P, S // 16], U16)
+        la_t = keep.tile([P, V // 16], U16)
+        lb_t = keep.tile([P, V // 16], U16)
+        x_word_table = shared.tile([P, T], U32, align_bytes=64, offset=0)
+        wa_t = keep.tile([P, V], F32)
+        wb_t = keep.tile([P, V], F32)
+        w2_word_raw = keep.tile([P, N], I32, align_bytes=64)
+
+        nc.sync.dma_start(out=w1_raw[0][:], in_=w1_rows[:, :, 0:half])
+        nc.sync.dma_start(out=offs_t[:], in_=offs)
+        for q in range(QUADS):
+            nc.sync.dma_start(
+                out=x_scale_table[32 * q : 32 * q + 4, :].bitcast(I32),
+                in_=x_scales[0, 4 * q : 4 * q + 4, :].bitcast(I32),
+            )
+        nc.sync.dma_start(out=w1_raw[1][:], in_=w1_rows[:, :, half:H])
+        nc.sync.dma_start(
+            out=x_word_table[:].bitcast(I32), in_=x_words[0].rearrange("p c r -> p (c r)").bitcast(I32)
+        )
+        nc.sync.dma_start(out=lb_t[:], in_=lb)
+        nc.sync.dma_start(out=la_t[:], in_=la)
+        nc.sync.dma_start(out=w2_word_raw[:], in_=w2_words[0].rearrange("p c r -> p (c r)").bitcast(I32))
+        nc.sync.dma_start(out=wb_t[:], in_=wb.rearrange("(p t) v -> p t v", t=PACK)[:, 0, :])
+        for q in range(QUADS):
+            queue = nc.sync if q < 2 else nc.gpsimd
+            queue.dma_start(
+                out=w2_scale_raw[32 * q : 32 * q + 4, :].bitcast(I32),
+                in_=w2_scales[0, 4 * q : 4 * q + 4, :].bitcast(I32),
+            )
+        nc.sync.dma_start(out=wa_t[:], in_=wa.rearrange("(p t) v -> p t v", t=PACK)[:, 0, :])
+
+        w1_codes = keep.tile([P, H], U32, align_bytes=64)
+        w1_scales = keep.tile([P, H], U8, align_bytes=64)
+        hm = P // 2
+        w1_bf = [
+            keep.tile([P, PACK, hm * PACK], BF16, name="w1_bf0", align_bytes=64),
+            shared.tile([P, PACK, hm * PACK], BF16, name="w1_bf1", align_bytes=64, offset=4 * T),
+        ]
+        x_scale_pick = keep.tile([P, S], U8, align_bytes=64)
+        x_word_pick = keep.tile([P, S], U32, align_bytes=64)
+
+        def round_w1(h, copy):
+            copy(
+                out=w1_bf[h][:].rearrange("p t (m j) -> p m t j", j=PACK),
+                in_=w1_raw[h][:].rearrange("p j (m t) -> p m t j", t=PACK),
+            )
+
+        def quantise_w1(h):
+            for t in range(PACK):
+                cols = slice(P * t + hm * h, P * t + hm * (h + 1))
+                nc.vector.quantize_mx(
+                    out=w1_codes[:, cols].bitcast(FP8X4), scales=w1_scales[:, cols], in_=w1_bf[h][:, t, :]
+                )
+
+        round_w1(0, nc.scalar.copy)
+        nc.vector.tensor_copy(out=x_scale_pick[:], in_=x_scale_table[:].indirect(offs_t[:]))
+        round_w1(1, nc.vector.tensor_copy)
+        quantise_w1(0)
+        quantise_w1(1)
+
+        hs = S // 2
+        for h in range(2):
+            nc.vector.tensor_copy(
+                out=x_word_pick[:, hs * h : hs * (h + 1)],
+                in_=x_word_table[:].indirect(offs_t[:, hs // 16 * h : hs // 16 * (h + 1)]),
+            )
+
+        w2_codes = shared.tile([P, N], I32, align_bytes=64, offset=0)
+        w2_scale_t = shared.tile([P, N], U8, align_bytes=64, offset=4 * N)
+        nc.vector.tensor_copy(
+            out=w2_codes[:].rearrange("p (t m) -> p m t", t=PACK),
+            in_=w2_word_raw[:].rearrange("p (m t) -> p m t", t=PACK),
+        )
+        nc.vector.tensor_copy(
+            out=w2_scale_t[:].rearrange("p (t m) -> p m t", t=PACK),
+            in_=w2_scale_raw[:].rearrange("p (m t) -> p m t", t=PACK),
+        )
+
+        y = [keep.tile([P, S], F32, name=f"y{t}") for t in range(PACK)]
+        for t in range(PACK):
+            pieces = 2 if t == 0 else 1
+            width = S // pieces
+            for i in range(pieces):
+                cols = slice(width * i, width * (i + 1))
+                bank = psum.tile([P, S], F32, name="bank")
+                mx(bank[:, 0:width], w1_codes, w1_scales, slice(P * t, P * (t + 1)), x_word_pick, x_scale_pick, cols)
+                nc.scalar.copy(out=y[t][:, cols], in_=bank[:, 0:width])
+
+        z = [keep.tile([P, S], F32, name=f"z{t}") for t in range(PACK)]
+        ya = [keep.tile([P, V], F32, name=f"ya{t}") for t in range(PACK)]
+        ga = [keep.tile([P, V], F32, name=f"ga{t}") for t in range(PACK)]
+        yb = [keep.tile([P, V], F32, name=f"yb{t}") for t in range(PACK)]
+        z_bf = [keep.tile([P, CHUNK, PACK], BF16, name=f"z_bf{c}", align_bytes=64) for c in range(CHUNKS)]
+
+        def fetch_b(t):
+            nc.vector.tensor_copy(out=yb[t][:], in_=y[t][:].indirect(lb_t[:]))
+
+        def fetch_a(t):
+            nc.vector.tensor_copy(out=ya[t][:], in_=y[t][:].indirect(la_t[:]))
+            nc.scalar.activation(out=ga[t][:], in_=ya[t][:], func=GELU)
+
+        def put_b(t):
+            nc.vector.tensor_tensor(out=z[t][:].indirect(lb_t[:]), in0=yb[t][:], in1=wb_t[:], op=MULT)
+
+        def put_a(t):
+            nc.vector.tensor_tensor(out=z[t][:].indirect(la_t[:]), in0=ga[t][:], in1=wa_t[:], op=MULT)
+
+        def round_z(t):
+            for c in range(CHUNKS):
+                src = z[t][:, CHUNK * c : CHUNK * (c + 1)]
+                if t == PACK - 2 and c < CHUNKS // 2:
+                    nc.scalar.copy(out=z_bf[c][:, :, t : t + 2], in_=src.unsqueeze(2).to_broadcast([P, CHUNK, 2]))
+                elif t == PACK - 1 and c < CHUNKS // 2:
+                    nc.vector.tensor_copy(out=z_bf[c][:, :, t], in_=src)
+                else:
+                    nc.scalar.copy(out=z_bf[c][:, :, t], in_=src)
+
+        fetch_b(0)
+        fetch_a(0)
+        for t in range(PACK):
+            put_b(t)
+            if t + 1 < PACK:
+                fetch_b(t + 1)
+            put_a(t)
+            if t + 1 < PACK:
+                fetch_a(t + 1)
+            round_z(t)
+
+        z_codes = keep.tile([P, S], U32, align_bytes=64)
+        z_scales = keep.tile([P, S], U8, align_bytes=64)
+        for c in range(CHUNKS):
+            cols = slice(CHUNK * c, CHUNK * (c + 1))
+            nc.vector.quantize_mx(
+                out=z_codes[:, cols].bitcast(FP8X4),
+                scales=z_scales[:, cols],
+                in_=z_bf[c][:].rearrange("p n t -> p (n t)"),
+            )
+
+        out_rows = out_0.rearrange("(p t) j -> p t j", t=PACK)
+        out_words = out_1[0].rearrange("p c r -> p (c r)").bitcast(I32)
+        o_codes = keep.tile([P, S], U32, align_bytes=64)
+        o_scales = keep.tile([P, S], U8, align_bytes=64)
+        o_bf = [keep.tile([P, CHUNK, PACK], BF16, name=f"o_bf{c}", align_bytes=64) for c in range(CHUNKS)]
+
+        def quantise_out(c):
+            cols = slice(CHUNK * c, CHUNK * (c + 1))
+            nc.vector.quantize_mx(
+                out=o_codes[:, cols].bitcast(FP8X4),
+                scales=o_scales[:, cols],
+                in_=o_bf[c][:].rearrange("p n t -> p (n t)"),
+            )
+
+        for c in range(CHUNKS):
+            cols = slice(CHUNK * c, CHUNK * (c + 1))
+            o_f = keep.tile([P, PACK, CHUNK], F32, name=f"o_f{c}")
+            for pair in range(2):
+                bank = psum.tile([P, S], F32, name="bank")
+                for u in range(2):
+                    t = 2 * pair + u
+                    mx(bank[:, CHUNK * u : CHUNK * (u + 1)], w2_codes, w2_scale_t, slice(P * t, P * (t + 1)), z_codes, z_scales, cols)
+                nc.scalar.copy(
+                    out=o_f[:, 2 * pair : 2 * pair + 2, :].rearrange("p t n -> p (t n)"), in_=bank[:, 0 : 2 * CHUNK]
+                )
+            nc.sync.dma_start(out=out_rows[:, :, cols], in_=o_f[:])
+            nc.vector.tensor_copy(
+                out=o_bf[c][:].rearrange("p (g i) t -> p g t i", i=4),
+                in_=o_f[:].rearrange("p t (g i) -> p g t i", i=4),
+            )
+            if c > 0:
+                quantise_out(c - 1)
+        last = CHUNK * (CHUNKS - 1)
+        nc.sync.dma_start(out=out_words[:, 0:last], in_=o_codes[:, 0:last].bitcast(I32))
+        quantise_out(CHUNKS - 1)
+        nc.sync.dma_start(out=out_words[:, last:S], in_=o_codes[:, last:S].bitcast(I32))
+        for q in range(QUADS):
+            queue = nc.scalar if q % 2 == 0 else nc.sync
+            queue.dma_start(
+                out=out_2[0, 4 * q : 4 * q + 4, :].bitcast(I32),
+                in_=o_scales[32 * q : 32 * q + 4, :].bitcast(I32),
+            )

@@ -42,7 +42,7 @@ def tile_picked_tworoute_gelu_po_kernel(
                 stop=True,
             )
 
-        x_scale_table = shared.tile([P, T], U8, align_bytes=64, offset=4 * T)
+        x_scale_table = keep.tile([P, T], U8, align_bytes=64)
         nc.vector.memset(x_scale_table[:, 0 : T // 2].bitcast(I32), 0)
         nc.gpsimd.memset(x_scale_table[:, T // 2 : T].bitcast(I32), 0)
         w2_scale_raw = keep.tile([P, N], U8, align_bytes=64)
@@ -88,10 +88,7 @@ def tile_picked_tworoute_gelu_po_kernel(
         w1_codes = keep.tile([P, H], U32, align_bytes=64)
         w1_scales = keep.tile([P, H], U8, align_bytes=64)
         hm = P // 2
-        w1_bf = [
-            keep.tile([P, PACK, hm * PACK], BF16, name="w1_bf0", align_bytes=64),
-            shared.tile([P, PACK, hm * PACK], BF16, name="w1_bf1", align_bytes=64, offset=4 * T),
-        ]
+        w1_bf = [keep.tile([P, PACK, hm * PACK], BF16, name=f"w1_bf{h}", align_bytes=64) for h in range(2)]
         x_scale_pick = keep.tile([P, S], U8, align_bytes=64)
         x_word_pick = keep.tile([P, S], U32, align_bytes=64)
 
@@ -110,7 +107,7 @@ def tile_picked_tworoute_gelu_po_kernel(
 
         round_w1(0, nc.scalar.copy)
         nc.vector.tensor_copy(out=x_scale_pick[:], in_=x_scale_table[:].indirect(offs_t[:]))
-        round_w1(1, nc.vector.tensor_copy)
+        round_w1(1, nc.scalar.copy)
         quantise_w1(0)
         quantise_w1(1)
 
@@ -134,10 +131,10 @@ def tile_picked_tworoute_gelu_po_kernel(
 
         y = [keep.tile([P, S], F32, name=f"y{t}") for t in range(PACK)]
         for t in range(PACK):
-            pieces = 2 if t == 0 else 1
-            width = S // pieces
-            for i in range(pieces):
-                cols = slice(width * i, width * (i + 1))
+            edges = (0, 256, 384, 512) if t == 0 else (0, S)
+            for lo, hi in zip(edges, edges[1:]):
+                cols = slice(lo, hi)
+                width = hi - lo
                 bank = psum.tile([P, S], F32, name="bank")
                 mx(bank[:, 0:width], w1_codes, w1_scales, slice(P * t, P * (t + 1)), x_word_pick, x_scale_pick, cols)
                 nc.scalar.copy(out=y[t][:, cols], in_=bank[:, 0:width])
@@ -198,12 +195,12 @@ def tile_picked_tworoute_gelu_po_kernel(
         o_scales = keep.tile([P, S], U8, align_bytes=64)
         o_bf = [keep.tile([P, CHUNK, PACK], BF16, name=f"o_bf{c}", align_bytes=64) for c in range(CHUNKS)]
 
-        def quantise_out(c):
-            cols = slice(CHUNK * c, CHUNK * (c + 1))
+        def quantise_out(c, lo, hi):
+            cols = slice(CHUNK * c + lo, CHUNK * c + hi)
             nc.vector.quantize_mx(
                 out=o_codes[:, cols].bitcast(FP8X4),
                 scales=o_scales[:, cols],
-                in_=o_bf[c][:].rearrange("p n t -> p (n t)"),
+                in_=o_bf[c][:, lo:hi, :].rearrange("p n t -> p (n t)"),
             )
 
         for c in range(CHUNKS):
@@ -218,15 +215,19 @@ def tile_picked_tworoute_gelu_po_kernel(
                     out=o_f[:, 2 * pair : 2 * pair + 2, :].rearrange("p t n -> p (t n)"), in_=bank[:, 0 : 2 * CHUNK]
                 )
             nc.sync.dma_start(out=out_rows[:, :, cols], in_=o_f[:])
-            nc.vector.tensor_copy(
-                out=o_bf[c][:].rearrange("p (g i) t -> p g t i", i=4),
-                in_=o_f[:].rearrange("p t (g i) -> p g t i", i=4),
-            )
+            parts = 2 if c == CHUNKS - 1 else 1
+            width = CHUNK // parts
+            for i in range(parts):
+                nc.vector.tensor_copy(
+                    out=o_bf[c][:, width * i : width * (i + 1), :].rearrange("p (g i) t -> p g t i", i=4),
+                    in_=o_f[:, :, width * i : width * (i + 1)].rearrange("p t (g i) -> p g t i", i=4),
+                )
             if c > 0:
-                quantise_out(c - 1)
+                quantise_out(c - 1, 0, CHUNK)
         last = CHUNK * (CHUNKS - 1)
         nc.sync.dma_start(out=out_words[:, 0:last], in_=o_codes[:, 0:last].bitcast(I32))
-        quantise_out(CHUNKS - 1)
+        quantise_out(CHUNKS - 1, 0, CHUNK // 2)
+        quantise_out(CHUNKS - 1, CHUNK // 2, CHUNK)
         nc.sync.dma_start(out=out_words[:, last:S], in_=o_codes[:, last:S].bitcast(I32))
         for q in range(QUADS):
             queue = nc.scalar if q % 2 == 0 else nc.sync

@@ -47,9 +47,6 @@ def tile_picked_tworoute_gelu_po_kernel(
         nc.gpsimd.memset(x_scale_table[:, T // 2 : T].bitcast(I32), 0)
         w2_scale_raw = keep.tile([P, N], U8, align_bytes=64)
         nc.gpsimd.memset(w2_scale_raw[:].bitcast(I32), 0)
-        warm = keep.tile([P, 8], F32)
-        nc.gpsimd.memset(warm[:, 0:1], 0.0)
-        nc.scalar.activation(out=warm[:, 1:2], in_=warm[:, 0:1], func=GELU)
 
         w1_rows = w1.rearrange("(p j) c -> p j c", j=PACK)
         half = H // 2
@@ -77,13 +74,13 @@ def tile_picked_tworoute_gelu_po_kernel(
         nc.sync.dma_start(out=la_t[:], in_=la)
         nc.sync.dma_start(out=w2_word_raw[:], in_=w2_words[0].rearrange("p c r -> p (c r)").bitcast(I32))
         nc.sync.dma_start(out=wb_t[:], in_=wb.rearrange("(p t) v -> p t v", t=PACK)[:, 0, :])
+        nc.sync.dma_start(out=wa_t[:], in_=wa.rearrange("(p t) v -> p t v", t=PACK)[:, 0, :])
         for q in range(QUADS):
             queue = nc.sync if q < 2 else nc.gpsimd
             queue.dma_start(
                 out=w2_scale_raw[32 * q : 32 * q + 4, :].bitcast(I32),
                 in_=w2_scales[0, 4 * q : 4 * q + 4, :].bitcast(I32),
             )
-        nc.sync.dma_start(out=wa_t[:], in_=wa.rearrange("(p t) v -> p t v", t=PACK)[:, 0, :])
 
         w1_codes = keep.tile([P, H], U32, align_bytes=64)
         w1_scales = keep.tile([P, H], U8, align_bytes=64)
@@ -130,7 +127,8 @@ def tile_picked_tworoute_gelu_po_kernel(
         )
 
         y = [keep.tile([P, S], F32, name=f"y{t}") for t in range(PACK)]
-        for t in range(PACK):
+
+        def project(t):
             edges = (0, 256, 384, 512) if t == 0 else (0, S)
             for lo, hi in zip(edges, edges[1:]):
                 cols = slice(lo, hi)
@@ -168,16 +166,16 @@ def tile_picked_tworoute_gelu_po_kernel(
                 else:
                     nc.scalar.copy(out=z_bf[c][:, :, t], in_=src)
 
-        fetch_b(0)
-        fetch_a(0)
         for t in range(PACK):
+            project(t)
+            fetch_b(t)
+            fetch_a(t)
             put_b(t)
-            if t + 1 < PACK:
-                fetch_b(t + 1)
-            put_a(t)
-            if t + 1 < PACK:
-                fetch_a(t + 1)
-            round_z(t)
+            if t > 0:
+                put_a(t - 1)
+                round_z(t - 1)
+        put_a(PACK - 1)
+        round_z(PACK - 1)
 
         z_codes = keep.tile([P, S], U32, align_bytes=64)
         z_scales = keep.tile([P, S], U8, align_bytes=64)
@@ -214,7 +212,10 @@ def tile_picked_tworoute_gelu_po_kernel(
                 nc.scalar.copy(
                     out=o_f[:, 2 * pair : 2 * pair + 2, :].rearrange("p t n -> p (t n)"), in_=bank[:, 0 : 2 * CHUNK]
                 )
-            nc.sync.dma_start(out=out_rows[:, :, cols], in_=o_f[:])
+                if c == 0:
+                    nc.sync.dma_start(out=out_rows[:, 2 * pair : 2 * pair + 2, cols], in_=o_f[:, 2 * pair : 2 * pair + 2, :])
+            if c > 0:
+                nc.sync.dma_start(out=out_rows[:, :, cols], in_=o_f[:])
             parts = 2 if c == CHUNKS - 1 else 1
             width = CHUNK // parts
             for i in range(parts):

@@ -201,27 +201,29 @@ def tile_picked_tworoute_gelu_po_kernel(
                 in_=o_bf[c][:, lo:hi, :].rearrange("p n t -> p (n t)"),
             )
 
+        wide = 2 * CHUNK
+        o_f = [keep.tile([P, PACK, wide], F32, name=f"o_f{h}") for h in range(2)]
         for c in range(CHUNKS):
             cols = slice(CHUNK * c, CHUNK * (c + 1))
-            o_f = keep.tile([P, PACK, CHUNK], F32, name=f"o_f{c}")
+            h, first = divmod(CHUNK * c, wide)
             for pair in range(2):
+                slots = slice(2 * pair, 2 * pair + 2)
                 bank = psum.tile([P, S], F32, name="bank")
                 for u in range(2):
                     t = 2 * pair + u
                     mx(bank[:, CHUNK * u : CHUNK * (u + 1)], w2_codes, w2_scale_t, slice(P * t, P * (t + 1)), z_codes, z_scales, cols)
                 nc.scalar.copy(
-                    out=o_f[:, 2 * pair : 2 * pair + 2, :].rearrange("p t n -> p (t n)"), in_=bank[:, 0 : 2 * CHUNK]
+                    out=o_f[h][:, slots, first : first + CHUNK],
+                    in_=bank[:, 0 : 2 * CHUNK].rearrange("p (t n) -> p t n", t=2),
                 )
-                if c == 0:
-                    nc.sync.dma_start(out=out_rows[:, 2 * pair : 2 * pair + 2, cols], in_=o_f[:, 2 * pair : 2 * pair + 2, :])
-            if c > 0:
-                nc.sync.dma_start(out=out_rows[:, :, cols], in_=o_f[:])
+                if first > 0:
+                    nc.sync.dma_start(out=out_rows[:, slots, wide * h : wide * (h + 1)], in_=o_f[h][:, slots, :])
             parts = 2 if c == CHUNKS - 1 else 1
             width = CHUNK // parts
             for i in range(parts):
                 nc.vector.tensor_copy(
                     out=o_bf[c][:, width * i : width * (i + 1), :].rearrange("p (g i) t -> p g t i", i=4),
-                    in_=o_f[:, :, width * i : width * (i + 1)].rearrange("p t (g i) -> p g t i", i=4),
+                    in_=o_f[h][:, :, first + width * i : first + width * (i + 1)].rearrange("p t (g i) -> p g t i", i=4),
                 )
             if c > 0:
                 quantise_out(c - 1, 0, CHUNK)

@@ -49,8 +49,7 @@ def tile_picked_tworoute_gelu_po_kernel(
         nc.gpsimd.memset(w2_scale_raw[:].bitcast(I32), 0)
 
         w1_rows = w1.rearrange("(p j) c -> p j c", j=PACK)
-        half = H // 2
-        w1_raw = [keep.tile([P, PACK, half], F32, name=f"w1_raw{h}") for h in range(2)]
+        w1_raw = [keep.tile([P, 2, H], F32, name=f"w1_raw{h}") for h in range(2)]
         offs_t = keep.tile([P, S // 16], U16)
         la_t = keep.tile([P, V // 16], U16)
         lb_t = keep.tile([P, V // 16], U16)
@@ -59,54 +58,49 @@ def tile_picked_tworoute_gelu_po_kernel(
         wb_t = keep.tile([P, V], F32)
         w2_word_raw = keep.tile([P, N], I32, align_bytes=64)
 
-        nc.sync.dma_start(out=w1_raw[0][:], in_=w1_rows[:, :, 0:half])
+        nc.sync.dma_start(out=w1_raw[0][:], in_=w1_rows[:, 0:2, :])
         nc.sync.dma_start(out=offs_t[:], in_=offs)
         for q in range(QUADS):
             nc.sync.dma_start(
                 out=x_scale_table[32 * q : 32 * q + 4, :].bitcast(I32),
                 in_=x_scales[0, 4 * q : 4 * q + 4, :].bitcast(I32),
             )
-        nc.sync.dma_start(out=w1_raw[1][:], in_=w1_rows[:, :, half:H])
+        nc.sync.dma_start(out=w1_raw[1][:], in_=w1_rows[:, 2:4, :])
         nc.sync.dma_start(
             out=x_word_table[:].bitcast(I32), in_=x_words[0].rearrange("p c r -> p (c r)").bitcast(I32)
         )
-        nc.sync.dma_start(out=lb_t[:], in_=lb)
-        nc.sync.dma_start(out=la_t[:], in_=la)
-        nc.sync.dma_start(out=w2_word_raw[:], in_=w2_words[0].rearrange("p c r -> p (c r)").bitcast(I32))
-        nc.sync.dma_start(out=wb_t[:], in_=wb.rearrange("(p t) v -> p t v", t=PACK)[:, 0, :])
-        nc.sync.dma_start(out=wa_t[:], in_=wa.rearrange("(p t) v -> p t v", t=PACK)[:, 0, :])
         for q in range(QUADS):
-            queue = nc.sync if q < 2 else nc.gpsimd
-            queue.dma_start(
+            nc.sync.dma_start(
                 out=w2_scale_raw[32 * q : 32 * q + 4, :].bitcast(I32),
                 in_=w2_scales[0, 4 * q : 4 * q + 4, :].bitcast(I32),
             )
+        nc.sync.dma_start(out=w2_word_raw[:], in_=w2_words[0].rearrange("p c r -> p (c r)").bitcast(I32))
+        nc.sync.dma_start(out=lb_t[:], in_=lb)
+        nc.sync.dma_start(out=la_t[:], in_=la)
+        nc.sync.dma_start(out=wb_t[:], in_=wb.rearrange("(p t) v -> p t v", t=PACK)[:, 0, :])
+        nc.sync.dma_start(out=wa_t[:], in_=wa.rearrange("(p t) v -> p t v", t=PACK)[:, 0, :])
 
         w1_codes = keep.tile([P, H], U32, align_bytes=64)
         w1_scales = keep.tile([P, H], U8, align_bytes=64)
-        hm = P // 2
-        w1_bf = [keep.tile([P, PACK, hm * PACK], BF16, name=f"w1_bf{h}", align_bytes=64) for h in range(2)]
+        w1_bf = keep.tile([P, PACK, H], BF16, align_bytes=64)
         x_scale_pick = keep.tile([P, S], U8, align_bytes=64)
         x_word_pick = keep.tile([P, S], U32, align_bytes=64)
 
         def round_w1(h, copy):
             copy(
-                out=w1_bf[h][:].rearrange("p t (m j) -> p m t j", j=PACK),
+                out=w1_bf[:].rearrange("p t (m j) -> p m t j", j=PACK)[:, :, :, 2 * h : 2 * h + 2],
                 in_=w1_raw[h][:].rearrange("p j (m t) -> p m t j", t=PACK),
             )
 
-        def quantise_w1(h):
-            for t in range(PACK):
-                cols = slice(P * t + hm * h, P * t + hm * (h + 1))
-                nc.vector.quantize_mx(
-                    out=w1_codes[:, cols].bitcast(FP8X4), scales=w1_scales[:, cols], in_=w1_bf[h][:, t, :]
-                )
+        def quantise_w1(t):
+            cols = slice(P * t, P * (t + 1))
+            nc.vector.quantize_mx(out=w1_codes[:, cols].bitcast(FP8X4), scales=w1_scales[:, cols], in_=w1_bf[:, t, :])
 
         round_w1(0, nc.scalar.copy)
+        round_w1(1, nc.vector.tensor_copy)
         nc.vector.tensor_copy(out=x_scale_pick[:], in_=x_scale_table[:].indirect(offs_t[:]))
-        round_w1(1, nc.scalar.copy)
-        quantise_w1(0)
-        quantise_w1(1)
+        for t in range(PACK):
+            quantise_w1(t)
 
         hs = S // 2
         for h in range(2):
@@ -212,12 +206,17 @@ def tile_picked_tworoute_gelu_po_kernel(
                 for u in range(2):
                     t = 2 * pair + u
                     mx(bank[:, CHUNK * u : CHUNK * (u + 1)], w2_codes, w2_scale_t, slice(P * t, P * (t + 1)), z_codes, z_scales, cols)
-                nc.scalar.copy(
+                copy = nc.vector.tensor_copy if (c, pair) == (0, 1) else nc.scalar.copy
+                copy(
                     out=o_f[h][:, slots, first : first + CHUNK],
                     in_=bank[:, 0 : 2 * CHUNK].rearrange("p (t n) -> p t n", t=2),
                 )
-                if first > 0:
-                    nc.sync.dma_start(out=out_rows[:, slots, wide * h : wide * (h + 1)], in_=o_f[h][:, slots, :])
+                if c == 0:
+                    nc.sync.dma_start(out=out_rows[:, slots, cols], in_=o_f[0][:, slots, cols])
+                if c == CHUNKS - 1:
+                    nc.sync.dma_start(out=out_rows[:, slots, wide:S], in_=o_f[1][:, slots, :])
+            if c == 1:
+                nc.sync.dma_start(out=out_rows[:, :, cols], in_=o_f[0][:, :, cols])
             parts = 2 if c == CHUNKS - 1 else 1
             width = CHUNK // parts
             for i in range(parts):
@@ -227,8 +226,9 @@ def tile_picked_tworoute_gelu_po_kernel(
                 )
             if c > 0:
                 quantise_out(c - 1, 0, CHUNK)
-        last = CHUNK * (CHUNKS - 1)
-        nc.sync.dma_start(out=out_words[:, 0:last], in_=o_codes[:, 0:last].bitcast(I32))
+            if c == 2:
+                nc.sync.dma_start(out=out_words[:, 0:wide], in_=o_codes[:, 0:wide].bitcast(I32))
+        last = wide
         quantise_out(CHUNKS - 1, 0, CHUNK // 2)
         quantise_out(CHUNKS - 1, CHUNK // 2, CHUNK)
         nc.sync.dma_start(out=out_words[:, last:S], in_=o_codes[:, last:S].bitcast(I32))

@@ -138,14 +138,14 @@ def tile_picked_tworoute_gelu_po_kernel(
         z_bf = [keep.tile([P, CHUNK, PACK], BF16, name=f"z_bf{c}", align_bytes=64) for c in range(CHUNKS)]
 
         def fetch_b(t):
-            nc.vector.tensor_copy(out=yb[t][:], in_=y[t][:].indirect(lb_t[:]))
+            nc.vector.tensor_tensor(out=yb[t][:], in0=y[t][:].indirect(lb_t[:]), in1=wb_t[:], op=MULT)
 
         def fetch_a(t):
             nc.vector.tensor_copy(out=ya[t][:], in_=y[t][:].indirect(la_t[:]))
             nc.scalar.activation(out=ga[t][:], in_=ya[t][:], func=GELU)
 
         def put_b(t):
-            nc.vector.tensor_tensor(out=z[t][:].indirect(lb_t[:]), in0=yb[t][:], in1=wb_t[:], op=MULT)
+            nc.vector.tensor_copy(out=z[t][:].indirect(lb_t[:]), in_=yb[t][:])
 
         def put_a(t):
             nc.vector.tensor_tensor(out=z[t][:].indirect(la_t[:]), in0=ga[t][:], in1=wa_t[:], op=MULT)

@@ -76,8 +76,8 @@ def tile_picked_tworoute_gelu_po_kernel(
             )
         nc.sync.dma_start(out=w2_word_raw[:], in_=w2_words[0].rearrange("p c r -> p (c r)").bitcast(I32))
         nc.sync.dma_start(out=lb_t[:], in_=lb)
-        nc.sync.dma_start(out=la_t[:], in_=la)
         nc.sync.dma_start(out=wb_t[:], in_=wb.rearrange("(p t) v -> p t v", t=PACK)[:, 0, :])
+        nc.sync.dma_start(out=la_t[:], in_=la)
         nc.sync.dma_start(out=wa_t[:], in_=wa.rearrange("(p t) v -> p t v", t=PACK)[:, 0, :])
 
         w1_codes = keep.tile([P, H], U32, align_bytes=64)
@@ -122,33 +122,37 @@ def tile_picked_tworoute_gelu_po_kernel(
 
         y = [keep.tile([P, S], F32, name=f"y{t}") for t in range(PACK)]
 
+        g = [keep.tile([P, S], F32, name=f"g{t}") for t in range(PACK)]
+
         def project(t):
-            edges = (0, 256, 384, 512) if t == 0 else (0, S)
+            edges = ((0, 256, 384, 512), (0, 256, 512), (0, S), (0, S))[t]
             for lo, hi in zip(edges, edges[1:]):
                 cols = slice(lo, hi)
                 width = hi - lo
                 bank = psum.tile([P, S], F32, name="bank")
                 mx(bank[:, 0:width], w1_codes, w1_scales, slice(P * t, P * (t + 1)), x_word_pick, x_scale_pick, cols)
-                nc.scalar.copy(out=y[t][:, cols], in_=bank[:, 0:width])
+                copy = nc.vector.tensor_copy if (t, lo) == (0, 256) else nc.scalar.copy
+                copy(out=y[t][:, cols], in_=bank[:, 0:width])
+
+        def activate(t):
+            nc.scalar.activation(out=g[t][:], in_=y[t][:], func=GELU)
 
         z = [keep.tile([P, S], F32, name=f"z{t}") for t in range(PACK)]
-        ya = [keep.tile([P, V], F32, name=f"ya{t}") for t in range(PACK)]
-        ga = [keep.tile([P, V], F32, name=f"ga{t}") for t in range(PACK)]
-        yb = [keep.tile([P, V], F32, name=f"yb{t}") for t in range(PACK)]
+        a = [keep.tile([P, V], F32, name=f"a{t}") for t in range(PACK)]
+        b = [keep.tile([P, V], F32, name=f"b{t}") for t in range(PACK)]
         z_bf = [keep.tile([P, CHUNK, PACK], BF16, name=f"z_bf{c}", align_bytes=64) for c in range(CHUNKS)]
 
         def fetch_b(t):
-            nc.vector.tensor_tensor(out=yb[t][:], in0=y[t][:].indirect(lb_t[:]), in1=wb_t[:], op=MULT)
+            nc.vector.tensor_tensor(out=b[t][:], in0=y[t][:].indirect(lb_t[:]), in1=wb_t[:], op=MULT)
 
         def fetch_a(t):
-            nc.vector.tensor_copy(out=ya[t][:], in_=y[t][:].indirect(la_t[:]))
-            nc.scalar.activation(out=ga[t][:], in_=ya[t][:], func=GELU)
+            nc.vector.tensor_tensor(out=a[t][:], in0=g[t][:].indirect(la_t[:]), in1=wa_t[:], op=MULT)
 
         def put_b(t):
-            nc.vector.tensor_copy(out=z[t][:].indirect(lb_t[:]), in_=yb[t][:])
+            nc.vector.tensor_copy(out=z[t][:].indirect(lb_t[:]), in_=b[t][:])
 
         def put_a(t):
-            nc.vector.tensor_tensor(out=z[t][:].indirect(la_t[:]), in0=ga[t][:], in1=wa_t[:], op=MULT)
+            nc.vector.tensor_copy(out=z[t][:].indirect(la_t[:]), in_=a[t][:])
 
         def round_z(t):
             for c in range(CHUNKS):
@@ -162,9 +166,14 @@ def tile_picked_tworoute_gelu_po_kernel(
 
         for t in range(PACK):
             project(t)
-            fetch_b(t)
-            fetch_a(t)
+        for t in range(PACK):
+            activate(t)
+        fetch_b(0)
+        for t in range(PACK):
+            if t + 1 < PACK:
+                fetch_b(t + 1)
             put_b(t)
+            fetch_a(t)
             if t > 0:
                 put_a(t - 1)
                 round_z(t - 1)

@@ -18,8 +18,14 @@ MULT = mybir.AluOpType.mult
 P = 128
 PACK = 4
 QUADS = 4
+GROUP = 16
+BANKS = 8
+HALF = S // 2
 CHUNK = 128
 CHUNKS = S // CHUNK
+W1_ON_VECTOR = 88
+Y_EDGES = ((0, HALF, HALF + CHUNK, S), (0, HALF, S), (0, S), (0, S))
+Z_ON_VECTOR = CHUNKS // 2
 
 
 def tile_picked_tworoute_gelu_po_kernel(
@@ -29,7 +35,9 @@ def tile_picked_tworoute_gelu_po_kernel(
     with ExitStack() as ctx:
         keep = ctx.enter_context(tc.tile_pool(name="keep", bufs=1))
         shared = ctx.enter_context(tc.tile_pool(name="shared", bufs=1))
-        psum = ctx.enter_context(tc.psum_pool(name="psum", bufs=8))
+        psum = ctx.enter_context(tc.psum_pool(name="psum", bufs=BANKS))
+        words_at = 0
+        late_at = 4 * T
 
         def mx(out, w_codes, w_scales, w_cols, a_codes, a_scales, a_cols):
             nc.tensor.matmul_mx(
@@ -49,31 +57,29 @@ def tile_picked_tworoute_gelu_po_kernel(
         nc.gpsimd.memset(w2_scale_raw[:].bitcast(I32), 0)
 
         w1_rows = w1.rearrange("(p j) c -> p j c", j=PACK)
-        w1_raw = [keep.tile([P, 2, H], F32, name=f"w1_raw{h}") for h in range(2)]
-        offs_t = keep.tile([P, S // 16], U16)
-        la_t = keep.tile([P, V // 16], U16)
-        lb_t = keep.tile([P, V // 16], U16)
-        x_word_table = shared.tile([P, T], U32, align_bytes=64, offset=0)
+        w1_raw = [keep.tile([P, 2, H], F32, name=f"w1_raw{pair}") for pair in range(2)]
+        offs_t = keep.tile([P, S // GROUP], U16)
+        la_t = keep.tile([P, V // GROUP], U16)
+        lb_t = keep.tile([P, V // GROUP], U16)
+        x_word_table = shared.tile([P, T], U32, align_bytes=64, offset=words_at)
         wa_t = keep.tile([P, V], F32)
         wb_t = keep.tile([P, V], F32)
         w2_word_raw = keep.tile([P, N], I32, align_bytes=64)
 
+        def load_scale_rows(tile, rows):
+            for q in range(QUADS):
+                nc.sync.dma_start(
+                    out=tile[32 * q : 32 * q + 4, :].bitcast(I32), in_=rows[0, 4 * q : 4 * q + 4, :].bitcast(I32)
+                )
+
         nc.sync.dma_start(out=w1_raw[0][:], in_=w1_rows[:, 0:2, :])
         nc.sync.dma_start(out=offs_t[:], in_=offs)
-        for q in range(QUADS):
-            nc.sync.dma_start(
-                out=x_scale_table[32 * q : 32 * q + 4, :].bitcast(I32),
-                in_=x_scales[0, 4 * q : 4 * q + 4, :].bitcast(I32),
-            )
+        load_scale_rows(x_scale_table, x_scales)
         nc.sync.dma_start(out=w1_raw[1][:], in_=w1_rows[:, 2:4, :])
         nc.sync.dma_start(
             out=x_word_table[:].bitcast(I32), in_=x_words[0].rearrange("p c r -> p (c r)").bitcast(I32)
         )
-        for q in range(QUADS):
-            nc.sync.dma_start(
-                out=w2_scale_raw[32 * q : 32 * q + 4, :].bitcast(I32),
-                in_=w2_scales[0, 4 * q : 4 * q + 4, :].bitcast(I32),
-            )
+        load_scale_rows(w2_scale_raw, w2_scales)
         nc.sync.dma_start(out=w2_word_raw[:], in_=w2_words[0].rearrange("p c r -> p (c r)").bitcast(I32))
         nc.sync.dma_start(out=lb_t[:], in_=lb)
         nc.sync.dma_start(out=wb_t[:], in_=wb.rearrange("(p t) v -> p t v", t=PACK)[:, 0, :])
@@ -86,59 +92,48 @@ def tile_picked_tworoute_gelu_po_kernel(
         x_scale_pick = keep.tile([P, S], U8, align_bytes=64)
         x_word_pick = keep.tile([P, S], U32, align_bytes=64)
 
-        def round_w1(h, copy):
+        def round_w1(pair, lo, hi, copy):
             copy(
-                out=w1_bf[:].rearrange("p t (m j) -> p m t j", j=PACK)[:, :, :, 2 * h : 2 * h + 2],
-                in_=w1_raw[h][:].rearrange("p j (m t) -> p m t j", t=PACK),
+                out=w1_bf[:].rearrange("p t (m j) -> p m t j", j=PACK)[:, lo:hi, :, 2 * pair : 2 * pair + 2],
+                in_=w1_raw[pair][:].rearrange("p j (m t) -> p m t j", t=PACK)[:, lo:hi],
             )
 
-        def quantise_w1(t):
-            cols = slice(P * t, P * (t + 1))
-            nc.vector.quantize_mx(out=w1_codes[:, cols].bitcast(FP8X4), scales=w1_scales[:, cols], in_=w1_bf[:, t, :])
-
-        round_w1(0, nc.scalar.copy)
-        round_w1(1, nc.vector.tensor_copy)
+        round_w1(0, 0, P, nc.scalar.copy)
+        round_w1(1, 0, W1_ON_VECTOR, nc.vector.tensor_copy)
+        round_w1(1, W1_ON_VECTOR, P, nc.scalar.copy)
         nc.vector.tensor_copy(out=x_scale_pick[:], in_=x_scale_table[:].indirect(offs_t[:]))
-        for t in range(PACK):
-            quantise_w1(t)
+        nc.vector.quantize_mx(
+            out=w1_codes[:].bitcast(FP8X4), scales=w1_scales[:], in_=w1_bf[:].rearrange("p t n -> p (t n)")
+        )
 
-        hs = S // 2
-        for h in range(2):
+        for lo in (0, HALF):
             nc.vector.tensor_copy(
-                out=x_word_pick[:, hs * h : hs * (h + 1)],
-                in_=x_word_table[:].indirect(offs_t[:, hs // 16 * h : hs // 16 * (h + 1)]),
+                out=x_word_pick[:, lo : lo + HALF],
+                in_=x_word_table[:].indirect(offs_t[:, lo // GROUP : (lo + HALF) // GROUP]),
             )
 
-        w2_codes = shared.tile([P, N], I32, align_bytes=64, offset=0)
-        w2_scale_t = shared.tile([P, N], U8, align_bytes=64, offset=4 * N)
+        w2_codes = shared.tile([P, N], I32, align_bytes=64, offset=words_at)
+        w2_scale_dealt = shared.tile([P, N], U8, align_bytes=64, offset=late_at)
         nc.vector.tensor_copy(
             out=w2_codes[:].rearrange("p (t m) -> p m t", t=PACK),
             in_=w2_word_raw[:].rearrange("p (m t) -> p m t", t=PACK),
         )
-        nc.vector.tensor_copy(
-            out=w2_scale_t[:].rearrange("p (t m) -> p m t", t=PACK),
-            in_=w2_scale_raw[:].rearrange("p (m t) -> p m t", t=PACK),
-        )
 
         y = [keep.tile([P, S], F32, name=f"y{t}") for t in range(PACK)]
-
-        g = [keep.tile([P, S], F32, name=f"g{t}") for t in range(PACK)]
+        gelu_y = [keep.tile([P, S], F32, name=f"gelu_y{t}") for t in range(PACK)]
 
         def project(t):
-            edges = ((0, 256, 384, 512), (0, 256, 512), (0, S), (0, S))[t]
-            for lo, hi in zip(edges, edges[1:]):
+            for lo, hi in zip(Y_EDGES[t], Y_EDGES[t][1:]):
                 cols = slice(lo, hi)
-                width = hi - lo
                 bank = psum.tile([P, S], F32, name="bank")
-                mx(bank[:, 0:width], w1_codes, w1_scales, slice(P * t, P * (t + 1)), x_word_pick, x_scale_pick, cols)
-                copy = nc.vector.tensor_copy if (t, lo) == (0, 256) else nc.scalar.copy
-                copy(out=y[t][:, cols], in_=bank[:, 0:width])
-
-        def activate(t):
-            nc.scalar.activation(out=g[t][:], in_=y[t][:], func=GELU)
+                mx(bank[:, 0 : hi - lo], w1_codes, w1_scales, slice(P * t, P * (t + 1)), x_word_pick, x_scale_pick, cols)
+                copy = nc.vector.tensor_copy if (t, lo) == (0, HALF) else nc.scalar.copy
+                copy(out=y[t][:, cols], in_=bank[:, 0 : hi - lo])
 
         z = [keep.tile([P, S], F32, name=f"z{t}") for t in range(PACK)]
-        a = [keep.tile([P, V], F32, name=f"a{t}") for t in range(PACK)]
+        a = [keep.tile([P, V], F32, name=f"a{t}") for t in (0, 1)]
+        a.append(shared.tile([P, V], F32, name="a2", align_bytes=64, offset=late_at))
+        a.append(keep.tile([P, V], F32, name="a3"))
         b = [keep.tile([P, V], F32, name=f"b{t}") for t in range(PACK)]
         z_bf = [keep.tile([P, CHUNK, PACK], BF16, name=f"z_bf{c}", align_bytes=64) for c in range(CHUNKS)]
 
@@ -146,7 +141,7 @@ def tile_picked_tworoute_gelu_po_kernel(
             nc.vector.tensor_tensor(out=b[t][:], in0=y[t][:].indirect(lb_t[:]), in1=wb_t[:], op=MULT)
 
         def fetch_a(t):
-            nc.vector.tensor_tensor(out=a[t][:], in0=g[t][:].indirect(la_t[:]), in1=wa_t[:], op=MULT)
+            nc.vector.tensor_tensor(out=a[t][:], in0=gelu_y[t][:].indirect(la_t[:]), in1=wa_t[:], op=MULT)
 
         def put_b(t):
             nc.vector.tensor_copy(out=z[t][:].indirect(lb_t[:]), in_=b[t][:])
@@ -157,9 +152,9 @@ def tile_picked_tworoute_gelu_po_kernel(
         def round_z(t):
             for c in range(CHUNKS):
                 src = z[t][:, CHUNK * c : CHUNK * (c + 1)]
-                if t == PACK - 2 and c < CHUNKS // 2:
+                if t == PACK - 2 and c < Z_ON_VECTOR:
                     nc.scalar.copy(out=z_bf[c][:, :, t : t + 2], in_=src.unsqueeze(2).to_broadcast([P, CHUNK, 2]))
-                elif t == PACK - 1 and c < CHUNKS // 2:
+                elif t == PACK - 1 and c < Z_ON_VECTOR:
                     nc.vector.tensor_copy(out=z_bf[c][:, :, t], in_=src)
                 else:
                     nc.scalar.copy(out=z_bf[c][:, :, t], in_=src)
@@ -167,17 +162,24 @@ def tile_picked_tworoute_gelu_po_kernel(
         for t in range(PACK):
             project(t)
         for t in range(PACK):
-            activate(t)
+            nc.scalar.activation(out=gelu_y[t][:], in_=y[t][:], func=GELU)
         fetch_b(0)
+        fetch_b(1)
+        put_b(0)
         for t in range(PACK):
+            if t + 2 < PACK:
+                fetch_b(t + 2)
             if t + 1 < PACK:
-                fetch_b(t + 1)
-            put_b(t)
+                put_b(t + 1)
             fetch_a(t)
             if t > 0:
                 put_a(t - 1)
                 round_z(t - 1)
         put_a(PACK - 1)
+        nc.vector.tensor_copy(
+            out=w2_scale_dealt[:].rearrange("p (t m) -> p t m", t=PACK),
+            in_=w2_scale_raw[:].rearrange("p (m t) -> p t m", t=PACK),
+        )
         round_z(PACK - 1)
 
         z_codes = keep.tile([P, S], U32, align_bytes=64)
@@ -195,6 +197,14 @@ def tile_picked_tworoute_gelu_po_kernel(
         o_codes = keep.tile([P, S], U32, align_bytes=64)
         o_scales = keep.tile([P, S], U8, align_bytes=64)
         o_bf = [keep.tile([P, CHUNK, PACK], BF16, name=f"o_bf{c}", align_bytes=64) for c in range(CHUNKS)]
+        o_f32 = [keep.tile([P, PACK, HALF], F32, name=f"o_f32_{h}") for h in range(2)]
+
+        def round_out(c, lo, hi):
+            h, first = divmod(CHUNK * c, HALF)
+            nc.vector.tensor_copy(
+                out=o_bf[c][:, lo:hi, :].rearrange("p (g i) t -> p g t i", i=4),
+                in_=o_f32[h][:, :, first + lo : first + hi].rearrange("p t (g i) -> p g t i", i=4),
+            )
 
         def quantise_out(c, lo, hi):
             cols = slice(CHUNK * c + lo, CHUNK * c + hi)
@@ -204,43 +214,40 @@ def tile_picked_tworoute_gelu_po_kernel(
                 in_=o_bf[c][:, lo:hi, :].rearrange("p n t -> p (n t)"),
             )
 
-        wide = 2 * CHUNK
-        o_f = [keep.tile([P, PACK, wide], F32, name=f"o_f{h}") for h in range(2)]
+        last = CHUNKS - 1
         for c in range(CHUNKS):
             cols = slice(CHUNK * c, CHUNK * (c + 1))
-            h, first = divmod(CHUNK * c, wide)
+            h, first = divmod(CHUNK * c, HALF)
             for pair in range(2):
                 slots = slice(2 * pair, 2 * pair + 2)
                 bank = psum.tile([P, S], F32, name="bank")
                 for u in range(2):
                     t = 2 * pair + u
-                    mx(bank[:, CHUNK * u : CHUNK * (u + 1)], w2_codes, w2_scale_t, slice(P * t, P * (t + 1)), z_codes, z_scales, cols)
+                    w_cols = slice(P * t, P * (t + 1))
+                    mx(bank[:, CHUNK * u : CHUNK * (u + 1)], w2_codes, w2_scale_dealt, w_cols, z_codes, z_scales, cols)
                 copy = nc.vector.tensor_copy if (c, pair) == (0, 1) else nc.scalar.copy
                 copy(
-                    out=o_f[h][:, slots, first : first + CHUNK],
+                    out=o_f32[h][:, slots, first : first + CHUNK],
                     in_=bank[:, 0 : 2 * CHUNK].rearrange("p (t n) -> p t n", t=2),
                 )
                 if c == 0:
-                    nc.sync.dma_start(out=out_rows[:, slots, cols], in_=o_f[0][:, slots, cols])
-                if c == CHUNKS - 1:
-                    nc.sync.dma_start(out=out_rows[:, slots, wide:S], in_=o_f[1][:, slots, :])
+                    nc.sync.dma_start(out=out_rows[:, slots, cols], in_=o_f32[0][:, slots, cols])
+                if c == last:
+                    nc.sync.dma_start(out=out_rows[:, slots, HALF:S], in_=o_f32[1][:, slots, :])
             if c == 1:
-                nc.sync.dma_start(out=out_rows[:, :, cols], in_=o_f[0][:, :, cols])
-            parts = 2 if c == CHUNKS - 1 else 1
-            width = CHUNK // parts
-            for i in range(parts):
-                nc.vector.tensor_copy(
-                    out=o_bf[c][:, width * i : width * (i + 1), :].rearrange("p (g i) t -> p g t i", i=4),
-                    in_=o_f[h][:, :, first + width * i : first + width * (i + 1)].rearrange("p t (g i) -> p g t i", i=4),
-                )
+                nc.sync.dma_start(out=out_rows[:, :, cols], in_=o_f32[0][:, :, cols])
+            if c < last:
+                round_out(c, 0, CHUNK)
+            else:
+                round_out(c, 0, CHUNK // 2)
+                round_out(c, CHUNK // 2, CHUNK)
             if c > 0:
                 quantise_out(c - 1, 0, CHUNK)
-            if c == 2:
-                nc.sync.dma_start(out=out_words[:, 0:wide], in_=o_codes[:, 0:wide].bitcast(I32))
-        last = wide
-        quantise_out(CHUNKS - 1, 0, CHUNK // 2)
-        quantise_out(CHUNKS - 1, CHUNK // 2, CHUNK)
-        nc.sync.dma_start(out=out_words[:, last:S], in_=o_codes[:, last:S].bitcast(I32))
+            if CHUNK * c == HALF:
+                nc.sync.dma_start(out=out_words[:, 0:HALF], in_=o_codes[:, 0:HALF].bitcast(I32))
+        quantise_out(last, 0, CHUNK // 2)
+        quantise_out(last, CHUNK // 2, CHUNK)
+        nc.sync.dma_start(out=out_words[:, HALF:S], in_=o_codes[:, HALF:S].bitcast(I32))
         for q in range(QUADS):
             queue = nc.scalar if q % 2 == 0 else nc.sync
             queue.dma_start(

@@ -23,7 +23,6 @@ BANKS = 8
 HALF = S // 2
 CHUNK = 128
 CHUNKS = S // CHUNK
-W1_ON_VECTOR = 88
 Y_EDGES = ((0, HALF, HALF + CHUNK, S), (0, HALF, S), (0, S), (0, S))
 Z_ON_VECTOR = CHUNKS // 2
 
@@ -88,23 +87,31 @@ def tile_picked_tworoute_gelu_po_kernel(
 
         w1_codes = keep.tile([P, H], U32, align_bytes=64)
         w1_scales = keep.tile([P, H], U8, align_bytes=64)
-        w1_bf = keep.tile([P, PACK, H], BF16, align_bytes=64)
+        w1_bf = [keep.tile([P, 2, H], BF16, name=f"w1_bf{slots}", align_bytes=64) for slots in range(2)]
         x_scale_pick = keep.tile([P, S], U8, align_bytes=64)
         x_word_pick = keep.tile([P, S], U32, align_bytes=64)
 
-        def round_w1(pair, lo, hi, copy):
+        def round_w1(rows, slots, copy):
             copy(
-                out=w1_bf[:].rearrange("p t (m j) -> p m t j", j=PACK)[:, lo:hi, :, 2 * pair : 2 * pair + 2],
-                in_=w1_raw[pair][:].rearrange("p j (m t) -> p m t j", t=PACK)[:, lo:hi],
+                out=w1_bf[slots][:].rearrange("p u (m j) -> p m u j", j=PACK)[:, :, :, 2 * rows : 2 * rows + 2],
+                in_=w1_raw[rows][:].rearrange("p j (m t) -> p m t j", t=PACK)[:, :, 2 * slots : 2 * slots + 2],
             )
 
-        round_w1(0, 0, P, nc.scalar.copy)
-        round_w1(1, 0, W1_ON_VECTOR, nc.vector.tensor_copy)
-        round_w1(1, W1_ON_VECTOR, P, nc.scalar.copy)
+        def quantise_w1(slots):
+            cols = slice(2 * P * slots, 2 * P * (slots + 1))
+            nc.vector.quantize_mx(
+                out=w1_codes[:, cols].bitcast(FP8X4),
+                scales=w1_scales[:, cols],
+                in_=w1_bf[slots][:].rearrange("p u n -> p (u n)"),
+            )
+
+        round_w1(0, 0, nc.vector.tensor_copy)
+        round_w1(0, 1, nc.scalar.copy)
         nc.vector.tensor_copy(out=x_scale_pick[:], in_=x_scale_table[:].indirect(offs_t[:]))
-        nc.vector.quantize_mx(
-            out=w1_codes[:].bitcast(FP8X4), scales=w1_scales[:], in_=w1_bf[:].rearrange("p t n -> p (t n)")
-        )
+        round_w1(1, 0, nc.vector.tensor_copy)
+        round_w1(1, 1, nc.scalar.copy)
+        quantise_w1(1)
+        quantise_w1(0)
 
         for lo in (0, HALF):
             nc.vector.tensor_copy(

@@ -25,6 +25,14 @@ CHUNK = 128
 CHUNKS = S // CHUNK
 Y_EDGES = ((0, HALF, HALF + CHUNK, S), (0, HALF, S), (0, S), (0, S))
 Z_ON_VECTOR = CHUNKS // 2
+PIECE = V // 2
+LEAD = 3
+RING = 4
+RING_PLACE = (0, 1, 3, 2)
+PIECES = (
+    ("b", 0, 0), ("b", 1, 0), ("b", 0, 1), ("b", 1, 1), ("b", 2, 0), ("b", 3, 0), ("a", 0, 0),
+    ("b", 2, 1), ("a", 0, 1), ("a", 1, 0), ("a", 2, 0), ("a", 1, 1), ("b", 3, 1), ("a", 2, 1),
+)
 
 
 def tile_picked_tworoute_gelu_po_kernel(
@@ -36,7 +44,8 @@ def tile_picked_tworoute_gelu_po_kernel(
         shared = ctx.enter_context(tc.tile_pool(name="shared", bufs=1))
         psum = ctx.enter_context(tc.psum_pool(name="psum", bufs=BANKS))
         words_at = 0
-        late_at = 4 * T
+        y_at = 4 * T
+        ring_at = y_at + 2 * 4 * S
 
         def mx(out, w_codes, w_scales, w_cols, a_codes, a_scales, a_cols):
             nc.tensor.matmul_mx(
@@ -120,13 +129,14 @@ def tile_picked_tworoute_gelu_po_kernel(
             )
 
         w2_codes = shared.tile([P, N], I32, align_bytes=64, offset=words_at)
-        w2_scale_dealt = shared.tile([P, N], U8, align_bytes=64, offset=late_at)
+        w2_scale_dealt = shared.tile([P, N], U8, align_bytes=64, offset=ring_at + 4 * PIECE * RING_PLACE[13 % RING])
         nc.vector.tensor_copy(
             out=w2_codes[:].rearrange("p (t m) -> p m t", t=PACK),
             in_=w2_word_raw[:].rearrange("p (m t) -> p m t", t=PACK),
         )
 
-        y = [keep.tile([P, S], F32, name=f"y{t}") for t in range(PACK)]
+        y = [shared.tile([P, S], F32, name=f"y{t}", align_bytes=64, offset=y_at + 4 * S * t) for t in (0, 1)]
+        y += [keep.tile([P, S], F32, name=f"y{t}") for t in (2, 3)]
         gelu_y = [keep.tile([P, S], F32, name=f"gelu_y{t}") for t in range(PACK)]
 
         def project(t):
@@ -137,24 +147,35 @@ def tile_picked_tworoute_gelu_po_kernel(
                 copy = nc.vector.tensor_copy if (t, lo) == (0, HALF) else nc.scalar.copy
                 copy(out=y[t][:, cols], in_=bank[:, 0 : hi - lo])
 
-        z = [keep.tile([P, S], F32, name=f"z{t}") for t in range(PACK)]
-        a = [keep.tile([P, V], F32, name=f"a{t}") for t in (0, 1)]
-        a.append(shared.tile([P, V], F32, name="a2", align_bytes=64, offset=late_at))
-        a.append(keep.tile([P, V], F32, name="a3"))
-        b = [keep.tile([P, V], F32, name=f"b{t}") for t in range(PACK)]
+        z = [keep.tile([P, S], F32, name=f"z{t}") for t in (0, 1)]
+        z += [shared.tile([P, S], F32, name=f"z{t}", align_bytes=64, offset=y_at + 4 * S * (t - 2)) for t in (2, 3)]
         z_bf = [keep.tile([P, CHUNK, PACK], BF16, name=f"z_bf{c}", align_bytes=64) for c in range(CHUNKS)]
 
-        def fetch_b(t):
-            nc.vector.tensor_tensor(out=b[t][:], in0=y[t][:].indirect(lb_t[:]), in1=wb_t[:], op=MULT)
+        routes = {"a": (gelu_y, la_t, wa_t), "b": (y, lb_t, wb_t)}
+        picked = [
+            shared.tile([P, PIECE], F32, name=f"picked{k}", align_bytes=64, offset=ring_at + 4 * PIECE * RING_PLACE[k % RING])
+            for k in range(len(PIECES))
+        ]
+        last_picked = shared.tile(
+            [P, V], F32, align_bytes=64, offset=ring_at + 4 * PIECE * RING_PLACE[len(PIECES) % RING]
+        )
 
-        def fetch_a(t):
-            nc.vector.tensor_tensor(out=a[t][:], in0=gelu_y[t][:].indirect(la_t[:]), in1=wa_t[:], op=MULT)
+        def fetch(route, t, h, out):
+            table, offsets, weight = routes[route]
+            lo = PIECE * h
+            nc.vector.tensor_tensor(
+                out=out,
+                in0=table[t][:].indirect(offsets[:, lo // GROUP : (lo + PIECE) // GROUP]),
+                in1=weight[:, lo : lo + PIECE],
+                op=MULT,
+            )
 
-        def put_b(t):
-            nc.vector.tensor_copy(out=z[t][:].indirect(lb_t[:]), in_=b[t][:])
-
-        def put_a(t):
-            nc.vector.tensor_copy(out=z[t][:].indirect(la_t[:]), in_=a[t][:])
+        def put(k):
+            route, t, h = PIECES[k]
+            lo = PIECE * h
+            nc.vector.tensor_copy(
+                out=z[t][:].indirect(routes[route][1][:, lo // GROUP : (lo + PIECE) // GROUP]), in_=picked[k][:]
+            )
 
         def round_z(t):
             for c in range(CHUNKS):
@@ -170,19 +191,19 @@ def tile_picked_tworoute_gelu_po_kernel(
             project(t)
         for t in range(PACK):
             nc.scalar.activation(out=gelu_y[t][:], in_=y[t][:], func=GELU)
-        fetch_b(0)
-        fetch_b(1)
-        put_b(0)
-        for t in range(PACK):
-            if t + 2 < PACK:
-                fetch_b(t + 2)
-            if t + 1 < PACK:
-                put_b(t + 1)
-            fetch_a(t)
-            if t > 0:
-                put_a(t - 1)
-                round_z(t - 1)
-        put_a(PACK - 1)
+        for k in (0, 2, 1):
+            fetch(*PIECES[k], picked[k][:])
+        for k in range(len(PIECES)):
+            put(k)
+            t = PIECES[k][1]
+            if t < PACK - 1 and all(later[1] != t for later in PIECES[k + 1 :]):
+                round_z(t)
+            if k + LEAD < len(PIECES):
+                fetch(*PIECES[k + LEAD], picked[k + LEAD][:])
+            elif k + LEAD < len(PIECES) + 2:
+                h = k + LEAD - len(PIECES)
+                fetch("a", PACK - 1, h, last_picked[:, PIECE * h : PIECE * (h + 1)])
+        nc.vector.tensor_copy(out=z[PACK - 1][:].indirect(la_t[:]), in_=last_picked[:])
         nc.vector.tensor_copy(
             out=w2_scale_dealt[:].rearrange("p (t m) -> p t m", t=PACK),
             in_=w2_scale_raw[:].rearrange("p (m t) -> p t m", t=PACK),

@@ -44,8 +44,10 @@ def tile_picked_tworoute_gelu_po_kernel(
         shared = ctx.enter_context(tc.tile_pool(name="shared", bufs=1))
         psum = ctx.enter_context(tc.psum_pool(name="psum", bufs=BANKS))
         words_at = 0
-        y_at = 4 * T
-        ring_at = y_at + 2 * 4 * S
+        first_at = 4 * T
+        y_at = first_at + N
+        late_at = y_at + 2 * 4 * S
+        ring_at = late_at + 4 * PIECE
 
         def mx(out, w_codes, w_scales, w_cols, a_codes, a_scales, a_cols):
             nc.tensor.matmul_mx(
@@ -83,57 +85,50 @@ def tile_picked_tworoute_gelu_po_kernel(
         nc.sync.dma_start(out=w1_raw[0][:], in_=w1_rows[:, 0:2, :])
         nc.sync.dma_start(out=offs_t[:], in_=offs)
         load_scale_rows(x_scale_table, x_scales)
-        nc.sync.dma_start(out=w1_raw[1][:], in_=w1_rows[:, 2:4, :])
         nc.sync.dma_start(
             out=x_word_table[:].bitcast(I32), in_=x_words[0].rearrange("p c r -> p (c r)").bitcast(I32)
         )
+        nc.sync.dma_start(out=w1_raw[1][:], in_=w1_rows[:, 2:4, :])
         load_scale_rows(w2_scale_raw, w2_scales)
-        nc.sync.dma_start(out=w2_word_raw[:], in_=w2_words[0].rearrange("p c r -> p (c r)").bitcast(I32))
         nc.sync.dma_start(out=lb_t[:], in_=lb)
         nc.sync.dma_start(out=wb_t[:], in_=wb.rearrange("(p t) v -> p t v", t=PACK)[:, 0, :])
         nc.sync.dma_start(out=la_t[:], in_=la)
         nc.sync.dma_start(out=wa_t[:], in_=wa.rearrange("(p t) v -> p t v", t=PACK)[:, 0, :])
 
-        w1_codes = keep.tile([P, H], U32, align_bytes=64)
-        w1_scales = keep.tile([P, H], U8, align_bytes=64)
-        w1_bf = [keep.tile([P, 2, H], BF16, name=f"w1_bf{slots}", align_bytes=64) for slots in range(2)]
+        nc.sync.dma_start(out=w2_word_raw[:], in_=w2_words[0].rearrange("p c r -> p (c r)").bitcast(I32))
+
         x_scale_pick = keep.tile([P, S], U8, align_bytes=64)
         x_word_pick = keep.tile([P, S], U32, align_bytes=64)
+        w1_groups = ((0, 1), (1, 2), (2, 4))
+        w1_codes = [shared.tile([P, P], U32, name="w1_codes0", align_bytes=64, offset=first_at)]
+        w1_codes += [keep.tile([P, P * (hi - lo)], U32, name=f"w1_codes{lo}", align_bytes=64) for lo, hi in w1_groups[1:]]
+        w1_scales = [keep.tile([P, P * (hi - lo)], U8, name=f"w1_scales{lo}", align_bytes=64) for lo, hi in w1_groups]
+        w1_bf = [keep.tile([P, hi - lo, H], BF16, name=f"w1_bf{lo}", align_bytes=64) for lo, hi in w1_groups]
 
-        def round_w1(rows, slots, copy):
+        def round_w1(rows, g, copy):
+            lo, hi = w1_groups[g]
             copy(
-                out=w1_bf[slots][:].rearrange("p u (m j) -> p m u j", j=PACK)[:, :, :, 2 * rows : 2 * rows + 2],
-                in_=w1_raw[rows][:].rearrange("p j (m t) -> p m t j", t=PACK)[:, :, 2 * slots : 2 * slots + 2],
+                out=w1_bf[g][:].rearrange("p u (m j) -> p m u j", j=PACK)[:, :, :, 2 * rows : 2 * rows + 2],
+                in_=w1_raw[rows][:].rearrange("p j (m t) -> p m t j", t=PACK)[:, :, lo:hi],
             )
 
-        def quantise_w1(slots):
-            cols = slice(2 * P * slots, 2 * P * (slots + 1))
+        def quantise_w1(g):
             nc.vector.quantize_mx(
-                out=w1_codes[:, cols].bitcast(FP8X4),
-                scales=w1_scales[:, cols],
-                in_=w1_bf[slots][:].rearrange("p u n -> p (u n)"),
+                out=w1_codes[g][:].bitcast(FP8X4),
+                scales=w1_scales[g][:],
+                in_=w1_bf[g][:].rearrange("p u n -> p (u n)"),
             )
 
         round_w1(0, 0, nc.vector.tensor_copy)
-        round_w1(0, 1, nc.scalar.copy)
+        round_w1(0, 1, nc.vector.tensor_copy)
+        round_w1(0, 2, nc.scalar.copy)
         nc.vector.tensor_copy(out=x_scale_pick[:], in_=x_scale_table[:].indirect(offs_t[:]))
+        nc.vector.tensor_copy(out=x_word_pick[:], in_=x_word_table[:].indirect(offs_t[:]))
         round_w1(1, 0, nc.vector.tensor_copy)
-        round_w1(1, 1, nc.scalar.copy)
-        quantise_w1(1)
-        quantise_w1(0)
-
-        for lo in (0, HALF):
-            nc.vector.tensor_copy(
-                out=x_word_pick[:, lo : lo + HALF],
-                in_=x_word_table[:].indirect(offs_t[:, lo // GROUP : (lo + HALF) // GROUP]),
-            )
-
-        w2_codes = shared.tile([P, N], I32, align_bytes=64, offset=words_at)
-        w2_scale_dealt = shared.tile([P, N], U8, align_bytes=64, offset=ring_at + 4 * PIECE * RING_PLACE[13 % RING])
-        nc.vector.tensor_copy(
-            out=w2_codes[:].rearrange("p (t m) -> p m t", t=PACK),
-            in_=w2_word_raw[:].rearrange("p (m t) -> p m t", t=PACK),
-        )
+        round_w1(1, 1, nc.vector.tensor_copy)
+        round_w1(1, 2, nc.scalar.copy)
+        for g in range(len(w1_groups)):
+            quantise_w1(g)
 
         y = [shared.tile([P, S], F32, name=f"y{t}", align_bytes=64, offset=y_at + 4 * S * t) for t in (0, 1)]
         y += [keep.tile([P, S], F32, name=f"y{t}") for t in (2, 3)]
@@ -143,8 +138,10 @@ def tile_picked_tworoute_gelu_po_kernel(
             for lo, hi in zip(Y_EDGES[t], Y_EDGES[t][1:]):
                 cols = slice(lo, hi)
                 bank = psum.tile([P, S], F32, name="bank")
-                mx(bank[:, 0 : hi - lo], w1_codes, w1_scales, slice(P * t, P * (t + 1)), x_word_pick, x_scale_pick, cols)
-                copy = nc.vector.tensor_copy if (t, lo) == (0, HALF) else nc.scalar.copy
+                g = min(t, 2)
+                w_cols = slice(P * (t - g), P * (t - g + 1))
+                mx(bank[:, 0 : hi - lo], w1_codes[g], w1_scales[g], w_cols, x_word_pick, x_scale_pick, cols)
+                copy = nc.vector.tensor_copy if (t, lo) == (0, 0) else nc.scalar.copy
                 copy(out=y[t][:, cols], in_=bank[:, 0 : hi - lo])
 
         z = [keep.tile([P, S], F32, name=f"z{t}") for t in (0, 1)]
@@ -187,14 +184,23 @@ def tile_picked_tworoute_gelu_po_kernel(
                 else:
                     nc.scalar.copy(out=z_bf[c][:, :, t], in_=src)
 
-        for t in range(PACK):
+        project(0)
+        w2_scale_dealt = shared.tile([P, N], U8, align_bytes=64, offset=first_at)
+        nc.vector.tensor_copy(
+            out=w2_scale_dealt[:].rearrange("p (t m) -> p t m", t=PACK),
+            in_=w2_scale_raw[:].rearrange("p (m t) -> p t m", t=PACK),
+        )
+
+        for t in range(1, PACK):
             project(t)
         for t in range(PACK):
             nc.scalar.activation(out=gelu_y[t][:], in_=y[t][:], func=GELU)
-        for k in (0, 2, 1):
+        for k in (0, 2):
             fetch(*PIECES[k], picked[k][:])
         for k in range(len(PIECES)):
             put(k)
+            if k == 0:
+                fetch(*PIECES[1], picked[1][:])
             t = PIECES[k][1]
             if t < PACK - 1 and all(later[1] != t for later in PIECES[k + 1 :]):
                 round_z(t)
@@ -204,9 +210,10 @@ def tile_picked_tworoute_gelu_po_kernel(
                 h = k + LEAD - len(PIECES)
                 fetch("a", PACK - 1, h, last_picked[:, PIECE * h : PIECE * (h + 1)])
         nc.vector.tensor_copy(out=z[PACK - 1][:].indirect(la_t[:]), in_=last_picked[:])
+        w2_codes = shared.tile([P, N], I32, align_bytes=64, offset=late_at)
         nc.vector.tensor_copy(
-            out=w2_scale_dealt[:].rearrange("p (t m) -> p t m", t=PACK),
-            in_=w2_scale_raw[:].rearrange("p (m t) -> p t m", t=PACK),
+            out=w2_codes[:].rearrange("p (t m) -> p m t", t=PACK),
+            in_=w2_word_raw[:].rearrange("p (m t) -> p m t", t=PACK),
         )
         round_z(PACK - 1)
 

@@ -105,11 +105,11 @@ def tile_picked_tworoute_gelu_po_kernel(
         w1_scales = [keep.tile([P, P * (hi - lo)], U8, name=f"w1_scales{lo}", align_bytes=64) for lo, hi in w1_groups]
         w1_bf = [keep.tile([P, hi - lo, H], BF16, name=f"w1_bf{lo}", align_bytes=64) for lo, hi in w1_groups]
 
-        def round_w1(rows, g, copy):
+        def round_w1(rows, g, copy, part=slice(0, P)):
             lo, hi = w1_groups[g]
             copy(
-                out=w1_bf[g][:].rearrange("p u (m j) -> p m u j", j=PACK)[:, :, :, 2 * rows : 2 * rows + 2],
-                in_=w1_raw[rows][:].rearrange("p j (m t) -> p m t j", t=PACK)[:, :, lo:hi],
+                out=w1_bf[g][:].rearrange("p u (m j) -> p m u j", j=PACK)[:, part, :, 2 * rows : 2 * rows + 2],
+                in_=w1_raw[rows][:].rearrange("p j (m t) -> p m t j", t=PACK)[:, part, lo:hi],
             )
 
         def quantise_w1(g):
@@ -124,7 +124,8 @@ def tile_picked_tworoute_gelu_po_kernel(
         round_w1(0, 2, nc.scalar.copy)
         nc.vector.tensor_copy(out=x_scale_pick[:], in_=x_scale_table[:].indirect(offs_t[:]))
         nc.vector.tensor_copy(out=x_word_pick[:], in_=x_word_table[:].indirect(offs_t[:]))
-        round_w1(1, 0, nc.vector.tensor_copy)
+        round_w1(1, 0, nc.scalar.copy, slice(0, P // 2))
+        round_w1(1, 0, nc.vector.tensor_copy, slice(P // 2, P))
         round_w1(1, 1, nc.vector.tensor_copy)
         round_w1(1, 2, nc.scalar.copy)
         for g in range(len(w1_groups)):
@@ -234,11 +235,11 @@ def tile_picked_tworoute_gelu_po_kernel(
         o_bf = [keep.tile([P, CHUNK, PACK], BF16, name=f"o_bf{c}", align_bytes=64) for c in range(CHUNKS)]
         o_f32 = [keep.tile([P, PACK, HALF], F32, name=f"o_f32_{h}") for h in range(2)]
 
-        def round_out(c, lo, hi):
+        def round_out(c, lo, hi, slots=slice(0, PACK)):
             h, first = divmod(CHUNK * c, HALF)
             nc.vector.tensor_copy(
-                out=o_bf[c][:, lo:hi, :].rearrange("p (g i) t -> p g t i", i=4),
-                in_=o_f32[h][:, :, first + lo : first + hi].rearrange("p t (g i) -> p g t i", i=4),
+                out=o_bf[c][:, lo:hi, slots].rearrange("p (g i) t -> p g t i", i=4),
+                in_=o_f32[h][:, slots, first + lo : first + hi].rearrange("p t (g i) -> p g t i", i=4),
             )
 
         def quantise_out(c, lo, hi):
@@ -253,30 +254,34 @@ def tile_picked_tworoute_gelu_po_kernel(
         for c in range(CHUNKS):
             cols = slice(CHUNK * c, CHUNK * (c + 1))
             h, first = divmod(CHUNK * c, HALF)
-            for pair in range(2):
-                slots = slice(2 * pair, 2 * pair + 2)
+            groups = ((0, 2), (2, 4)) if c < last else ((0, 2), (2, 3), (3, 4))
+            for lo, hi in groups:
+                slots = slice(lo, hi)
                 bank = psum.tile([P, S], F32, name="bank")
-                for u in range(2):
-                    t = 2 * pair + u
+                for t in range(lo, hi):
                     w_cols = slice(P * t, P * (t + 1))
-                    mx(bank[:, CHUNK * u : CHUNK * (u + 1)], w2_codes, w2_scale_dealt, w_cols, z_codes, z_scales, cols)
-                copy = nc.vector.tensor_copy if (c, pair) == (0, 1) else nc.scalar.copy
+                    out_cols = slice(CHUNK * (t - lo), CHUNK * (t - lo + 1))
+                    mx(bank[:, out_cols], w2_codes, w2_scale_dealt, w_cols, z_codes, z_scales, cols)
+                copy = nc.vector.tensor_copy if (c, lo) == (0, 2) else nc.scalar.copy
                 copy(
                     out=o_f32[h][:, slots, first : first + CHUNK],
-                    in_=bank[:, 0 : 2 * CHUNK].rearrange("p (t n) -> p t n", t=2),
+                    in_=bank[:, 0 : (hi - lo) * CHUNK].rearrange("p (t n) -> p t n", t=hi - lo),
                 )
                 if c == 0:
                     nc.sync.dma_start(out=out_rows[:, slots, cols], in_=o_f32[0][:, slots, cols])
-                if c == last:
-                    nc.sync.dma_start(out=out_rows[:, slots, HALF:S], in_=o_f32[1][:, slots, :])
+                if c == last and hi % 2 == 0:
+                    nc.sync.dma_start(out=out_rows[:, hi - 2 : hi, HALF:S], in_=o_f32[1][:, hi - 2 : hi, :])
+                if c == last and hi == 2:
+                    round_out(c, 0, CHUNK, slots)
+                    quantise_out(c - 1, 0, CHUNK)
             if c == 1:
                 nc.sync.dma_start(out=out_rows[:, :, cols], in_=o_f32[0][:, :, cols])
             if c < last:
                 round_out(c, 0, CHUNK)
             else:
-                round_out(c, 0, CHUNK // 2)
-                round_out(c, CHUNK // 2, CHUNK)
-            if c > 0:
+                round_out(c, 0, CHUNK // 2, slice(2, PACK))
+                round_out(c, CHUNK // 2, CHUNK, slice(2, PACK))
+            if 0 < c < last:
                 quantise_out(c - 1, 0, CHUNK)
             if CHUNK * c == HALF:
                 nc.sync.dma_start(out=out_words[:, 0:HALF], in_=o_codes[:, 0:HALF].bitcast(I32))

@@ -13,6 +13,7 @@ U16 = mybir.dt.uint16
 U8 = mybir.dt.uint8
 FP8X4 = mybir.dt.float8_e4m3fn_x4
 GELU = mybir.ActivationFunctionType.Gelu_apprx_tanh
+COPY = mybir.ActivationFunctionType.Copy
 MULT = mybir.AluOpType.mult
 
 P = 128
@@ -25,14 +26,6 @@ CHUNK = 128
 CHUNKS = S // CHUNK
 Y_EDGES = ((0, HALF, HALF + CHUNK, S), (0, HALF, S), (0, S), (0, S))
 Z_ON_VECTOR = CHUNKS // 2
-PIECE = V // 2
-LEAD = 3
-RING = 4
-RING_PLACE = (0, 1, 3, 2)
-PIECES = (
-    ("b", 0, 0), ("b", 1, 0), ("b", 0, 1), ("b", 1, 1), ("b", 2, 0), ("b", 3, 0), ("a", 0, 0),
-    ("b", 2, 1), ("a", 0, 1), ("a", 1, 0), ("a", 2, 0), ("a", 1, 1), ("b", 3, 1), ("a", 2, 1),
-)
 
 
 def tile_picked_tworoute_gelu_po_kernel(
@@ -47,7 +40,6 @@ def tile_picked_tworoute_gelu_po_kernel(
         first_at = 4 * T
         y_at = first_at + N
         late_at = y_at + 2 * 4 * S
-        ring_at = late_at + 4 * PIECE
 
         def mx(out, w_codes, w_scales, w_cols, a_codes, a_scales, a_cols):
             nc.tensor.matmul_mx(
@@ -131,9 +123,8 @@ def tile_picked_tworoute_gelu_po_kernel(
         for g in range(len(w1_groups)):
             quantise_w1(g)
 
-        y = [shared.tile([P, S], F32, name=f"y{t}", align_bytes=64, offset=y_at + 4 * S * t) for t in (0, 1)]
-        y += [keep.tile([P, S], F32, name=f"y{t}") for t in (2, 3)]
-        gelu_y = [keep.tile([P, S], F32, name=f"gelu_y{t}") for t in range(PACK)]
+        y = [keep.tile([P, S], F32, name=f"y{t}") for t in (0, 1)]
+        y += [shared.tile([P, S], F32, name=f"y{t}", align_bytes=64, offset=y_at + 4 * S * (t - 2)) for t in (2, 3)]
 
         def project(t):
             for lo, hi in zip(Y_EDGES[t], Y_EDGES[t][1:]):
@@ -142,38 +133,37 @@ def tile_picked_tworoute_gelu_po_kernel(
                 g = min(t, 2)
                 w_cols = slice(P * (t - g), P * (t - g + 1))
                 mx(bank[:, 0 : hi - lo], w1_codes[g], w1_scales[g], w_cols, x_word_pick, x_scale_pick, cols)
-                copy = nc.vector.tensor_copy if (t, lo) == (0, 0) else nc.scalar.copy
+                copy = nc.vector.tensor_copy if t < 2 and lo == 0 else nc.scalar.copy
                 copy(out=y[t][:, cols], in_=bank[:, 0 : hi - lo])
 
-        z = [keep.tile([P, S], F32, name=f"z{t}") for t in (0, 1)]
-        z += [shared.tile([P, S], F32, name=f"z{t}", align_bytes=64, offset=y_at + 4 * S * (t - 2)) for t in (2, 3)]
-        z_bf = [keep.tile([P, CHUNK, PACK], BF16, name=f"z_bf{c}", align_bytes=64) for c in range(CHUNKS)]
-
-        routes = {"a": (gelu_y, la_t, wa_t), "b": (y, lb_t, wb_t)}
-        picked = [
-            shared.tile([P, PIECE], F32, name=f"picked{k}", align_bytes=64, offset=ring_at + 4 * PIECE * RING_PLACE[k % RING])
-            for k in range(len(PIECES))
+        z = [keep.tile([P, S], F32, name=f"z{t}") for t in range(PACK)]
+        z_bf = [
+            shared.tile([P, CHUNK, PACK], BF16, name=f"z_bf{c}", align_bytes=64, offset=y_at + 2 * PACK * CHUNK * c)
+            for c in range(CHUNKS)
         ]
-        last_picked = shared.tile(
-            [P, V], F32, align_bytes=64, offset=ring_at + 4 * PIECE * RING_PLACE[len(PIECES) % RING]
-        )
+        y_a = [keep.tile([P, V], F32, name=f"y_a{t}") for t in range(PACK)]
+        y_b = [keep.tile([P, V], F32, name=f"y_b{t}") for t in range(PACK)]
+        gelu_a = [
+            shared.tile([P, V], F32, name="gelu_a2", align_bytes=64, offset=late_at)
+            if t == PACK - 2
+            else keep.tile([P, V], F32, name=f"gelu_a{t}")
+            for t in range(PACK)
+        ]
 
-        def fetch(route, t, h, out):
-            table, offsets, weight = routes[route]
-            lo = PIECE * h
-            nc.vector.tensor_tensor(
-                out=out,
-                in0=table[t][:].indirect(offsets[:, lo // GROUP : (lo + PIECE) // GROUP]),
-                in1=weight[:, lo : lo + PIECE],
-                op=MULT,
-            )
+        def fetch_a(t):
+            nc.scalar.activation(out=y_a[t][:], in_=y[t][:].indirect(la_t[:]), func=COPY)
 
-        def put(k):
-            route, t, h = PIECES[k]
-            lo = PIECE * h
-            nc.vector.tensor_copy(
-                out=z[t][:].indirect(routes[route][1][:, lo // GROUP : (lo + PIECE) // GROUP]), in_=picked[k][:]
-            )
+        def fetch_b(t):
+            nc.scalar.activation(out=y_b[t][:], in_=y[t][:].indirect(lb_t[:]), func=COPY)
+
+        def gelu(t):
+            nc.scalar.activation(out=gelu_a[t][:], in_=y_a[t][:], func=GELU)
+
+        def put_a(t):
+            nc.vector.tensor_tensor(out=z[t][:].indirect(la_t[:]), in0=gelu_a[t][:], in1=wa_t[:], op=MULT)
+
+        def put_b(t):
+            nc.vector.tensor_tensor(out=z[t][:].indirect(lb_t[:]), in0=y_b[t][:], in1=wb_t[:], op=MULT)
 
         def round_z(t):
             for c in range(CHUNKS):
@@ -192,25 +182,33 @@ def tile_picked_tworoute_gelu_po_kernel(
             in_=w2_scale_raw[:].rearrange("p (m t) -> p t m", t=PACK),
         )
 
-        for t in range(1, PACK):
-            project(t)
-        for t in range(PACK):
-            nc.scalar.activation(out=gelu_y[t][:], in_=y[t][:], func=GELU)
-        for k in (0, 2):
-            fetch(*PIECES[k], picked[k][:])
-        for k in range(len(PIECES)):
-            put(k)
-            if k == 0:
-                fetch(*PIECES[1], picked[1][:])
-            t = PIECES[k][1]
-            if t < PACK - 1 and all(later[1] != t for later in PIECES[k + 1 :]):
-                round_z(t)
-            if k + LEAD < len(PIECES):
-                fetch(*PIECES[k + LEAD], picked[k + LEAD][:])
-            elif k + LEAD < len(PIECES) + 2:
-                h = k + LEAD - len(PIECES)
-                fetch("a", PACK - 1, h, last_picked[:, PIECE * h : PIECE * (h + 1)])
-        nc.vector.tensor_copy(out=z[PACK - 1][:].indirect(la_t[:]), in_=last_picked[:])
+        cut = V // 2
+        nc.vector.tensor_copy(out=y_b[0][:, 0:cut], in_=y[0][:].indirect(lb_t[:, 0 : cut // GROUP]))
+        nc.scalar.activation(out=y_b[0][:, cut:V], in_=y[0][:].indirect(lb_t[:, cut // GROUP : V // GROUP]), func=COPY)
+        project(1)
+        put_b(0)
+        fetch_b(1)
+        put_b(1)
+        fetch_a(0)
+        project(2)
+        gelu(0)
+        put_a(0)
+        fetch_a(1)
+        project(3)
+        gelu(1)
+        put_a(1)
+        fetch_b(2)
+        put_b(2)
+        fetch_b(3)
+        put_b(3)
+        fetch_a(2)
+        fetch_a(3)
+        gelu(2)
+        put_a(2)
+        gelu(3)
+        put_a(3)
+        for t in range(PACK - 1):
+            round_z(t)
         w2_codes = shared.tile([P, N], I32, align_bytes=64, offset=late_at)
         nc.vector.tensor_copy(
             out=w2_codes[:].rearrange("p (t m) -> p m t", t=PACK),

@@ -52,6 +52,11 @@ def tile_picked_tworoute_gelu_po_kernel(
                 stop=True,
             )
 
+        table_in = keep.tile([P, 1], F32)
+        table_out = keep.tile([P, 1], F32)
+        nc.gpsimd.memset(table_in[:], 0.0)
+        nc.scalar.activation(out=table_out[:], in_=table_in[:], func=GELU)
+
         x_scale_table = keep.tile([P, T], U8, align_bytes=64)
         nc.vector.memset(x_scale_table[:, 0 : T // 2].bitcast(I32), 0)
         nc.gpsimd.memset(x_scale_table[:, T // 2 : T].bitcast(I32), 0)

@@ -37,8 +37,8 @@ def tile_picked_tworoute_gelu_po_kernel(
         shared = ctx.enter_context(tc.tile_pool(name="shared", bufs=1))
         psum = ctx.enter_context(tc.psum_pool(name="psum", bufs=BANKS))
         words_at = 0
-        first_at = 4 * T
-        y_at = first_at + N
+        mid_at = 4 * T
+        y_at = mid_at + 4 * V
         late_at = y_at + 2 * 4 * S
 
         def mx(out, w_codes, w_scales, w_cols, a_codes, a_scales, a_cols):
@@ -86,18 +86,18 @@ def tile_picked_tworoute_gelu_po_kernel(
             out=x_word_table[:].bitcast(I32), in_=x_words[0].rearrange("p c r -> p (c r)").bitcast(I32)
         )
         nc.sync.dma_start(out=w1_raw[1][:], in_=w1_rows[:, 2:4, :])
-        load_scale_rows(w2_scale_raw, w2_scales)
         nc.sync.dma_start(out=lb_t[:], in_=lb)
         nc.sync.dma_start(out=wb_t[:], in_=wb.rearrange("(p t) v -> p t v", t=PACK)[:, 0, :])
         nc.sync.dma_start(out=la_t[:], in_=la)
         nc.sync.dma_start(out=wa_t[:], in_=wa.rearrange("(p t) v -> p t v", t=PACK)[:, 0, :])
 
         nc.sync.dma_start(out=w2_word_raw[:], in_=w2_words[0].rearrange("p c r -> p (c r)").bitcast(I32))
+        load_scale_rows(w2_scale_raw, w2_scales)
 
         x_scale_pick = keep.tile([P, S], U8, align_bytes=64)
         x_word_pick = keep.tile([P, S], U32, align_bytes=64)
         w1_groups = ((0, 1), (1, 2), (2, 4))
-        w1_codes = [shared.tile([P, P], U32, name="w1_codes0", align_bytes=64, offset=first_at)]
+        w1_codes = [keep.tile([P, P], U32, name="w1_codes0", align_bytes=64)]
         w1_codes += [keep.tile([P, P * (hi - lo)], U32, name=f"w1_codes{lo}", align_bytes=64) for lo, hi in w1_groups[1:]]
         w1_scales = [keep.tile([P, P * (hi - lo)], U8, name=f"w1_scales{lo}", align_bytes=64) for lo, hi in w1_groups]
         w1_bf = [keep.tile([P, hi - lo, H], BF16, name=f"w1_bf{lo}", align_bytes=64) for lo, hi in w1_groups]
@@ -146,14 +146,14 @@ def tile_picked_tworoute_gelu_po_kernel(
             shared.tile([P, CHUNK, PACK], BF16, name=f"z_bf{c}", align_bytes=64, offset=y_at + 2 * PACK * CHUNK * c)
             for c in range(CHUNKS)
         ]
-        y_a = [keep.tile([P, V], F32, name=f"y_a{t}") for t in range(PACK)]
-        y_b = [keep.tile([P, V], F32, name=f"y_b{t}") for t in range(PACK)]
-        gelu_a = [
-            shared.tile([P, V], F32, name="gelu_a2", align_bytes=64, offset=late_at)
-            if t == PACK - 2
-            else keep.tile([P, V], F32, name=f"gelu_a{t}")
+        y_a = [
+            shared.tile([P, V], F32, name=f"y_a{t}", align_bytes=64, offset=mid_at if t == 1 else late_at)
+            if t % 2
+            else keep.tile([P, V], F32, name=f"y_a{t}")
             for t in range(PACK)
         ]
+        y_b = [keep.tile([P, V], F32, name=f"y_b{t}") for t in range(PACK)]
+        gelu_a = [keep.tile([P, V], F32, name=f"gelu_a{t}") for t in range(PACK)]
 
         def fetch_a(t):
             nc.scalar.activation(out=y_a[t][:], in_=y[t][:].indirect(la_t[:]), func=COPY)
@@ -181,11 +181,6 @@ def tile_picked_tworoute_gelu_po_kernel(
                     nc.scalar.copy(out=z_bf[c][:, :, t], in_=src)
 
         project(0)
-        w2_scale_dealt = shared.tile([P, N], U8, align_bytes=64, offset=first_at)
-        nc.vector.tensor_copy(
-            out=w2_scale_dealt[:].rearrange("p (t m) -> p t m", t=PACK),
-            in_=w2_scale_raw[:].rearrange("p (m t) -> p t m", t=PACK),
-        )
 
         cut = V // 2
         nc.vector.tensor_copy(out=y_b[0][:, 0:cut], in_=y[0][:].indirect(lb_t[:, 0 : cut // GROUP]))
@@ -202,6 +197,11 @@ def tile_picked_tworoute_gelu_po_kernel(
         project(3)
         gelu(1)
         put_a(1)
+        w2_scale_dealt = shared.tile([P, N], U8, align_bytes=64, offset=mid_at)
+        nc.vector.tensor_copy(
+            out=w2_scale_dealt[:].rearrange("p (t m) -> p t m", t=PACK),
+            in_=w2_scale_raw[:].rearrange("p (m t) -> p t m", t=PACK),
+        )
         fetch_b(2)
         put_b(2)
         fetch_b(3)
@@ -212,13 +212,14 @@ def tile_picked_tworoute_gelu_po_kernel(
         put_a(2)
         gelu(3)
         put_a(3)
-        for t in range(PACK - 1):
-            round_z(t)
-        w2_codes = shared.tile([P, N], I32, align_bytes=64, offset=late_at)
-        nc.vector.tensor_copy(
+        round_z(0)
+        round_z(1)
+        w2_codes = shared.tile([P, N], U32, align_bytes=64, offset=late_at)
+        nc.scalar.copy(
             out=w2_codes[:].rearrange("p (t m) -> p m t", t=PACK),
-            in_=w2_word_raw[:].rearrange("p (m t) -> p m t", t=PACK),
+            in_=w2_word_raw[:].bitcast(U32).rearrange("p (m t) -> p m t", t=PACK),
         )
+        round_z(2)
         round_z(PACK - 1)
 
         z_codes = keep.tile([P, S], U32, align_bytes=64)

@@ -26,6 +26,8 @@ CHUNK = 128
 CHUNKS = S // CHUNK
 Y_EDGES = ((0, HALF, HALF + CHUNK, S), (0, HALF, S), (0, S), (0, S))
 Z_ON_VECTOR = CHUNKS // 2
+WHOLE = slice(0, V)
+PARTS = (slice(0, V // 2), slice(V // 2, V))
 
 
 def tile_picked_tworoute_gelu_po_kernel(
@@ -37,8 +39,7 @@ def tile_picked_tworoute_gelu_po_kernel(
         shared = ctx.enter_context(tc.tile_pool(name="shared", bufs=1))
         psum = ctx.enter_context(tc.psum_pool(name="psum", bufs=BANKS))
         words_at = 0
-        mid_at = 4 * T
-        y_at = mid_at + 4 * V
+        y_at = 4 * T
         late_at = y_at + 2 * 4 * S
 
         def mx(out, w_codes, w_scales, w_cols, a_codes, a_scales, a_cols):
@@ -146,29 +147,32 @@ def tile_picked_tworoute_gelu_po_kernel(
             shared.tile([P, CHUNK, PACK], BF16, name=f"z_bf{c}", align_bytes=64, offset=y_at + 2 * PACK * CHUNK * c)
             for c in range(CHUNKS)
         ]
-        y_a = [
-            shared.tile([P, V], F32, name=f"y_a{t}", align_bytes=64, offset=mid_at if t == 1 else late_at)
-            if t % 2
-            else keep.tile([P, V], F32, name=f"y_a{t}")
-            for t in range(PACK)
-        ]
+        y_a = [keep.tile([P, V], F32, name=f"y_a{t}") for t in range(PACK - 1)]
+        y_a.append(shared.tile([P, V], F32, name="y_a3", align_bytes=64, offset=late_at))
         y_b = [keep.tile([P, V], F32, name=f"y_b{t}") for t in range(PACK)]
         gelu_a = [keep.tile([P, V], F32, name=f"gelu_a{t}") for t in range(PACK)]
 
-        def fetch_a(t):
-            nc.scalar.activation(out=y_a[t][:], in_=y[t][:].indirect(la_t[:]), func=COPY)
+        def entries(lists, part):
+            return lists[:, part.start // GROUP : part.stop // GROUP]
 
-        def fetch_b(t):
-            nc.scalar.activation(out=y_b[t][:], in_=y[t][:].indirect(lb_t[:]), func=COPY)
+        def fetch_a(t, part=WHOLE):
+            nc.scalar.activation(out=y_a[t][:, part], in_=y[t][:].indirect(entries(la_t, part)), func=COPY)
 
-        def gelu(t):
-            nc.scalar.activation(out=gelu_a[t][:], in_=y_a[t][:], func=GELU)
+        def fetch_b(t, part=WHOLE):
+            nc.scalar.activation(out=y_b[t][:, part], in_=y[t][:].indirect(entries(lb_t, part)), func=COPY)
 
-        def put_a(t):
-            nc.vector.tensor_tensor(out=z[t][:].indirect(la_t[:]), in0=gelu_a[t][:], in1=wa_t[:], op=MULT)
+        def gelu(t, part=WHOLE):
+            nc.scalar.activation(out=gelu_a[t][:, part], in_=y_a[t][:, part], func=GELU)
 
-        def put_b(t):
-            nc.vector.tensor_tensor(out=z[t][:].indirect(lb_t[:]), in0=y_b[t][:], in1=wb_t[:], op=MULT)
+        def put_a(t, part=WHOLE):
+            nc.vector.tensor_tensor(
+                out=z[t][:].indirect(entries(la_t, part)), in0=gelu_a[t][:, part], in1=wa_t[:, part], op=MULT
+            )
+
+        def put_b(t, part=WHOLE):
+            nc.vector.tensor_tensor(
+                out=z[t][:].indirect(entries(lb_t, part)), in0=y_b[t][:, part], in1=wb_t[:, part], op=MULT
+            )
 
         def round_z(t):
             for c in range(CHUNKS):
@@ -187,34 +191,26 @@ def tile_picked_tworoute_gelu_po_kernel(
         nc.scalar.activation(out=y_b[0][:, cut:V], in_=y[0][:].indirect(lb_t[:, cut // GROUP : V // GROUP]), func=COPY)
         project(1)
         put_b(0)
-        fetch_b(1)
-        put_b(1)
-        fetch_a(0)
-        project(2)
-        gelu(0)
-        put_a(0)
-        fetch_a(1)
-        project(3)
-        gelu(1)
-        put_a(1)
-        w2_scale_dealt = shared.tile([P, N], U8, align_bytes=64, offset=mid_at)
+        for t in range(PACK - 1):
+            for part in PARTS:
+                fetch_a(t, part)
+                fetch_b(t + 1, part)
+                gelu(t, part)
+                put_b(t + 1, part)
+                put_a(t, part)
+                if t + 2 < PACK and part == PARTS[0]:
+                    project(t + 2)
+        fetch_a(PACK - 1)
+        gelu(PACK - 1)
+        put_a(PACK - 1)
+        w2_scale_dealt = shared.tile([P, N], U8, align_bytes=64, offset=late_at)
         nc.vector.tensor_copy(
             out=w2_scale_dealt[:].rearrange("p (t m) -> p t m", t=PACK),
             in_=w2_scale_raw[:].rearrange("p (m t) -> p t m", t=PACK),
         )
-        fetch_b(2)
-        put_b(2)
-        fetch_b(3)
-        put_b(3)
-        fetch_a(2)
-        fetch_a(3)
-        gelu(2)
-        put_a(2)
-        gelu(3)
-        put_a(3)
         round_z(0)
         round_z(1)
-        w2_codes = shared.tile([P, N], U32, align_bytes=64, offset=late_at)
+        w2_codes = shared.tile([P, N], U32, align_bytes=64, offset=late_at + N)
         nc.scalar.copy(
             out=w2_codes[:].rearrange("p (t m) -> p m t", t=PACK),
             in_=w2_word_raw[:].bitcast(U32).rearrange("p (m t) -> p m t", t=PACK),

@@ -75,10 +75,8 @@ def tile_picked_tworoute_gelu_po_kernel(
         w2_word_raw = keep.tile([P, N], I32, align_bytes=64)
 
         def load_scale_rows(tile, rows):
-            for q in range(QUADS):
-                nc.sync.dma_start(
-                    out=tile[32 * q : 32 * q + 4, :].bitcast(I32), in_=rows[0, 4 * q : 4 * q + 4, :].bitcast(I32)
-                )
+            for r in range(QUADS):
+                nc.sync.dma_start(out=tile[r:P:32, :].bitcast(I32), in_=rows[0, r : 4 * QUADS : 4, :].bitcast(I32))
 
         nc.sync.dma_start(out=w1_raw[0][:], in_=w1_rows[:, 0:2, :])
         nc.sync.dma_start(out=offs_t[:], in_=offs)
@@ -269,13 +267,11 @@ def tile_picked_tworoute_gelu_po_kernel(
                 )
                 if c == 0:
                     nc.sync.dma_start(out=out_rows[:, slots, cols], in_=o_f32[0][:, slots, cols])
-                if c == last and hi % 2 == 0:
-                    nc.sync.dma_start(out=out_rows[:, hi - 2 : hi, HALF:S], in_=o_f32[1][:, hi - 2 : hi, :])
                 if c == last and hi == 2:
                     round_out(c, 0, CHUNK, slots)
                     quantise_out(c - 1, 0, CHUNK)
-            if c == 1:
-                nc.sync.dma_start(out=out_rows[:, :, cols], in_=o_f32[0][:, :, cols])
+            if c > 0:
+                nc.sync.dma_start(out=out_rows[:, :, cols], in_=o_f32[h][:, :, first : first + CHUNK])
             if c < last:
                 round_out(c, 0, CHUNK)
             else:
@@ -283,11 +279,11 @@ def tile_picked_tworoute_gelu_po_kernel(
                 round_out(c, CHUNK // 2, CHUNK, slice(2, PACK))
             if 0 < c < last:
                 quantise_out(c - 1, 0, CHUNK)
-            if CHUNK * c == HALF:
-                nc.sync.dma_start(out=out_words[:, 0:HALF], in_=o_codes[:, 0:HALF].bitcast(I32))
+        early = CHUNK * last
+        nc.sync.dma_start(out=out_words[:, 0:early], in_=o_codes[:, 0:early].bitcast(I32))
         quantise_out(last, 0, CHUNK // 2)
         quantise_out(last, CHUNK // 2, CHUNK)
-        nc.sync.dma_start(out=out_words[:, HALF:S], in_=o_codes[:, HALF:S].bitcast(I32))
+        nc.sync.dma_start(out=out_words[:, early:S], in_=o_codes[:, early:S].bitcast(I32))
         for q in range(QUADS):
             queue = nc.scalar if q % 2 == 0 else nc.sync
             queue.dma_start(

@@ -265,12 +265,12 @@ def tile_picked_tworoute_gelu_po_kernel(
                     out=o_f32[h][:, slots, first : first + CHUNK],
                     in_=bank[:, 0 : (hi - lo) * CHUNK].rearrange("p (t n) -> p t n", t=hi - lo),
                 )
-                if c == 0:
+                if c < 2:
                     nc.sync.dma_start(out=out_rows[:, slots, cols], in_=o_f32[0][:, slots, cols])
                 if c == last and hi == 2:
                     round_out(c, 0, CHUNK, slots)
                     quantise_out(c - 1, 0, CHUNK)
-            if c > 0:
+            if c > 1:
                 nc.sync.dma_start(out=out_rows[:, :, cols], in_=o_f32[h][:, :, first : first + CHUNK])
             if c < last:
                 round_out(c, 0, CHUNK)

@@ -233,9 +233,9 @@ def tile_picked_tworoute_gelu_po_kernel(
         o_bf = [keep.tile([P, CHUNK, PACK], BF16, name=f"o_bf{c}", align_bytes=64) for c in range(CHUNKS)]
         o_f32 = [keep.tile([P, PACK, HALF], F32, name=f"o_f32_{h}") for h in range(2)]
 
-        def round_out(c, lo, hi, slots=slice(0, PACK)):
+        def round_out(c, lo, hi, slots=slice(0, PACK), copy=nc.vector.tensor_copy):
             h, first = divmod(CHUNK * c, HALF)
-            nc.vector.tensor_copy(
+            copy(
                 out=o_bf[c][:, lo:hi, slots].rearrange("p (g i) t -> p g t i", i=4),
                 in_=o_f32[h][:, slots, first + lo : first + hi].rearrange("p t (g i) -> p g t i", i=4),
             )
@@ -265,18 +265,21 @@ def tile_picked_tworoute_gelu_po_kernel(
                     out=o_f32[h][:, slots, first : first + CHUNK],
                     in_=bank[:, 0 : (hi - lo) * CHUNK].rearrange("p (t n) -> p t n", t=hi - lo),
                 )
-                if c < 2:
+                if c == 0:
                     nc.sync.dma_start(out=out_rows[:, slots, cols], in_=o_f32[0][:, slots, cols])
                 if c == last and hi == 2:
                     round_out(c, 0, CHUNK, slots)
                     quantise_out(c - 1, 0, CHUNK)
-            if c > 1:
+            if c > 0:
                 nc.sync.dma_start(out=out_rows[:, :, cols], in_=o_f32[h][:, :, first : first + CHUNK])
-            if c < last:
+            if c == 0:
+                round_out(c, 0, CHUNK, slice(0, 2))
+                round_out(c, 0, CHUNK, slice(2, PACK))
+            elif c < last:
                 round_out(c, 0, CHUNK)
             else:
                 round_out(c, 0, CHUNK // 2, slice(2, PACK))
-                round_out(c, CHUNK // 2, CHUNK, slice(2, PACK))
+                round_out(c, CHUNK // 2, CHUNK, slice(2, PACK), nc.scalar.copy)
             if 0 < c < last:
                 quantise_out(c - 1, 0, CHUNK)
         early = CHUNK * last

@@ -137,7 +137,7 @@ def tile_picked_tworoute_gelu_po_kernel(
                 g = min(t, 2)
                 w_cols = slice(P * (t - g), P * (t - g + 1))
                 mx(bank[:, 0 : hi - lo], w1_codes[g], w1_scales[g], w_cols, x_word_pick, x_scale_pick, cols)
-                copy = nc.vector.tensor_copy if t < 2 and lo == 0 else nc.scalar.copy
+                copy = nc.vector.tensor_copy if (t, lo) == (0, HALF) else nc.scalar.copy
                 copy(out=y[t][:, cols], in_=bank[:, 0 : hi - lo])
 
         z = [keep.tile([P, S], F32, name=f"z{t}") for t in range(PACK)]
@@ -184,9 +184,7 @@ def tile_picked_tworoute_gelu_po_kernel(
 
         project(0)
 
-        cut = V // 2
-        nc.vector.tensor_copy(out=y_b[0][:, 0:cut], in_=y[0][:].indirect(lb_t[:, 0 : cut // GROUP]))
-        nc.scalar.activation(out=y_b[0][:, cut:V], in_=y[0][:].indirect(lb_t[:, cut // GROUP : V // GROUP]), func=COPY)
+        nc.vector.tensor_copy(out=y_b[0][:], in_=y[0][:].indirect(lb_t[:]))
         project(1)
         put_b(0)
         for t in range(PACK - 1):

@@ -24,7 +24,7 @@ BANKS = 8
 HALF = S // 2
 CHUNK = 128
 CHUNKS = S // CHUNK
-Y_EDGES = ((0, HALF, HALF + CHUNK, S), (0, HALF, S), (0, S), (0, S))
+Y_EDGES = ((0, HALF, HALF + CHUNK, S), (0, CHUNK, HALF, S), (0, S), (0, S))
 Z_ON_VECTOR = CHUNKS // 2
 WHOLE = slice(0, V)
 PARTS = (slice(0, V // 2), slice(V // 2, V))
@@ -184,7 +184,8 @@ def tile_picked_tworoute_gelu_po_kernel(
 
         project(0)
 
-        nc.vector.tensor_copy(out=y_b[0][:], in_=y[0][:].indirect(lb_t[:]))
+        nc.vector.tensor_copy(out=y_b[0][:, PARTS[0]], in_=y[0][:].indirect(entries(lb_t, PARTS[0])))
+        fetch_b(0, PARTS[1])
         project(1)
         put_b(0)
         for t in range(PACK - 1):

@@ -251,7 +251,7 @@ def tile_picked_tworoute_gelu_po_kernel(
         for c in range(CHUNKS):
             cols = slice(CHUNK * c, CHUNK * (c + 1))
             h, first = divmod(CHUNK * c, HALF)
-            groups = ((0, 2), (2, 4)) if c < last else ((0, 2), (2, 3), (3, 4))
+            groups = ((0, 2), (2, 3), (3, 4))
             for lo, hi in groups:
                 slots = slice(lo, hi)
                 bank = psum.tile([P, S], F32, name="bank")
@@ -259,22 +259,20 @@ def tile_picked_tworoute_gelu_po_kernel(
                     w_cols = slice(P * t, P * (t + 1))
                     out_cols = slice(CHUNK * (t - lo), CHUNK * (t - lo + 1))
                     mx(bank[:, out_cols], w2_codes, w2_scale_dealt, w_cols, z_codes, z_scales, cols)
-                copy = nc.vector.tensor_copy if (c, lo) == (0, 2) else nc.scalar.copy
+                copy = nc.vector.tensor_copy if lo == 2 and c < last else nc.scalar.copy
                 copy(
                     out=o_f32[h][:, slots, first : first + CHUNK],
                     in_=bank[:, 0 : (hi - lo) * CHUNK].rearrange("p (t n) -> p t n", t=hi - lo),
                 )
-                if c == 0:
-                    nc.sync.dma_start(out=out_rows[:, slots, cols], in_=o_f32[0][:, slots, cols])
+                if c == 0 and hi % 2 == 0:
+                    pair = slice(hi - 2, hi)
+                    nc.sync.dma_start(out=out_rows[:, pair, cols], in_=o_f32[0][:, pair, cols])
                 if c == last and hi == 2:
                     round_out(c, 0, CHUNK, slots)
                     quantise_out(c - 1, 0, CHUNK)
             if c > 0:
                 nc.sync.dma_start(out=out_rows[:, :, cols], in_=o_f32[h][:, :, first : first + CHUNK])
-            if c == 0:
-                round_out(c, 0, CHUNK, slice(0, 2))
-                round_out(c, 0, CHUNK, slice(2, PACK))
-            elif c < last:
+            if c < last:
                 round_out(c, 0, CHUNK)
             else:
                 round_out(c, 0, CHUNK // 2, slice(2, PACK))

@@ -147,7 +147,8 @@ def tile_picked_tworoute_gelu_po_kernel(
         ]
         y_a = [keep.tile([P, V], F32, name=f"y_a{t}") for t in range(PACK - 1)]
         y_a.append(shared.tile([P, V], F32, name="y_a3", align_bytes=64, offset=late_at))
-        y_b = [keep.tile([P, V], F32, name=f"y_b{t}") for t in range(PACK)]
+        y_b = [keep.tile([P, V], F32, name=f"y_b{t}") for t in range(PACK - 1)]
+        y_b.append(shared.tile([P, V], F32, name="y_b3", align_bytes=64, offset=late_at + 4 * V))
         gelu_a = [keep.tile([P, V], F32, name=f"gelu_a{t}") for t in range(PACK)]
 
         def entries(lists, part):
@@ -212,6 +213,9 @@ def tile_picked_tworoute_gelu_po_kernel(
             out=w2_codes[:].rearrange("p (t m) -> p m t", t=PACK),
             in_=w2_word_raw[:].bitcast(U32).rearrange("p (m t) -> p m t", t=PACK),
         )
+        for u in range(3):
+            idle_bank = psum.tile([P, S], F32, name="bank")
+            mx(idle_bank[0:32, :], w2_codes, w2_scale_raw, slice(0, 32), w2_codes, w2_scale_raw, slice(0, N))
         round_z(2)
         round_z(PACK - 1)
 

@@ -24,10 +24,6 @@ BANKS = 8
 HALF = S // 2
 CHUNK = 128
 CHUNKS = S // CHUNK
-Y_EDGES = ((0, HALF, HALF + CHUNK, S), (0, CHUNK, HALF, S), (0, S), (0, S))
-Z_ON_VECTOR = CHUNKS // 2
-WHOLE = slice(0, V)
-PARTS = (slice(0, V // 2), slice(V // 2, V))
 
 
 def tile_picked_tworoute_gelu_po_kernel(
@@ -38,17 +34,16 @@ def tile_picked_tworoute_gelu_po_kernel(
         keep = ctx.enter_context(tc.tile_pool(name="keep", bufs=1))
         shared = ctx.enter_context(tc.tile_pool(name="shared", bufs=1))
         psum = ctx.enter_context(tc.psum_pool(name="psum", bufs=BANKS))
-        words_at = 0
+        list_bytes = 4 * V
         y_at = 4 * T
-        late_at = y_at + 2 * 4 * S
 
-        def mx(out, w_codes, w_scales, w_cols, a_codes, a_scales, a_cols):
+        def mx(out, w_codes, w_scales, a_codes, a_scales):
             nc.tensor.matmul_mx(
                 out=out,
-                lhsT=w_codes[:, w_cols].bitcast(FP8X4),
-                lhsT_scale=w_scales[:, w_cols],
-                rhs=a_codes[:, a_cols].bitcast(FP8X4),
-                rhs_scale=a_scales[:, a_cols],
+                lhsT=w_codes.bitcast(FP8X4),
+                lhsT_scale=w_scales,
+                rhs=a_codes.bitcast(FP8X4),
+                rhs_scale=a_scales,
                 start=True,
                 stop=True,
             )
@@ -69,7 +64,7 @@ def tile_picked_tworoute_gelu_po_kernel(
         offs_t = keep.tile([P, S // GROUP], U16)
         la_t = keep.tile([P, V // GROUP], U16)
         lb_t = keep.tile([P, V // GROUP], U16)
-        x_word_table = shared.tile([P, T], U32, align_bytes=64, offset=words_at)
+        x_word_table = shared.tile([P, T], U32, align_bytes=64, offset=0)
         wa_t = keep.tile([P, V], F32)
         wb_t = keep.tile([P, V], F32)
         w2_word_raw = keep.tile([P, N], I32, align_bytes=64)
@@ -86,11 +81,10 @@ def tile_picked_tworoute_gelu_po_kernel(
         )
         nc.sync.dma_start(out=w1_raw[1][:], in_=w1_rows[:, 2:4, :])
         nc.sync.dma_start(out=lb_t[:], in_=lb)
-        nc.sync.dma_start(out=wb_t[:], in_=wb.rearrange("(p t) v -> p t v", t=PACK)[:, 0, :])
         nc.sync.dma_start(out=la_t[:], in_=la)
-        nc.sync.dma_start(out=wa_t[:], in_=wa.rearrange("(p t) v -> p t v", t=PACK)[:, 0, :])
-
         nc.sync.dma_start(out=w2_word_raw[:], in_=w2_words[0].rearrange("p c r -> p (c r)").bitcast(I32))
+        nc.sync.dma_start(out=wb_t[:], in_=wb.rearrange("(p t) v -> p t v", t=PACK)[:, 0, :])
+        nc.sync.dma_start(out=wa_t[:], in_=wa.rearrange("(p t) v -> p t v", t=PACK)[:, 0, :])
         load_scale_rows(w2_scale_raw, w2_scales)
 
         x_scale_pick = keep.tile([P, S], U8, align_bytes=64)
@@ -127,97 +121,102 @@ def tile_picked_tworoute_gelu_po_kernel(
         for g in range(len(w1_groups)):
             quantise_w1(g)
 
-        y = [keep.tile([P, S], F32, name=f"y{t}") for t in (0, 1)]
-        y += [shared.tile([P, S], F32, name=f"y{t}", align_bytes=64, offset=y_at + 4 * S * (t - 2)) for t in (2, 3)]
+        def placed(shape, dtype, name, place):
+            return shared.tile(shape, dtype, name=name, align_bytes=64, offset=y_at + list_bytes * place)
+
+        y = [keep.tile([P, S], F32, name=f"y{t}") for t in range(PACK)]
 
         def project(t):
-            for lo, hi in zip(Y_EDGES[t], Y_EDGES[t][1:]):
+            edges = (0, HALF, S) if t == 0 else (0, S)
+            for lo, hi in zip(edges, edges[1:]):
                 cols = slice(lo, hi)
                 bank = psum.tile([P, S], F32, name="bank")
                 g = min(t, 2)
                 w_cols = slice(P * (t - g), P * (t - g + 1))
-                mx(bank[:, 0 : hi - lo], w1_codes[g], w1_scales[g], w_cols, x_word_pick, x_scale_pick, cols)
-                copy = nc.vector.tensor_copy if (t, lo) == (0, HALF) else nc.scalar.copy
+                mx(bank[:, 0 : hi - lo], w1_codes[g][:, w_cols], w1_scales[g][:, w_cols], x_word_pick[:, cols], x_scale_pick[:, cols])
+                copy = nc.vector.tensor_copy if lo > 0 else nc.scalar.copy
                 copy(out=y[t][:, cols], in_=bank[:, 0 : hi - lo])
 
         z = [keep.tile([P, S], F32, name=f"z{t}") for t in range(PACK)]
-        z_bf = [
-            shared.tile([P, CHUNK, PACK], BF16, name=f"z_bf{c}", align_bytes=64, offset=y_at + 2 * PACK * CHUNK * c)
-            for c in range(CHUNKS)
-        ]
-        y_a = [keep.tile([P, V], F32, name=f"y_a{t}") for t in range(PACK - 1)]
-        y_a.append(shared.tile([P, V], F32, name="y_a3", align_bytes=64, offset=late_at))
-        y_b = [keep.tile([P, V], F32, name=f"y_b{t}") for t in range(PACK - 1)]
-        y_b.append(shared.tile([P, V], F32, name="y_b3", align_bytes=64, offset=late_at + 4 * V))
+        y_a = [placed([P, V], F32, "y_a2", 1) if t == 2 else keep.tile([P, V], F32, name=f"y_a{t}") for t in range(PACK)]
         gelu_a = [keep.tile([P, V], F32, name=f"gelu_a{t}") for t in range(PACK)]
+        b = [placed([P, V], F32, "b0", 0) if t == 0 else keep.tile([P, V], F32, name=f"b{t}") for t in range(PACK)]
 
-        def entries(lists, part):
-            return lists[:, part.start // GROUP : part.stop // GROUP]
+        def fetch_b(t):
+            nc.vector.tensor_tensor(out=b[t][:], in0=y[t][:].indirect(lb_t[:]), in1=wb_t[:], op=MULT)
 
-        def fetch_a(t, part=WHOLE):
-            nc.scalar.activation(out=y_a[t][:, part], in_=y[t][:].indirect(entries(la_t, part)), func=COPY)
+        def fetch_a(t):
+            nc.scalar.activation(out=y_a[t][:], in_=y[t][:].indirect(la_t[:]), func=COPY)
 
-        def fetch_b(t, part=WHOLE):
-            nc.scalar.activation(out=y_b[t][:, part], in_=y[t][:].indirect(entries(lb_t, part)), func=COPY)
+        def gelu(t):
+            nc.scalar.activation(out=gelu_a[t][:], in_=y_a[t][:], func=GELU)
 
-        def gelu(t, part=WHOLE):
-            nc.scalar.activation(out=gelu_a[t][:, part], in_=y_a[t][:, part], func=GELU)
-
-        def put_a(t, part=WHOLE):
+        def put_a(t, lo=0, hi=V):
             nc.vector.tensor_tensor(
-                out=z[t][:].indirect(entries(la_t, part)), in0=gelu_a[t][:, part], in1=wa_t[:, part], op=MULT
+                out=z[t][:].indirect(la_t[:, lo // GROUP : hi // GROUP]), in0=gelu_a[t][:, lo:hi], in1=wa_t[:, lo:hi], op=MULT
             )
 
-        def put_b(t, part=WHOLE):
-            nc.vector.tensor_tensor(
-                out=z[t][:].indirect(entries(lb_t, part)), in0=y_b[t][:, part], in1=wb_t[:, part], op=MULT
+        def put_b(t):
+            nc.scalar.activation(out=z[t][:].indirect(lb_t[:]), in_=b[t][:], func=COPY)
+
+        w2_scale_dealt = [placed([P, 2 * P], U8, f"w2_scale_dealt{u}", u) for u in range(2)]
+
+        def deal_scales(u):
+            nc.vector.tensor_copy(
+                out=w2_scale_dealt[u][:].rearrange("p (t m) -> p t m", t=2),
+                in_=w2_scale_raw[:].rearrange("p (m t) -> p t m", t=PACK)[:, 2 * u : 2 * u + 2, :],
             )
 
-        def round_z(t):
-            for c in range(CHUNKS):
-                src = z[t][:, CHUNK * c : CHUNK * (c + 1)]
-                if t == PACK - 2 and c < Z_ON_VECTOR:
-                    nc.scalar.copy(out=z_bf[c][:, :, t : t + 2], in_=src.unsqueeze(2).to_broadcast([P, CHUNK, 2]))
-                elif t == PACK - 1 and c < Z_ON_VECTOR:
-                    nc.vector.tensor_copy(out=z_bf[c][:, :, t], in_=src)
-                else:
-                    nc.scalar.copy(out=z_bf[c][:, :, t], in_=src)
+        z_pairs = keep.tile([P, 2, S, 2], BF16, align_bytes=64)
 
-        project(0)
+        def round_z(t, cols=slice(0, S)):
+            nc.vector.tensor_copy(out=z_pairs[:, t // 2, cols, t % 2], in_=z[t][:, cols])
 
-        nc.vector.tensor_copy(out=y_b[0][:, PARTS[0]], in_=y[0][:].indirect(entries(lb_t, PARTS[0])))
-        fetch_b(0, PARTS[1])
-        project(1)
-        put_b(0)
-        for t in range(PACK - 1):
-            for part in PARTS:
-                fetch_a(t, part)
-                fetch_b(t + 1, part)
-                gelu(t, part)
-                put_b(t + 1, part)
-                put_a(t, part)
-                if t + 2 < PACK and part == PARTS[0]:
-                    project(t + 2)
-        fetch_a(PACK - 1)
-        gelu(PACK - 1)
-        put_a(PACK - 1)
-        w2_scale_dealt = shared.tile([P, N], U8, align_bytes=64, offset=late_at)
+        for t in range(PACK):
+            project(t)
+        fetch_b(0)
+        nc.vector.tensor_copy(out=y_a[1][:], in_=y[1][:].indirect(la_t[:]))
+        for t in (1, 2, 3):
+            fetch_b(t)
+        w2_codes = keep.tile([P, N], U32, align_bytes=64)
         nc.vector.tensor_copy(
-            out=w2_scale_dealt[:].rearrange("p (t m) -> p t m", t=PACK),
-            in_=w2_scale_raw[:].rearrange("p (m t) -> p t m", t=PACK),
-        )
-        round_z(0)
-        round_z(1)
-        w2_codes = shared.tile([P, N], U32, align_bytes=64, offset=late_at + N)
-        nc.scalar.copy(
             out=w2_codes[:].rearrange("p (t m) -> p m t", t=PACK),
             in_=w2_word_raw[:].bitcast(U32).rearrange("p (m t) -> p m t", t=PACK),
         )
+        fetch_a(3)
+        gelu(1)
+        fetch_a(0)
+        gelu(3)
+        gelu(0)
+        put_a(1)
+        put_a(3)
+        put_b(0)
+        fetch_a(2)
+        put_b(2)
+        gelu(2)
+        put_b(1)
+        put_b(3)
+        put_a(0)
+        deal_scales(0)
+        round_z(0)
+        put_a(2, 0, V // 2)
+        deal_scales(1)
         for u in range(3):
             idle_bank = psum.tile([P, S], F32, name="bank")
-            mx(idle_bank[0:32, :], w2_codes, w2_scale_raw, slice(0, 32), w2_codes, w2_scale_raw, slice(0, N))
+            mx(idle_bank[0:32, :], w2_codes[:, 0:32], w2_scale_dealt[1][:, 0:32], w2_codes[:], w2_scale_raw[:])
+        put_a(2, V // 2, V)
+        round_z(1)
         round_z(2)
-        round_z(PACK - 1)
+        z_bf = [keep.tile([P, CHUNK, PACK], BF16, name=f"z_bf{c}", align_bytes=64) for c in range(CHUNKS)]
+        pair_words = z_pairs[:].rearrange("p u n e -> p u (n e)").bitcast(U32)
+        for c in range(CHUNKS):
+            if c % 2 == 0:
+                round_z(3, slice(CHUNK * c, CHUNK * (c + 2)))
+            copy = nc.vector.tensor_copy if c < 2 else nc.scalar.copy
+            copy(
+                out=z_bf[c][:].rearrange("p n t -> p (n t)").bitcast(U32).rearrange("p (n u) -> p n u", u=2),
+                in_=pair_words[:, :, CHUNK * c : CHUNK * (c + 1)].rearrange("p u n -> p n u"),
+            )
 
         z_codes = keep.tile([P, S], U32, align_bytes=64)
         z_scales = keep.tile([P, S], U8, align_bytes=64)
@@ -262,7 +261,8 @@ def tile_picked_tworoute_gelu_po_kernel(
                 for t in range(lo, hi):
                     w_cols = slice(P * t, P * (t + 1))
                     out_cols = slice(CHUNK * (t - lo), CHUNK * (t - lo + 1))
-                    mx(bank[:, out_cols], w2_codes, w2_scale_dealt, w_cols, z_codes, z_scales, cols)
+                    w_scales = w2_scale_dealt[t // 2][:, P * (t % 2) : P * (t % 2 + 1)]
+                    mx(bank[:, out_cols], w2_codes[:, w_cols], w_scales, z_codes[:, cols], z_scales[:, cols])
                 copy = nc.vector.tensor_copy if lo == 2 and c < last else nc.scalar.copy
                 copy(
                     out=o_f32[h][:, slots, first : first + CHUNK],

@@ -138,9 +138,9 @@ def tile_picked_tworoute_gelu_po_kernel(
                 copy(out=y[t][:, cols], in_=bank[:, 0 : hi - lo])
 
         z = [keep.tile([P, S], F32, name=f"z{t}") for t in range(PACK)]
-        y_a = [placed([P, V], F32, "y_a2", 1) if t == 2 else keep.tile([P, V], F32, name=f"y_a{t}") for t in range(PACK)]
+        y_a = [placed([P, V], F32, "y_a2", 0) if t == 2 else keep.tile([P, V], F32, name=f"y_a{t}") for t in range(PACK)]
         gelu_a = [keep.tile([P, V], F32, name=f"gelu_a{t}") for t in range(PACK)]
-        b = [placed([P, V], F32, "b0", 0) if t == 0 else keep.tile([P, V], F32, name=f"b{t}") for t in range(PACK)]
+        b = [keep.tile([P, V], F32, name=f"b{t}") for t in range(PACK)]
 
         def fetch_b(t):
             nc.vector.tensor_tensor(out=b[t][:], in0=y[t][:].indirect(lb_t[:]), in1=wb_t[:], op=MULT)
@@ -151,62 +151,52 @@ def tile_picked_tworoute_gelu_po_kernel(
         def gelu(t):
             nc.scalar.activation(out=gelu_a[t][:], in_=y_a[t][:], func=GELU)
 
-        def put_a(t, lo=0, hi=V):
-            nc.vector.tensor_tensor(
-                out=z[t][:].indirect(la_t[:, lo // GROUP : hi // GROUP]), in0=gelu_a[t][:, lo:hi], in1=wa_t[:, lo:hi], op=MULT
-            )
+        def put_a(t):
+            nc.vector.tensor_tensor(out=z[t][:].indirect(la_t[:]), in0=gelu_a[t][:], in1=wa_t[:], op=MULT)
 
         def put_b(t):
             nc.scalar.activation(out=z[t][:].indirect(lb_t[:]), in_=b[t][:], func=COPY)
 
-        w2_scale_dealt = [placed([P, 2 * P], U8, f"w2_scale_dealt{u}", u) for u in range(2)]
-
-        def deal_scales(u):
-            nc.vector.tensor_copy(
-                out=w2_scale_dealt[u][:].rearrange("p (t m) -> p t m", t=2),
-                in_=w2_scale_raw[:].rearrange("p (m t) -> p t m", t=PACK)[:, 2 * u : 2 * u + 2, :],
-            )
-
-        z_pairs = keep.tile([P, 2, S, 2], BF16, align_bytes=64)
+        z_pairs = shared.tile([P, 2, S, 2], BF16, align_bytes=64, offset=y_at + N)
 
         def round_z(t, cols=slice(0, S)):
             nc.vector.tensor_copy(out=z_pairs[:, t // 2, cols, t % 2], in_=z[t][:, cols])
 
         for t in range(PACK):
             project(t)
-        fetch_b(0)
-        nc.vector.tensor_copy(out=y_a[1][:], in_=y[1][:].indirect(la_t[:]))
-        for t in (1, 2, 3):
+        nc.vector.tensor_copy(out=y_a[0][:], in_=y[0][:].indirect(la_t[:]))
+        for t in range(PACK):
             fetch_b(t)
         w2_codes = keep.tile([P, N], U32, align_bytes=64)
         nc.vector.tensor_copy(
             out=w2_codes[:].rearrange("p (t m) -> p m t", t=PACK),
             in_=w2_word_raw[:].bitcast(U32).rearrange("p (m t) -> p m t", t=PACK),
         )
-        fetch_a(3)
-        gelu(1)
-        fetch_a(0)
-        gelu(3)
         gelu(0)
-        put_a(1)
+        fetch_a(3)
+        fetch_a(1)
+        gelu(3)
+        gelu(1)
+        put_a(0)
         put_a(3)
-        put_b(0)
+        put_b(1)
         fetch_a(2)
         put_b(2)
         gelu(2)
-        put_b(1)
+        put_b(0)
         put_b(3)
-        put_a(0)
-        deal_scales(0)
-        round_z(0)
-        put_a(2, 0, V // 2)
-        deal_scales(1)
+        put_a(1)
+        put_a(2)
+        w2_scale_dealt = placed([P, N], U8, "w2_scale_dealt", 0)
+        nc.vector.tensor_copy(
+            out=w2_scale_dealt[:].rearrange("p (t m) -> p t m", t=PACK),
+            in_=w2_scale_raw[:].rearrange("p (m t) -> p t m", t=PACK),
+        )
         for u in range(3):
             idle_bank = psum.tile([P, S], F32, name="bank")
-            mx(idle_bank[0:32, :], w2_codes[:, 0:32], w2_scale_dealt[1][:, 0:32], w2_codes[:], w2_scale_raw[:])
-        put_a(2, V // 2, V)
-        round_z(1)
-        round_z(2)
+            mx(idle_bank[0:32, :], w2_codes[:, 0:32], w2_scale_dealt[:, 0:32], w2_codes[:], w2_scale_dealt[:])
+        for t in (1, 0, 2):
+            round_z(t)
         z_bf = [keep.tile([P, CHUNK, PACK], BF16, name=f"z_bf{c}", align_bytes=64) for c in range(CHUNKS)]
         pair_words = z_pairs[:].rearrange("p u n e -> p u (n e)").bitcast(U32)
         for c in range(CHUNKS):
@@ -261,8 +251,7 @@ def tile_picked_tworoute_gelu_po_kernel(
                 for t in range(lo, hi):
                     w_cols = slice(P * t, P * (t + 1))
                     out_cols = slice(CHUNK * (t - lo), CHUNK * (t - lo + 1))
-                    w_scales = w2_scale_dealt[t // 2][:, P * (t % 2) : P * (t % 2 + 1)]
-                    mx(bank[:, out_cols], w2_codes[:, w_cols], w_scales, z_codes[:, cols], z_scales[:, cols])
+                    mx(bank[:, out_cols], w2_codes[:, w_cols], w2_scale_dealt[:, w_cols], z_codes[:, cols], z_scales[:, cols])
                 copy = nc.vector.tensor_copy if lo == 2 and c < last else nc.scalar.copy
                 copy(
                     out=o_f32[h][:, slots, first : first + CHUNK],

@@ -53,11 +53,12 @@ def tile_picked_tworoute_gelu_po_kernel(
         nc.gpsimd.memset(table_in[:], 0.0)
         nc.scalar.activation(out=table_out[:], in_=table_in[:], func=GELU)
 
-        x_scale_table = keep.tile([P, T], U8, align_bytes=64)
+        scale_at = y_at + N + 8 * S + 4 * N - 64
+        x_scale_table = shared.tile([P, T], U8, align_bytes=64, offset=scale_at)
         nc.vector.memset(x_scale_table[:, 0 : T // 2].bitcast(I32), 0)
         nc.gpsimd.memset(x_scale_table[:, T // 2 : T].bitcast(I32), 0)
-        w2_scale_raw = keep.tile([P, N], U8, align_bytes=64)
-        nc.gpsimd.memset(w2_scale_raw[:].bitcast(I32), 0)
+        x_scale_mm = keep.tile([P, S], U8, align_bytes=64)
+        nc.gpsimd.memset(x_scale_mm[:].bitcast(I32), 0)
 
         w1_rows = w1.rearrange("(p j) c -> p j c", j=PACK)
         w1_raw = [keep.tile([P, 2, H], F32, name=f"w1_raw{pair}") for pair in range(2)]
@@ -65,9 +66,6 @@ def tile_picked_tworoute_gelu_po_kernel(
         la_t = keep.tile([P, V // GROUP], U16)
         lb_t = keep.tile([P, V // GROUP], U16)
         x_word_table = shared.tile([P, T], U32, align_bytes=64, offset=0)
-        wa_t = keep.tile([P, V], F32)
-        wb_t = keep.tile([P, V], F32)
-        w2_word_raw = keep.tile([P, N], I32, align_bytes=64)
 
         def load_scale_rows(tile, rows):
             for r in range(QUADS):
@@ -75,19 +73,27 @@ def tile_picked_tworoute_gelu_po_kernel(
 
         nc.sync.dma_start(out=w1_raw[0][:], in_=w1_rows[:, 0:2, :])
         nc.sync.dma_start(out=offs_t[:], in_=offs)
-        load_scale_rows(x_scale_table, x_scales)
+        nc.sync.dma_start(out=x_scale_table[0:P:8, :].bitcast(I32), in_=x_scales[0].bitcast(I32))
         nc.sync.dma_start(
             out=x_word_table[:].bitcast(I32), in_=x_words[0].rearrange("p c r -> p (c r)").bitcast(I32)
         )
         nc.sync.dma_start(out=w1_raw[1][:], in_=w1_rows[:, 2:4, :])
         nc.sync.dma_start(out=lb_t[:], in_=lb)
         nc.sync.dma_start(out=la_t[:], in_=la)
+        x_scale_pick = keep.tile([P, S], U8, align_bytes=64)
+        nc.vector.tensor_copy(out=x_scale_pick[:], in_=x_scale_table[:].indirect(offs_t[:]))
+        for r in range(QUADS):
+            nc.sync.dma_start(out=x_scale_mm[r:P:32, :].bitcast(I32), in_=x_scale_pick[8 * r : P : 32, :].bitcast(I32))
+        w2_word_raw = shared.tile([P, N], I32, align_bytes=64, offset=scale_at + 64 - 4 * N)
+        wb_t = shared.tile([P, V], F32, align_bytes=64, offset=scale_at + 64)
+        w2_scale_raw = shared.tile([P, N], U8, align_bytes=64, offset=scale_at + 64 + list_bytes)
+        wa_t = shared.tile([P, V], F32, align_bytes=64, offset=scale_at + 64 + list_bytes + N)
         nc.sync.dma_start(out=w2_word_raw[:], in_=w2_words[0].rearrange("p c r -> p (c r)").bitcast(I32))
         nc.sync.dma_start(out=wb_t[:], in_=wb.rearrange("(p t) v -> p t v", t=PACK)[:, 0, :])
         nc.sync.dma_start(out=wa_t[:], in_=wa.rearrange("(p t) v -> p t v", t=PACK)[:, 0, :])
+        nc.gpsimd.memset(w2_scale_raw[:].bitcast(I32), 0)
         load_scale_rows(w2_scale_raw, w2_scales)
 
-        x_scale_pick = keep.tile([P, S], U8, align_bytes=64)
         x_word_pick = keep.tile([P, S], U32, align_bytes=64)
         w1_groups = ((0, 1), (1, 2), (2, 4))
         w1_codes = [keep.tile([P, P], U32, name="w1_codes0", align_bytes=64)]
@@ -109,10 +115,9 @@ def tile_picked_tworoute_gelu_po_kernel(
                 in_=w1_bf[g][:].rearrange("p u n -> p (u n)"),
             )
 
-        round_w1(0, 0, nc.vector.tensor_copy)
-        round_w1(0, 1, nc.vector.tensor_copy)
+        round_w1(0, 0, nc.scalar.copy)
+        round_w1(0, 1, nc.scalar.copy)
         round_w1(0, 2, nc.scalar.copy)
-        nc.vector.tensor_copy(out=x_scale_pick[:], in_=x_scale_table[:].indirect(offs_t[:]))
         nc.vector.tensor_copy(out=x_word_pick[:], in_=x_word_table[:].indirect(offs_t[:]))
         round_w1(1, 0, nc.scalar.copy, slice(0, P // 2))
         round_w1(1, 0, nc.vector.tensor_copy, slice(P // 2, P))
@@ -133,7 +138,7 @@ def tile_picked_tworoute_gelu_po_kernel(
                 bank = psum.tile([P, S], F32, name="bank")
                 g = min(t, 2)
                 w_cols = slice(P * (t - g), P * (t - g + 1))
-                mx(bank[:, 0 : hi - lo], w1_codes[g][:, w_cols], w1_scales[g][:, w_cols], x_word_pick[:, cols], x_scale_pick[:, cols])
+                mx(bank[:, 0 : hi - lo], w1_codes[g][:, w_cols], w1_scales[g][:, w_cols], x_word_pick[:, cols], x_scale_mm[:, cols])
                 copy = nc.vector.tensor_copy if lo > 0 else nc.scalar.copy
                 copy(out=y[t][:, cols], in_=bank[:, 0 : hi - lo])
 

@@ -48,15 +48,17 @@ def tile_picked_tworoute_gelu_po_kernel(
                 stop=True,
             )
 
+        scale_at = y_at + N + 8 * S + 4 * N - 64
+        x_scale_table = shared.tile([P, T], U8, align_bytes=64, offset=scale_at)
+        first_row = P - 4 * QUADS
+        nc.scalar.dma_start(out=x_scale_table[first_row:P, :].bitcast(I32), in_=x_scales[0].bitcast(I32))
         table_in = keep.tile([P, 1], F32)
         table_out = keep.tile([P, 1], F32)
         nc.gpsimd.memset(table_in[:], 0.0)
         nc.scalar.activation(out=table_out[:], in_=table_in[:], func=GELU)
 
-        scale_at = y_at + N + 8 * S + 4 * N - 64
-        x_scale_table = shared.tile([P, T], U8, align_bytes=64, offset=scale_at)
-        nc.vector.memset(x_scale_table[:, 0 : T // 2].bitcast(I32), 0)
-        nc.gpsimd.memset(x_scale_table[:, T // 2 : T].bitcast(I32), 0)
+        nc.vector.memset(x_scale_table[0:96, :].bitcast(I32), 0)
+        nc.gpsimd.memset(x_scale_table[96:first_row, :].bitcast(I32), 0)
         x_scale_mm = keep.tile([P, S], U8, align_bytes=64)
         nc.gpsimd.memset(x_scale_mm[:].bitcast(I32), 0)
 
@@ -71,9 +73,8 @@ def tile_picked_tworoute_gelu_po_kernel(
             for r in range(QUADS):
                 nc.sync.dma_start(out=tile[r:P:32, :].bitcast(I32), in_=rows[0, r : 4 * QUADS : 4, :].bitcast(I32))
 
-        nc.sync.dma_start(out=w1_raw[0][:], in_=w1_rows[:, 0:2, :])
         nc.sync.dma_start(out=offs_t[:], in_=offs)
-        nc.sync.dma_start(out=x_scale_table[0:P:8, :].bitcast(I32), in_=x_scales[0].bitcast(I32))
+        nc.sync.dma_start(out=w1_raw[0][:], in_=w1_rows[:, 0:2, :])
         nc.sync.dma_start(
             out=x_word_table[:].bitcast(I32), in_=x_words[0].rearrange("p c r -> p (c r)").bitcast(I32)
         )
@@ -83,7 +84,7 @@ def tile_picked_tworoute_gelu_po_kernel(
         x_scale_pick = keep.tile([P, S], U8, align_bytes=64)
         nc.vector.tensor_copy(out=x_scale_pick[:], in_=x_scale_table[:].indirect(offs_t[:]))
         for r in range(QUADS):
-            nc.sync.dma_start(out=x_scale_mm[r:P:32, :].bitcast(I32), in_=x_scale_pick[8 * r : P : 32, :].bitcast(I32))
+            nc.sync.dma_start(out=x_scale_mm[r:P:32, :].bitcast(I32), in_=x_scale_pick[first_row + r : P : 4, :].bitcast(I32))
         w2_word_raw = shared.tile([P, N], I32, align_bytes=64, offset=scale_at + 64 - 4 * N)
         wb_t = shared.tile([P, V], F32, align_bytes=64, offset=scale_at + 64)
         w2_scale_raw = shared.tile([P, N], U8, align_bytes=64, offset=scale_at + 64 + list_bytes)

@@ -48,8 +48,7 @@ def tile_picked_tworoute_gelu_po_kernel(
                 stop=True,
             )
 
-        scale_at = y_at + N + 8 * S + 4 * N - 64
-        x_scale_table = shared.tile([P, T], U8, align_bytes=64, offset=scale_at)
+        x_scale_table = keep.tile([P, T], U8, align_bytes=64)
         first_row = P - 4 * QUADS
         nc.scalar.dma_start(out=x_scale_table[first_row:P, :].bitcast(I32), in_=x_scales[0].bitcast(I32))
         table_in = keep.tile([P, 1], F32)
@@ -74,28 +73,27 @@ def tile_picked_tworoute_gelu_po_kernel(
                 nc.sync.dma_start(out=tile[r:P:32, :].bitcast(I32), in_=rows[0, r : 4 * QUADS : 4, :].bitcast(I32))
 
         nc.sync.dma_start(out=offs_t[:], in_=offs)
-        nc.sync.dma_start(out=w1_raw[0][:], in_=w1_rows[:, 0:2, :])
         nc.sync.dma_start(
             out=x_word_table[:].bitcast(I32), in_=x_words[0].rearrange("p c r -> p (c r)").bitcast(I32)
         )
+        nc.sync.dma_start(out=w1_raw[0][:], in_=w1_rows[:, 0:2, :])
         nc.sync.dma_start(out=w1_raw[1][:], in_=w1_rows[:, 2:4, :])
         nc.sync.dma_start(out=lb_t[:], in_=lb)
         nc.sync.dma_start(out=la_t[:], in_=la)
         x_scale_pick = keep.tile([P, S], U8, align_bytes=64)
         nc.vector.tensor_copy(out=x_scale_pick[:], in_=x_scale_table[:].indirect(offs_t[:]))
         for r in range(QUADS):
-            nc.sync.dma_start(out=x_scale_mm[r:P:32, :].bitcast(I32), in_=x_scale_pick[first_row + r : P : 4, :].bitcast(I32))
-        w2_word_raw = shared.tile([P, N], I32, align_bytes=64, offset=scale_at + 64 - 4 * N)
-        wb_t = shared.tile([P, V], F32, align_bytes=64, offset=scale_at + 64)
-        w2_scale_raw = shared.tile([P, N], U8, align_bytes=64, offset=scale_at + 64 + list_bytes)
-        wa_t = shared.tile([P, V], F32, align_bytes=64, offset=scale_at + 64 + list_bytes + N)
+            nc.scalar.dma_start(out=x_scale_mm[r:P:32, :].bitcast(I32), in_=x_scale_pick[first_row + r : P : 4, :].bitcast(I32))
+        x_word_pick = keep.tile([P, S], U32, align_bytes=64)
+        nc.vector.tensor_copy(out=x_word_pick[:], in_=x_word_table[:].indirect(offs_t[:]))
+        w2_word_raw = shared.tile([P, N], I32, align_bytes=64, offset=0)
+        wb_t = shared.tile([P, V], F32, align_bytes=64, offset=4 * N)
+        wa_t = shared.tile([P, V], F32, align_bytes=64, offset=4 * N + list_bytes)
+        w2_scale_raw = shared.tile([P, N], U8, align_bytes=64, offset=4 * N + 2 * list_bytes)
         nc.sync.dma_start(out=w2_word_raw[:], in_=w2_words[0].rearrange("p c r -> p (c r)").bitcast(I32))
         nc.sync.dma_start(out=wb_t[:], in_=wb.rearrange("(p t) v -> p t v", t=PACK)[:, 0, :])
         nc.sync.dma_start(out=wa_t[:], in_=wa.rearrange("(p t) v -> p t v", t=PACK)[:, 0, :])
-        nc.gpsimd.memset(w2_scale_raw[:].bitcast(I32), 0)
-        load_scale_rows(w2_scale_raw, w2_scales)
 
-        x_word_pick = keep.tile([P, S], U32, align_bytes=64)
         w1_groups = ((0, 1), (1, 2), (2, 4))
         w1_codes = [keep.tile([P, P], U32, name="w1_codes0", align_bytes=64)]
         w1_codes += [keep.tile([P, P * (hi - lo)], U32, name=f"w1_codes{lo}", align_bytes=64) for lo, hi in w1_groups[1:]]
@@ -116,10 +114,11 @@ def tile_picked_tworoute_gelu_po_kernel(
                 in_=w1_bf[g][:].rearrange("p u n -> p (u n)"),
             )
 
-        round_w1(0, 0, nc.scalar.copy)
+        round_w1(0, 0, nc.vector.tensor_copy)
         round_w1(0, 1, nc.scalar.copy)
-        round_w1(0, 2, nc.scalar.copy)
-        nc.vector.tensor_copy(out=x_word_pick[:], in_=x_word_table[:].indirect(offs_t[:]))
+        round_w1(0, 2, nc.vector.tensor_copy)
+        nc.vector.memset(w2_scale_raw[:].bitcast(I32), 0)
+        load_scale_rows(w2_scale_raw, w2_scales)
         round_w1(1, 0, nc.scalar.copy, slice(0, P // 2))
         round_w1(1, 0, nc.vector.tensor_copy, slice(P // 2, P))
         round_w1(1, 1, nc.vector.tensor_copy)

@@ -51,6 +51,8 @@ def tile_picked_tworoute_gelu_po_kernel(
         x_scale_table = keep.tile([P, T], U8, align_bytes=64)
         first_row = P - 4 * QUADS
         nc.scalar.dma_start(out=x_scale_table[first_row:P, :].bitcast(I32), in_=x_scales[0].bitcast(I32))
+        w2_scale_raw = keep.tile([P, N], U8, align_bytes=64)
+        nc.scalar.dma_start(out=w2_scale_raw[48:64, :].bitcast(I32), in_=w2_scales[0].bitcast(I32))
         table_in = keep.tile([P, 1], F32)
         table_out = keep.tile([P, 1], F32)
         nc.gpsimd.memset(table_in[:], 0.0)
@@ -58,6 +60,8 @@ def tile_picked_tworoute_gelu_po_kernel(
 
         nc.vector.memset(x_scale_table[0:96, :].bitcast(I32), 0)
         nc.gpsimd.memset(x_scale_table[96:first_row, :].bitcast(I32), 0)
+        for lo, hi in ((0, 32), (32, 48), (64, P)):
+            nc.gpsimd.memset(w2_scale_raw[lo:hi, :].bitcast(I32), 0)
         x_scale_mm = keep.tile([P, S], U8, align_bytes=64)
         nc.gpsimd.memset(x_scale_mm[:].bitcast(I32), 0)
 
@@ -67,10 +71,6 @@ def tile_picked_tworoute_gelu_po_kernel(
         la_t = keep.tile([P, V // GROUP], U16)
         lb_t = keep.tile([P, V // GROUP], U16)
         x_word_table = shared.tile([P, T], U32, align_bytes=64, offset=0)
-
-        def load_scale_rows(tile, rows):
-            for r in range(QUADS):
-                nc.sync.dma_start(out=tile[r:P:32, :].bitcast(I32), in_=rows[0, r : 4 * QUADS : 4, :].bitcast(I32))
 
         nc.sync.dma_start(out=offs_t[:], in_=offs)
         nc.sync.dma_start(
@@ -84,12 +84,16 @@ def tile_picked_tworoute_gelu_po_kernel(
         nc.vector.tensor_copy(out=x_scale_pick[:], in_=x_scale_table[:].indirect(offs_t[:]))
         for r in range(QUADS):
             nc.scalar.dma_start(out=x_scale_mm[r:P:32, :].bitcast(I32), in_=x_scale_pick[first_row + r : P : 4, :].bitcast(I32))
+        w2_scale_dealt = keep.tile([P, N], U8, align_bytes=64)
+        nc.vector.tensor_copy(
+            out=w2_scale_dealt[:].rearrange("p (t m) -> p t m", t=PACK),
+            in_=w2_scale_raw[:].rearrange("p (m t) -> p t m", t=PACK),
+        )
         x_word_pick = keep.tile([P, S], U32, align_bytes=64)
         nc.vector.tensor_copy(out=x_word_pick[:], in_=x_word_table[:].indirect(offs_t[:]))
         w2_word_raw = shared.tile([P, N], I32, align_bytes=64, offset=0)
         wb_t = shared.tile([P, V], F32, align_bytes=64, offset=4 * N)
         wa_t = shared.tile([P, V], F32, align_bytes=64, offset=4 * N + list_bytes)
-        w2_scale_raw = shared.tile([P, N], U8, align_bytes=64, offset=4 * N + 2 * list_bytes)
         nc.sync.dma_start(out=w2_word_raw[:], in_=w2_words[0].rearrange("p c r -> p (c r)").bitcast(I32))
         nc.sync.dma_start(out=wb_t[:], in_=wb.rearrange("(p t) v -> p t v", t=PACK)[:, 0, :])
         nc.sync.dma_start(out=wa_t[:], in_=wa.rearrange("(p t) v -> p t v", t=PACK)[:, 0, :])
@@ -117,8 +121,6 @@ def tile_picked_tworoute_gelu_po_kernel(
         round_w1(0, 0, nc.vector.tensor_copy)
         round_w1(0, 1, nc.scalar.copy)
         round_w1(0, 2, nc.vector.tensor_copy)
-        nc.vector.memset(w2_scale_raw[:].bitcast(I32), 0)
-        load_scale_rows(w2_scale_raw, w2_scales)
         round_w1(1, 0, nc.scalar.copy, slice(0, P // 2))
         round_w1(1, 0, nc.vector.tensor_copy, slice(P // 2, P))
         round_w1(1, 1, nc.vector.tensor_copy)
@@ -132,20 +134,20 @@ def tile_picked_tworoute_gelu_po_kernel(
         y = [keep.tile([P, S], F32, name=f"y{t}") for t in range(PACK)]
 
         def project(t):
-            edges = (0, HALF, S) if t == 0 else (0, S)
+            edges = (0, HALF, S)
             for lo, hi in zip(edges, edges[1:]):
                 cols = slice(lo, hi)
                 bank = psum.tile([P, S], F32, name="bank")
                 g = min(t, 2)
                 w_cols = slice(P * (t - g), P * (t - g + 1))
                 mx(bank[:, 0 : hi - lo], w1_codes[g][:, w_cols], w1_scales[g][:, w_cols], x_word_pick[:, cols], x_scale_mm[:, cols])
-                copy = nc.vector.tensor_copy if lo > 0 else nc.scalar.copy
-                copy(out=y[t][:, cols], in_=bank[:, 0 : hi - lo])
+                nc.scalar.copy(out=y[t][:, cols], in_=bank[:, 0 : hi - lo])
 
         z = [keep.tile([P, S], F32, name=f"z{t}") for t in range(PACK)]
         y_a = [placed([P, V], F32, "y_a2", 0) if t == 2 else keep.tile([P, V], F32, name=f"y_a{t}") for t in range(PACK)]
         gelu_a = [keep.tile([P, V], F32, name=f"gelu_a{t}") for t in range(PACK)]
-        b = [keep.tile([P, V], F32, name=f"b{t}") for t in range(PACK)]
+        b_at = y_at + N + 8 * S
+        b = [shared.tile([P, V], F32, name="b2", align_bytes=64, offset=b_at) if t == 2 else keep.tile([P, V], F32, name=f"b{t}") for t in range(PACK)]
 
         def fetch_b(t):
             nc.vector.tensor_tensor(out=b[t][:], in0=y[t][:].indirect(lb_t[:]), in1=wb_t[:], op=MULT)
@@ -192,14 +194,13 @@ def tile_picked_tworoute_gelu_po_kernel(
         put_b(3)
         put_a(1)
         put_a(2)
-        w2_scale_dealt = placed([P, N], U8, "w2_scale_dealt", 0)
-        nc.vector.tensor_copy(
-            out=w2_scale_dealt[:].rearrange("p (t m) -> p t m", t=PACK),
-            in_=w2_scale_raw[:].rearrange("p (m t) -> p t m", t=PACK),
-        )
+        w2_scale_mm = shared.tile([P, N], U8, align_bytes=64, offset=b_at)
+        nc.gpsimd.memset(w2_scale_mm[:].bitcast(I32), 0)
+        for r in range(QUADS):
+            nc.sync.dma_start(out=w2_scale_mm[r:P:32, :].bitcast(I32), in_=w2_scale_dealt[48 + r : 64 : 4, :].bitcast(I32))
         for u in range(3):
             idle_bank = psum.tile([P, S], F32, name="bank")
-            mx(idle_bank[0:32, :], w2_codes[:, 0:32], w2_scale_dealt[:, 0:32], w2_codes[:], w2_scale_dealt[:])
+            mx(idle_bank[0:32, :], w2_codes[:, 0:32], w2_scale_mm[:, 0:32], w2_codes[:], w2_scale_mm[:])
         for t in (1, 0, 2):
             round_z(t)
         z_bf = [keep.tile([P, CHUNK, PACK], BF16, name=f"z_bf{c}", align_bytes=64) for c in range(CHUNKS)]
@@ -256,7 +257,7 @@ def tile_picked_tworoute_gelu_po_kernel(
                 for t in range(lo, hi):
                     w_cols = slice(P * t, P * (t + 1))
                     out_cols = slice(CHUNK * (t - lo), CHUNK * (t - lo + 1))
-                    mx(bank[:, out_cols], w2_codes[:, w_cols], w2_scale_dealt[:, w_cols], z_codes[:, cols], z_scales[:, cols])
+                    mx(bank[:, out_cols], w2_codes[:, w_cols], w2_scale_mm[:, w_cols], z_codes[:, cols], z_scales[:, cols])
                 copy = nc.vector.tensor_copy if lo == 2 and c < last else nc.scalar.copy
                 copy(
                     out=o_f32[h][:, slots, first : first + CHUNK],

@@ -48,7 +48,8 @@ def tile_picked_tworoute_gelu_po_kernel(
                 stop=True,
             )
 
-        x_scale_table = keep.tile([P, T], U8, align_bytes=64)
+        scale_at = y_at + N + 8 * S + list_bytes
+        x_scale_table = shared.tile([P, T], U8, align_bytes=64, offset=scale_at)
         first_row = P - 4 * QUADS
         nc.scalar.dma_start(out=x_scale_table[first_row:P, :].bitcast(I32), in_=x_scales[0].bitcast(I32))
         w2_scale_raw = keep.tile([P, N], U8, align_bytes=64)
@@ -84,6 +85,8 @@ def tile_picked_tworoute_gelu_po_kernel(
         nc.vector.tensor_copy(out=x_scale_pick[:], in_=x_scale_table[:].indirect(offs_t[:]))
         for r in range(QUADS):
             nc.scalar.dma_start(out=x_scale_mm[r:P:32, :].bitcast(I32), in_=x_scale_pick[first_row + r : P : 4, :].bitcast(I32))
+        w2_word_raw = shared.tile([P, N], I32, align_bytes=64, offset=scale_at)
+        nc.scalar.dma_start(out=w2_word_raw[:], in_=w2_words[0].rearrange("p c r -> p (c r)").bitcast(I32))
         w2_scale_dealt = keep.tile([P, N], U8, align_bytes=64)
         nc.vector.tensor_copy(
             out=w2_scale_dealt[:].rearrange("p (t m) -> p t m", t=PACK),
@@ -91,10 +94,8 @@ def tile_picked_tworoute_gelu_po_kernel(
         )
         x_word_pick = keep.tile([P, S], U32, align_bytes=64)
         nc.vector.tensor_copy(out=x_word_pick[:], in_=x_word_table[:].indirect(offs_t[:]))
-        w2_word_raw = shared.tile([P, N], I32, align_bytes=64, offset=0)
         wb_t = shared.tile([P, V], F32, align_bytes=64, offset=4 * N)
         wa_t = shared.tile([P, V], F32, align_bytes=64, offset=4 * N + list_bytes)
-        nc.sync.dma_start(out=w2_word_raw[:], in_=w2_words[0].rearrange("p c r -> p (c r)").bitcast(I32))
         nc.sync.dma_start(out=wb_t[:], in_=wb.rearrange("(p t) v -> p t v", t=PACK)[:, 0, :])
         nc.sync.dma_start(out=wa_t[:], in_=wa.rearrange("(p t) v -> p t v", t=PACK)[:, 0, :])
 
@@ -144,10 +145,12 @@ def tile_picked_tworoute_gelu_po_kernel(
                 nc.scalar.copy(out=y[t][:, cols], in_=bank[:, 0 : hi - lo])
 
         z = [keep.tile([P, S], F32, name=f"z{t}") for t in range(PACK)]
-        y_a = [placed([P, V], F32, "y_a2", 0) if t == 2 else keep.tile([P, V], F32, name=f"y_a{t}") for t in range(PACK)]
-        gelu_a = [keep.tile([P, V], F32, name=f"gelu_a{t}") for t in range(PACK)]
+        y_a = {t: keep.tile([P, V], F32, name=f"y_a{t}") for t in (1, 3)}
+        y_a[0] = shared.tile([P, V], F32, name="y_a_first", align_bytes=64, offset=scale_at)
+        y_a[2] = placed([P, V], F32, "y_a_late", 0)
         b_at = y_at + N + 8 * S
-        b = [shared.tile([P, V], F32, name="b2", align_bytes=64, offset=b_at) if t == 2 else keep.tile([P, V], F32, name=f"b{t}") for t in range(PACK)]
+        gelu_a = [shared.tile([P, V], F32, name="gelu_a3", align_bytes=64, offset=b_at) if t == 3 else keep.tile([P, V], F32, name=f"gelu_a{t}") for t in range(PACK)]
+        b = [keep.tile([P, V], F32, name=f"b{t}") for t in range(PACK)]
 
         def fetch_b(t):
             nc.vector.tensor_tensor(out=b[t][:], in0=y[t][:].indirect(lb_t[:]), in1=wb_t[:], op=MULT)
@@ -171,14 +174,14 @@ def tile_picked_tworoute_gelu_po_kernel(
 
         for t in range(PACK):
             project(t)
-        nc.vector.tensor_copy(out=y_a[0][:], in_=y[0][:].indirect(la_t[:]))
-        for t in range(PACK):
-            fetch_b(t)
         w2_codes = keep.tile([P, N], U32, align_bytes=64)
         nc.vector.tensor_copy(
             out=w2_codes[:].rearrange("p (t m) -> p m t", t=PACK),
             in_=w2_word_raw[:].bitcast(U32).rearrange("p (m t) -> p m t", t=PACK),
         )
+        nc.vector.tensor_copy(out=y_a[0][:], in_=y[0][:].indirect(la_t[:]))
+        for t in range(PACK):
+            fetch_b(t)
         gelu(0)
         fetch_a(3)
         fetch_a(1)

@@ -48,7 +48,7 @@ def tile_picked_tworoute_gelu_po_kernel(
                 stop=True,
             )
 
-        scale_at = y_at + N + 8 * S + list_bytes
+        scale_at = y_at + N + 8 * S
         x_scale_table = shared.tile([P, T], U8, align_bytes=64, offset=scale_at)
         first_row = P - 4 * QUADS
         nc.scalar.dma_start(out=x_scale_table[first_row:P, :].bitcast(I32), in_=x_scales[0].bitcast(I32))
@@ -61,17 +61,17 @@ def tile_picked_tworoute_gelu_po_kernel(
 
         nc.vector.memset(x_scale_table[0:96, :].bitcast(I32), 0)
         nc.gpsimd.memset(x_scale_table[96:first_row, :].bitcast(I32), 0)
-        for lo, hi in ((0, 32), (32, 48), (64, P)):
-            nc.gpsimd.memset(w2_scale_raw[lo:hi, :].bitcast(I32), 0)
         x_scale_mm = keep.tile([P, S], U8, align_bytes=64)
         nc.gpsimd.memset(x_scale_mm[:].bitcast(I32), 0)
+        for lo, hi in ((0, 32), (32, 48), (64, P)):
+            nc.gpsimd.memset(w2_scale_raw[lo:hi, :].bitcast(I32), 0)
 
         w1_rows = w1.rearrange("(p j) c -> p j c", j=PACK)
-        w1_raw = [keep.tile([P, 2, H], F32, name=f"w1_raw{pair}") for pair in range(2)]
+        w1_raw = [shared.tile([P, 2, H], F32, name="w1_raw0", align_bytes=64, offset=0), keep.tile([P, 2, H], F32, name="w1_raw1")]
         offs_t = keep.tile([P, S // GROUP], U16)
         la_t = keep.tile([P, V // GROUP], U16)
         lb_t = keep.tile([P, V // GROUP], U16)
-        x_word_table = shared.tile([P, T], U32, align_bytes=64, offset=0)
+        x_word_table = keep.tile([P, T], U32, align_bytes=64)
 
         nc.sync.dma_start(out=offs_t[:], in_=offs)
         nc.sync.dma_start(
@@ -94,16 +94,18 @@ def tile_picked_tworoute_gelu_po_kernel(
         )
         x_word_pick = keep.tile([P, S], U32, align_bytes=64)
         nc.vector.tensor_copy(out=x_word_pick[:], in_=x_word_table[:].indirect(offs_t[:]))
-        wb_t = shared.tile([P, V], F32, align_bytes=64, offset=4 * N)
-        wa_t = shared.tile([P, V], F32, align_bytes=64, offset=4 * N + list_bytes)
-        nc.sync.dma_start(out=wb_t[:], in_=wb.rearrange("(p t) v -> p t v", t=PACK)[:, 0, :])
-        nc.sync.dma_start(out=wa_t[:], in_=wa.rearrange("(p t) v -> p t v", t=PACK)[:, 0, :])
 
         w1_groups = ((0, 1), (1, 2), (2, 4))
         w1_codes = [keep.tile([P, P], U32, name="w1_codes0", align_bytes=64)]
         w1_codes += [keep.tile([P, P * (hi - lo)], U32, name=f"w1_codes{lo}", align_bytes=64) for lo, hi in w1_groups[1:]]
         w1_scales = [keep.tile([P, P * (hi - lo)], U8, name=f"w1_scales{lo}", align_bytes=64) for lo, hi in w1_groups]
-        w1_bf = [keep.tile([P, hi - lo, H], BF16, name=f"w1_bf{lo}", align_bytes=64) for lo, hi in w1_groups]
+        dealt_at = scale_at + T
+        w1_bf = [
+            shared.tile([P, 1, H], BF16, name=f"w1_bf{lo}", align_bytes=64, offset=dealt_at + (1 - lo) * 6 * list_bytes // 4)
+            if lo < 2
+            else keep.tile([P, hi - lo, H], BF16, name=f"w1_bf{lo}", align_bytes=64)
+            for lo, hi in w1_groups
+        ]
 
         def round_w1(rows, g, copy, part=slice(0, P)):
             lo, hi = w1_groups[g]
@@ -122,12 +124,21 @@ def tile_picked_tworoute_gelu_po_kernel(
         round_w1(0, 0, nc.vector.tensor_copy)
         round_w1(0, 1, nc.scalar.copy)
         round_w1(0, 2, nc.vector.tensor_copy)
+        wb_t = shared.tile([P, V], F32, align_bytes=64, offset=0)
+        wa_t = shared.tile([P, V], F32, align_bytes=64, offset=list_bytes)
+        nc.sync.dma_start(out=wb_t[:], in_=wb.rearrange("(p t) v -> p t v", t=PACK)[:, 0, :])
+        nc.sync.dma_start(out=wa_t[:], in_=wa.rearrange("(p t) v -> p t v", t=PACK)[:, 0, :])
         round_w1(1, 0, nc.scalar.copy, slice(0, P // 2))
         round_w1(1, 0, nc.vector.tensor_copy, slice(P // 2, P))
         round_w1(1, 1, nc.vector.tensor_copy)
         round_w1(1, 2, nc.scalar.copy)
         for g in range(len(w1_groups)):
             quantise_w1(g)
+
+        w2_scale_mm = shared.tile([P, N], U8, align_bytes=64, offset=dealt_at + 6 * list_bytes // 4)
+        nc.vector.memset(w2_scale_mm[:].bitcast(I32), 0)
+        for r in range(QUADS):
+            nc.sync.dma_start(out=w2_scale_mm[r:P:32, :].bitcast(I32), in_=w2_scale_dealt[48 + r : 64 : 4, :].bitcast(I32))
 
         def placed(shape, dtype, name, place):
             return shared.tile(shape, dtype, name=name, align_bytes=64, offset=y_at + list_bytes * place)
@@ -145,12 +156,9 @@ def tile_picked_tworoute_gelu_po_kernel(
                 nc.scalar.copy(out=y[t][:, cols], in_=bank[:, 0 : hi - lo])
 
         z = [keep.tile([P, S], F32, name=f"z{t}") for t in range(PACK)]
-        y_a = {t: keep.tile([P, V], F32, name=f"y_a{t}") for t in (1, 3)}
-        y_a[0] = shared.tile([P, V], F32, name="y_a_first", align_bytes=64, offset=scale_at)
-        y_a[2] = placed([P, V], F32, "y_a_late", 0)
-        b_at = y_at + N + 8 * S
-        gelu_a = [shared.tile([P, V], F32, name="gelu_a3", align_bytes=64, offset=b_at) if t == 3 else keep.tile([P, V], F32, name=f"gelu_a{t}") for t in range(PACK)]
-        b = [keep.tile([P, V], F32, name=f"b{t}") for t in range(PACK)]
+        y_a = [keep.tile([P, V], F32, name=f"y_a{t}") for t in range(PACK)]
+        gelu_a = [keep.tile([P, V], F32, name=f"gelu_a{t}") for t in range(PACK)]
+        b = [placed([P, V], F32, "b0", 0) if t == 0 else keep.tile([P, V], F32, name=f"b{t}") for t in range(PACK)]
 
         def fetch_b(t):
             nc.vector.tensor_tensor(out=b[t][:], in0=y[t][:].indirect(lb_t[:]), in1=wb_t[:], op=MULT)
@@ -167,50 +175,47 @@ def tile_picked_tworoute_gelu_po_kernel(
         def put_b(t):
             nc.scalar.activation(out=z[t][:].indirect(lb_t[:]), in_=b[t][:], func=COPY)
 
-        z_pairs = shared.tile([P, 2, S, 2], BF16, align_bytes=64, offset=y_at + N)
+        z_pairs = keep.tile([P, 2, S, 2], BF16, align_bytes=64)
 
         def round_z(t, cols=slice(0, S)):
             nc.vector.tensor_copy(out=z_pairs[:, t // 2, cols, t % 2], in_=z[t][:, cols])
 
         for t in range(PACK):
             project(t)
-        w2_codes = keep.tile([P, N], U32, align_bytes=64)
-        nc.vector.tensor_copy(
-            out=w2_codes[:].rearrange("p (t m) -> p m t", t=PACK),
-            in_=w2_word_raw[:].bitcast(U32).rearrange("p (m t) -> p m t", t=PACK),
-        )
+        w2_words_by_slot = w2_word_raw[:].bitcast(U32).rearrange("p (m t) -> p m t", t=PACK)
+        w2_codes_rest = shared.tile([P, PACK - 1, P], U32, align_bytes=64, offset=dealt_at)
+        nc.vector.tensor_copy(out=w2_codes_rest[:].rearrange("p t m -> p m t"), in_=w2_words_by_slot[:, :, 1:PACK])
         nc.vector.tensor_copy(out=y_a[0][:], in_=y[0][:].indirect(la_t[:]))
-        for t in range(PACK):
+        for t in (0, 1, 2, 3):
             fetch_b(t)
         gelu(0)
         fetch_a(3)
         fetch_a(1)
         gelu(3)
+        fetch_a(2)
         gelu(1)
+        gelu(2)
         put_a(0)
         put_a(3)
         put_b(1)
-        fetch_a(2)
-        put_b(2)
-        gelu(2)
         put_b(0)
-        put_b(3)
-        put_a(1)
         put_a(2)
-        w2_scale_mm = shared.tile([P, N], U8, align_bytes=64, offset=b_at)
-        nc.gpsimd.memset(w2_scale_mm[:].bitcast(I32), 0)
-        for r in range(QUADS):
-            nc.sync.dma_start(out=w2_scale_mm[r:P:32, :].bitcast(I32), in_=w2_scale_dealt[48 + r : 64 : 4, :].bitcast(I32))
+        put_a(1)
+        put_b(3)
+        put_b(2)
+        w2_codes_first = placed([P, P], U32, "w2_codes_first", 0)
+        nc.vector.tensor_copy(out=w2_codes_first[:], in_=w2_words_by_slot[:, :, 0])
+        w2_codes = [w2_codes_first[:]] + [w2_codes_rest[:, t, :] for t in range(PACK - 1)]
         for u in range(3):
             idle_bank = psum.tile([P, S], F32, name="bank")
-            mx(idle_bank[0:32, :], w2_codes[:, 0:32], w2_scale_mm[:, 0:32], w2_codes[:], w2_scale_mm[:])
-        for t in (1, 0, 2):
+            mx(idle_bank[0:32, :], w2_codes_first[:, 0:32], w2_scale_mm[:, 0:32], w2_word_raw[:], w2_scale_mm[:])
+        for t in (0, 3, 1):
             round_z(t)
         z_bf = [keep.tile([P, CHUNK, PACK], BF16, name=f"z_bf{c}", align_bytes=64) for c in range(CHUNKS)]
         pair_words = z_pairs[:].rearrange("p u n e -> p u (n e)").bitcast(U32)
         for c in range(CHUNKS):
             if c % 2 == 0:
-                round_z(3, slice(CHUNK * c, CHUNK * (c + 2)))
+                round_z(2, slice(CHUNK * c, CHUNK * (c + 2)))
             copy = nc.vector.tensor_copy if c < 2 else nc.scalar.copy
             copy(
                 out=z_bf[c][:].rearrange("p n t -> p (n t)").bitcast(U32).rearrange("p (n u) -> p n u", u=2),
@@ -260,7 +265,7 @@ def tile_picked_tworoute_gelu_po_kernel(
                 for t in range(lo, hi):
                     w_cols = slice(P * t, P * (t + 1))
                     out_cols = slice(CHUNK * (t - lo), CHUNK * (t - lo + 1))
-                    mx(bank[:, out_cols], w2_codes[:, w_cols], w2_scale_mm[:, w_cols], z_codes[:, cols], z_scales[:, cols])
+                    mx(bank[:, out_cols], w2_codes[t], w2_scale_mm[:, w_cols], z_codes[:, cols], z_scales[:, cols])
                 copy = nc.vector.tensor_copy if lo == 2 and c < last else nc.scalar.copy
                 copy(
                     out=o_f32[h][:, slots, first : first + CHUNK],

@@ -156,44 +156,40 @@ def tile_picked_tworoute_gelu_po_kernel(
                 nc.scalar.copy(out=y[t][:, cols], in_=bank[:, 0 : hi - lo])
 
         z = [keep.tile([P, S], F32, name=f"z{t}") for t in range(PACK)]
-        y_a = [keep.tile([P, V], F32, name=f"y_a{t}") for t in range(PACK)]
-        gelu_a = [keep.tile([P, V], F32, name=f"gelu_a{t}") for t in range(PACK)]
+        y_a_odd = keep.tile([P, 2, V], F32)
+        gelu_a_odd = keep.tile([P, 2, V], F32)
+        y_a = [y_a_odd[:, t // 2, :] if t % 2 else keep.tile([P, V], F32, name=f"y_a{t}")[:] for t in range(PACK)]
+        gelu_a = [gelu_a_odd[:, t // 2, :] if t % 2 else keep.tile([P, V], F32, name=f"gelu_a{t}")[:] for t in range(PACK)]
         b = [placed([P, V], F32, "b0", 0) if t == 0 else keep.tile([P, V], F32, name=f"b{t}") for t in range(PACK)]
 
         def fetch_b(t):
             nc.vector.tensor_tensor(out=b[t][:], in0=y[t][:].indirect(lb_t[:]), in1=wb_t[:], op=MULT)
 
         def fetch_a(t):
-            nc.scalar.activation(out=y_a[t][:], in_=y[t][:].indirect(la_t[:]), func=COPY)
+            nc.scalar.activation(out=y_a[t], in_=y[t][:].indirect(la_t[:]), func=COPY)
 
         def gelu(t):
-            nc.scalar.activation(out=gelu_a[t][:], in_=y_a[t][:], func=GELU)
+            nc.scalar.activation(out=gelu_a[t], in_=y_a[t], func=GELU)
 
         def put_a(t):
-            nc.vector.tensor_tensor(out=z[t][:].indirect(la_t[:]), in0=gelu_a[t][:], in1=wa_t[:], op=MULT)
+            nc.vector.tensor_tensor(out=z[t][:].indirect(la_t[:]), in0=gelu_a[t], in1=wa_t[:], op=MULT)
 
         def put_b(t):
             nc.scalar.activation(out=z[t][:].indirect(lb_t[:]), in_=b[t][:], func=COPY)
-
-        z_pairs = keep.tile([P, 2, S, 2], BF16, align_bytes=64)
-
-        def round_z(t, cols=slice(0, S)):
-            nc.vector.tensor_copy(out=z_pairs[:, t // 2, cols, t % 2], in_=z[t][:, cols])
 
         for t in range(PACK):
             project(t)
         w2_words_by_slot = w2_word_raw[:].bitcast(U32).rearrange("p (m t) -> p m t", t=PACK)
         w2_codes_rest = shared.tile([P, PACK - 1, P], U32, align_bytes=64, offset=dealt_at)
         nc.vector.tensor_copy(out=w2_codes_rest[:].rearrange("p t m -> p m t"), in_=w2_words_by_slot[:, :, 1:PACK])
-        nc.vector.tensor_copy(out=y_a[0][:], in_=y[0][:].indirect(la_t[:]))
+        nc.vector.tensor_copy(out=y_a[0], in_=y[0][:].indirect(la_t[:]))
         for t in (0, 1, 2, 3):
             fetch_b(t)
         gelu(0)
         fetch_a(3)
         fetch_a(1)
-        gelu(3)
         fetch_a(2)
-        gelu(1)
+        nc.scalar.activation(out=gelu_a_odd[:], in_=y_a_odd[:], func=GELU)
         gelu(2)
         put_a(0)
         put_a(3)
@@ -209,28 +205,45 @@ def tile_picked_tworoute_gelu_po_kernel(
         for u in range(3):
             idle_bank = psum.tile([P, S], F32, name="bank")
             mx(idle_bank[0:32, :], w2_codes_first[:, 0:32], w2_scale_mm[:, 0:32], w2_word_raw[:], w2_scale_mm[:])
-        for t in (0, 3, 1):
-            round_z(t)
+        z_pairs = keep.tile([P, 2, S - CHUNK, 2], BF16, align_bytes=64)
         z_bf = [keep.tile([P, CHUNK, PACK], BF16, name=f"z_bf{c}", align_bytes=64) for c in range(CHUNKS)]
         pair_words = z_pairs[:].rearrange("p u n e -> p u (n e)").bitcast(U32)
-        for c in range(CHUNKS):
-            if c % 2 == 0:
-                round_z(2, slice(CHUNK * c, CHUNK * (c + 2)))
-            copy = nc.vector.tensor_copy if c < 2 else nc.scalar.copy
-            copy(
-                out=z_bf[c][:].rearrange("p n t -> p (n t)").bitcast(U32).rearrange("p (n u) -> p n u", u=2),
-                in_=pair_words[:, :, CHUNK * c : CHUNK * (c + 1)].rearrange("p u n -> p n u"),
-            )
 
+        def round_first(t):
+            nc.vector.tensor_copy(out=z_bf[0][:, :, t], in_=z[t][:, 0:CHUNK])
+
+        def round_z(t, lo=CHUNK, hi=S):
+            nc.vector.tensor_copy(out=z_pairs[:, t // 2, lo - CHUNK : hi - CHUNK, t % 2], in_=z[t][:, lo:hi])
+
+        for t in (0, 3, 1):
+            round_first(t)
+            round_z(t)
         z_codes = keep.tile([P, S], U32, align_bytes=64)
         z_scales = keep.tile([P, S], U8, align_bytes=64)
-        for c in range(CHUNKS):
+
+        def weave(c, copy):
+            copy(
+                out=z_bf[c][:].rearrange("p n t -> p (n t)").bitcast(U32).rearrange("p (n u) -> p n u", u=2),
+                in_=pair_words[:, :, CHUNK * (c - 1) : CHUNK * c].rearrange("p u n -> p n u"),
+            )
+
+        def quantise_z(c):
             cols = slice(CHUNK * c, CHUNK * (c + 1))
             nc.vector.quantize_mx(
                 out=z_codes[:, cols].bitcast(FP8X4),
                 scales=z_scales[:, cols],
                 in_=z_bf[c][:].rearrange("p n t -> p (n t)"),
             )
+
+        round_first(2)
+        round_z(2, CHUNK, HALF)
+        round_z(2, HALF, S)
+        quantise_z(0)
+        weave(1, nc.vector.tensor_copy)
+        weave(2, nc.scalar.copy)
+        weave(3, nc.scalar.copy)
+        for c in range(1, CHUNKS):
+            quantise_z(c)
 
         out_rows = out_0.rearrange("(p t) j -> p t j", t=PACK)
         out_words = out_1[0].rearrange("p c r -> p (c r)").bitcast(I32)

@@ -48,8 +48,7 @@ def tile_picked_tworoute_gelu_po_kernel(
                 stop=True,
             )
 
-        scale_at = y_at + N + 8 * S
-        x_scale_table = shared.tile([P, T], U8, align_bytes=64, offset=scale_at)
+        x_scale_table = keep.tile([P, T], U8, align_bytes=64)
         first_row = P - 4 * QUADS
         nc.scalar.dma_start(out=x_scale_table[first_row:P, :].bitcast(I32), in_=x_scales[0].bitcast(I32))
         w2_scale_raw = keep.tile([P, N], U8, align_bytes=64)
@@ -79,19 +78,14 @@ def tile_picked_tworoute_gelu_po_kernel(
         )
         nc.sync.dma_start(out=w1_raw[0][:], in_=w1_rows[:, 0:2, :])
         nc.sync.dma_start(out=w1_raw[1][:], in_=w1_rows[:, 2:4, :])
+        w2_word_raw = keep.tile([P, N], I32, align_bytes=64)
+        nc.sync.dma_start(out=w2_word_raw[:], in_=w2_words[0].rearrange("p c r -> p (c r)").bitcast(I32))
         nc.sync.dma_start(out=lb_t[:], in_=lb)
         nc.sync.dma_start(out=la_t[:], in_=la)
         x_scale_pick = keep.tile([P, S], U8, align_bytes=64)
         nc.vector.tensor_copy(out=x_scale_pick[:], in_=x_scale_table[:].indirect(offs_t[:]))
         for r in range(QUADS):
             nc.scalar.dma_start(out=x_scale_mm[r:P:32, :].bitcast(I32), in_=x_scale_pick[first_row + r : P : 4, :].bitcast(I32))
-        w2_word_raw = shared.tile([P, N], I32, align_bytes=64, offset=scale_at)
-        nc.scalar.dma_start(out=w2_word_raw[:], in_=w2_words[0].rearrange("p c r -> p (c r)").bitcast(I32))
-        w2_scale_dealt = keep.tile([P, N], U8, align_bytes=64)
-        nc.vector.tensor_copy(
-            out=w2_scale_dealt[:].rearrange("p (t m) -> p t m", t=PACK),
-            in_=w2_scale_raw[:].rearrange("p (m t) -> p t m", t=PACK),
-        )
         x_word_pick = keep.tile([P, S], U32, align_bytes=64)
         nc.vector.tensor_copy(out=x_word_pick[:], in_=x_word_table[:].indirect(offs_t[:]))
 
@@ -99,7 +93,7 @@ def tile_picked_tworoute_gelu_po_kernel(
         w1_codes = [keep.tile([P, P], U32, name="w1_codes0", align_bytes=64)]
         w1_codes += [keep.tile([P, P * (hi - lo)], U32, name=f"w1_codes{lo}", align_bytes=64) for lo, hi in w1_groups[1:]]
         w1_scales = [keep.tile([P, P * (hi - lo)], U8, name=f"w1_scales{lo}", align_bytes=64) for lo, hi in w1_groups]
-        dealt_at = scale_at + T
+        dealt_at = y_at + list_bytes
         w1_bf = [
             shared.tile([P, 1, H], BF16, name=f"w1_bf{lo}", align_bytes=64, offset=dealt_at + (1 - lo) * 6 * list_bytes // 4)
             if lo < 2
@@ -123,7 +117,8 @@ def tile_picked_tworoute_gelu_po_kernel(
 
         round_w1(0, 0, nc.vector.tensor_copy)
         round_w1(0, 1, nc.scalar.copy)
-        round_w1(0, 2, nc.vector.tensor_copy)
+        round_w1(0, 2, nc.vector.tensor_copy, slice(0, P // 2))
+        round_w1(0, 2, nc.scalar.copy, slice(P // 2, P))
         wb_t = shared.tile([P, V], F32, align_bytes=64, offset=0)
         wa_t = shared.tile([P, V], F32, align_bytes=64, offset=list_bytes)
         nc.sync.dma_start(out=wb_t[:], in_=wb.rearrange("(p t) v -> p t v", t=PACK)[:, 0, :])
@@ -135,6 +130,11 @@ def tile_picked_tworoute_gelu_po_kernel(
         for g in range(len(w1_groups)):
             quantise_w1(g)
 
+        w2_scale_dealt = shared.tile([P, N], U8, align_bytes=64, offset=dealt_at + 6 * list_bytes // 4 + N)
+        nc.vector.tensor_copy(
+            out=w2_scale_dealt[:].rearrange("p (t m) -> p t m", t=PACK),
+            in_=w2_scale_raw[:].rearrange("p (m t) -> p t m", t=PACK),
+        )
         w2_scale_mm = shared.tile([P, N], U8, align_bytes=64, offset=dealt_at + 6 * list_bytes // 4)
         nc.vector.memset(w2_scale_mm[:].bitcast(I32), 0)
         for r in range(QUADS):

@@ -146,14 +146,15 @@ def tile_picked_tworoute_gelu_po_kernel(
         y = [keep.tile([P, S], F32, name=f"y{t}") for t in range(PACK)]
 
         def project(t):
-            edges = (0, HALF, S)
+            edges = (0, CHUNK, S - CHUNK, S) if t == PACK - 1 else (0, HALF, S)
             for lo, hi in zip(edges, edges[1:]):
                 cols = slice(lo, hi)
                 bank = psum.tile([P, S], F32, name="bank")
                 g = min(t, 2)
                 w_cols = slice(P * (t - g), P * (t - g + 1))
                 mx(bank[:, 0 : hi - lo], w1_codes[g][:, w_cols], w1_scales[g][:, w_cols], x_word_pick[:, cols], x_scale_mm[:, cols])
-                nc.scalar.copy(out=y[t][:, cols], in_=bank[:, 0 : hi - lo])
+                copy = nc.vector.tensor_copy if hi == CHUNK else nc.scalar.copy
+                copy(out=y[t][:, cols], in_=bank[:, 0 : hi - lo])
 
         z = [keep.tile([P, S], F32, name=f"z{t}") for t in range(PACK)]
         y_a_odd = keep.tile([P, 2, V], F32)
@@ -177,12 +178,15 @@ def tile_picked_tworoute_gelu_po_kernel(
         def put_b(t):
             nc.scalar.activation(out=z[t][:].indirect(lb_t[:]), in_=b[t][:], func=COPY)
 
-        for t in range(PACK):
-            project(t)
+        project(0)
+        project(1)
+        nc.scalar.activation(out=y_a[0][:, V // 2 : V], in_=y[0][:].indirect(la_t[:, V // GROUP // 2 : V // GROUP]), func=COPY)
+        project(2)
+        project(3)
         w2_words_by_slot = w2_word_raw[:].bitcast(U32).rearrange("p (m t) -> p m t", t=PACK)
         w2_codes_rest = shared.tile([P, PACK - 1, P], U32, align_bytes=64, offset=dealt_at)
         nc.vector.tensor_copy(out=w2_codes_rest[:].rearrange("p t m -> p m t"), in_=w2_words_by_slot[:, :, 1:PACK])
-        nc.vector.tensor_copy(out=y_a[0], in_=y[0][:].indirect(la_t[:]))
+        nc.vector.tensor_copy(out=y_a[0][:, 0 : V // 2], in_=y[0][:].indirect(la_t[:, 0 : V // GROUP // 2]))
         for t in (0, 1, 2, 3):
             fetch_b(t)
         gelu(0)

from contextlib import ExitStack

import concourse.mybir as mybir

K, T, S, V, N, H = 512, 2048, 512, 256, 512, 512
FLOPS = 2 * K * H * S + 2 * H * N * S

F32 = mybir.dt.float32
BF16 = mybir.dt.bfloat16
I32 = mybir.dt.int32
U32 = mybir.dt.uint32
U16 = mybir.dt.uint16
U8 = mybir.dt.uint8
FP8X4 = mybir.dt.float8_e4m3fn_x4
GELU = mybir.ActivationFunctionType.Gelu_apprx_tanh
COPY = mybir.ActivationFunctionType.Copy
MULT = mybir.AluOpType.mult

P = 128
PACK = 4
QUADS = 4
GROUP = 16
BANKS = 8
HALF = S // 2
CHUNK = 128
CHUNKS = S // CHUNK


def tile_picked_tworoute_gelu_po_kernel(
    tc, x_words, x_scales, w1, wa, wb, w2_words, w2_scales, offs, la, lb, out_0, out_1, out_2
):
    nc = tc.nc
    with ExitStack() as ctx:
        keep = ctx.enter_context(tc.tile_pool(name="keep", bufs=1))
        shared = ctx.enter_context(tc.tile_pool(name="shared", bufs=1))
        psum = ctx.enter_context(tc.psum_pool(name="psum", bufs=BANKS))
        list_bytes = 4 * V
        y_at = 4 * T

        def mx(out, w_codes, w_scales, a_codes, a_scales):
            nc.tensor.matmul_mx(
                out=out,
                lhsT=w_codes.bitcast(FP8X4),
                lhsT_scale=w_scales,
                rhs=a_codes.bitcast(FP8X4),
                rhs_scale=a_scales,
                start=True,
                stop=True,
            )

        x_scale_table = keep.tile([P, T], U8, align_bytes=64)
        first_row = P - 4 * QUADS
        nc.scalar.dma_start(out=x_scale_table[first_row:P, :].bitcast(I32), in_=x_scales[0].bitcast(I32))
        w2_scale_raw = keep.tile([P, N], U8, align_bytes=64)
        nc.scalar.dma_start(out=w2_scale_raw[48:64, :].bitcast(I32), in_=w2_scales[0].bitcast(I32))
        table_in = keep.tile([P, 1], F32)
        table_out = keep.tile([P, 1], F32)
        nc.gpsimd.memset(table_in[:], 0.0)
        nc.scalar.activation(out=table_out[:], in_=table_in[:], func=GELU)

        nc.vector.memset(x_scale_table[0:96, :].bitcast(I32), 0)
        nc.gpsimd.memset(x_scale_table[96:first_row, :].bitcast(I32), 0)
        x_scale_mm = keep.tile([P, S], U8, align_bytes=64)
        nc.gpsimd.memset(x_scale_mm[:].bitcast(I32), 0)
        for lo, hi in ((0, 32), (32, 48), (64, P)):
            nc.gpsimd.memset(w2_scale_raw[lo:hi, :].bitcast(I32), 0)

        w1_rows = w1.rearrange("(p j) c -> p j c", j=PACK)
        w1_raw = [shared.tile([P, 2, H], F32, name="w1_raw0", align_bytes=64, offset=0), keep.tile([P, 2, H], F32, name="w1_raw1")]
        offs_t = keep.tile([P, S // GROUP], U16)
        la_t = keep.tile([P, V // GROUP], U16)
        lb_t = keep.tile([P, V // GROUP], U16)
        x_word_table = keep.tile([P, T], U32, align_bytes=64)

        nc.sync.dma_start(out=offs_t[:], in_=offs)
        nc.sync.dma_start(
            out=x_word_table[:].bitcast(I32), in_=x_words[0].rearrange("p c r -> p (c r)").bitcast(I32)
        )
        nc.sync.dma_start(out=w1_raw[0][:], in_=w1_rows[:, 0:2, :])
        nc.sync.dma_start(out=w1_raw[1][:], in_=w1_rows[:, 2:4, :])
        w2_word_raw = keep.tile([P, N], I32, align_bytes=64)
        nc.sync.dma_start(out=w2_word_raw[:], in_=w2_words[0].rearrange("p c r -> p (c r)").bitcast(I32))
        nc.sync.dma_start(out=lb_t[:], in_=lb)
        nc.sync.dma_start(out=la_t[:], in_=la)
        x_scale_pick = keep.tile([P, S], U8, align_bytes=64)
        nc.vector.tensor_copy(out=x_scale_pick[:], in_=x_scale_table[:].indirect(offs_t[:]))
        for r in range(QUADS):
            nc.scalar.dma_start(out=x_scale_mm[r:P:32, :].bitcast(I32), in_=x_scale_pick[first_row + r : P : 4, :].bitcast(I32))
        x_word_pick = keep.tile([P, S], U32, align_bytes=64)
        nc.vector.tensor_copy(out=x_word_pick[:], in_=x_word_table[:].indirect(offs_t[:]))

        w1_groups = ((0, 1), (1, 2), (2, 4))
        w1_codes = [keep.tile([P, P], U32, name="w1_codes0", align_bytes=64)]
        w1_codes += [keep.tile([P, P * (hi - lo)], U32, name=f"w1_codes{lo}", align_bytes=64) for lo, hi in w1_groups[1:]]
        w1_scales = [keep.tile([P, P * (hi - lo)], U8, name=f"w1_scales{lo}", align_bytes=64) for lo, hi in w1_groups]
        dealt_at = y_at + list_bytes
        w1_bf = [
            shared.tile([P, 1, H], BF16, name=f"w1_bf{lo}", align_bytes=64, offset=dealt_at + (1 - lo) * 6 * list_bytes // 4)
            if lo < 2
            else keep.tile([P, hi - lo, H], BF16, name=f"w1_bf{lo}", align_bytes=64)
            for lo, hi in w1_groups
        ]

        def round_w1(rows, g, copy, part=slice(0, P)):
            lo, hi = w1_groups[g]
            copy(
                out=w1_bf[g][:].rearrange("p u (m j) -> p m u j", j=PACK)[:, part, :, 2 * rows : 2 * rows + 2],
                in_=w1_raw[rows][:].rearrange("p j (m t) -> p m t j", t=PACK)[:, part, lo:hi],
            )

        def quantise_w1(g):
            nc.vector.quantize_mx(
                out=w1_codes[g][:].bitcast(FP8X4),
                scales=w1_scales[g][:],
                in_=w1_bf[g][:].rearrange("p u n -> p (u n)"),
            )

        round_w1(0, 0, nc.vector.tensor_copy)
        round_w1(0, 1, nc.scalar.copy)
        round_w1(0, 2, nc.vector.tensor_copy, slice(0, P // 2))
        round_w1(0, 2, nc.scalar.copy, slice(P // 2, P))
        wb_t = shared.tile([P, V], F32, align_bytes=64, offset=0)
        wa_t = shared.tile([P, V], F32, align_bytes=64, offset=list_bytes)
        nc.sync.dma_start(out=wb_t[:], in_=wb.rearrange("(p t) v -> p t v", t=PACK)[:, 0, :])
        nc.sync.dma_start(out=wa_t[:], in_=wa.rearrange("(p t) v -> p t v", t=PACK)[:, 0, :])
        round_w1(1, 0, nc.scalar.copy, slice(0, P // 2))
        round_w1(1, 0, nc.vector.tensor_copy, slice(P // 2, P))
        round_w1(1, 1, nc.vector.tensor_copy)
        round_w1(1, 2, nc.scalar.copy)
        for g in range(len(w1_groups)):
            quantise_w1(g)

        w2_scale_dealt = shared.tile([P, N], U8, align_bytes=64, offset=dealt_at + 6 * list_bytes // 4 + N)
        nc.vector.tensor_copy(
            out=w2_scale_dealt[:].rearrange("p (t m) -> p t m", t=PACK),
            in_=w2_scale_raw[:].rearrange("p (m t) -> p t m", t=PACK),
        )
        w2_scale_mm = shared.tile([P, N], U8, align_bytes=64, offset=dealt_at + 6 * list_bytes // 4)
        nc.vector.memset(w2_scale_mm[:].bitcast(I32), 0)
        for r in range(QUADS):
            nc.sync.dma_start(out=w2_scale_mm[r:P:32, :].bitcast(I32), in_=w2_scale_dealt[48 + r : 64 : 4, :].bitcast(I32))

        def placed(shape, dtype, name, place):
            return shared.tile(shape, dtype, name=name, align_bytes=64, offset=y_at + list_bytes * place)

        y = [keep.tile([P, S], F32, name=f"y{t}") for t in range(PACK)]

        def project(t):
            edges = (0, CHUNK, S - CHUNK, S) if t == PACK - 1 else (0, HALF, S)
            for lo, hi in zip(edges, edges[1:]):
                cols = slice(lo, hi)
                bank = psum.tile([P, S], F32, name="bank")
                g = min(t, 2)
                w_cols = slice(P * (t - g), P * (t - g + 1))
                mx(bank[:, 0 : hi - lo], w1_codes[g][:, w_cols], w1_scales[g][:, w_cols], x_word_pick[:, cols], x_scale_mm[:, cols])
                copy = nc.vector.tensor_copy if hi == CHUNK else nc.scalar.copy
                copy(out=y[t][:, cols], in_=bank[:, 0 : hi - lo])

        z = [keep.tile([P, S], F32, name=f"z{t}") for t in range(PACK)]
        y_a_odd = keep.tile([P, 2, V], F32)
        gelu_a_odd = keep.tile([P, 2, V], F32)
        y_a = [y_a_odd[:, t // 2, :] if t % 2 else keep.tile([P, V], F32, name=f"y_a{t}")[:] for t in range(PACK)]
        gelu_a = [gelu_a_odd[:, t // 2, :] if t % 2 else keep.tile([P, V], F32, name=f"gelu_a{t}")[:] for t in range(PACK)]
        b = [placed([P, V], F32, "b0", 0) if t == 0 else keep.tile([P, V], F32, name=f"b{t}") for t in range(PACK)]

        def fetch_b(t):
            nc.vector.tensor_tensor(out=b[t][:], in0=y[t][:].indirect(lb_t[:]), in1=wb_t[:], op=MULT)

        def fetch_a(t):
            nc.scalar.activation(out=y_a[t], in_=y[t][:].indirect(la_t[:]), func=COPY)

        def gelu(t):
            nc.scalar.activation(out=gelu_a[t], in_=y_a[t], func=GELU)

        def put_a(t):
            nc.vector.tensor_tensor(out=z[t][:].indirect(la_t[:]), in0=gelu_a[t], in1=wa_t[:], op=MULT)

        def put_b(t):
            nc.scalar.activation(out=z[t][:].indirect(lb_t[:]), in_=b[t][:], func=COPY)

        project(0)
        project(1)
        nc.scalar.activation(out=y_a[0][:, V // 2 : V], in_=y[0][:].indirect(la_t[:, V // GROUP // 2 : V // GROUP]), func=COPY)
        project(2)
        project(3)
        w2_words_by_slot = w2_word_raw[:].bitcast(U32).rearrange("p (m t) -> p m t", t=PACK)
        w2_codes_rest = shared.tile([P, PACK - 1, P], U32, align_bytes=64, offset=dealt_at)
        nc.vector.tensor_copy(out=w2_codes_rest[:].rearrange("p t m -> p m t"), in_=w2_words_by_slot[:, :, 1:PACK])
        nc.vector.tensor_copy(out=y_a[0][:, 0 : V // 2], in_=y[0][:].indirect(la_t[:, 0 : V // GROUP // 2]))
        for t in (0, 1, 2, 3):
            fetch_b(t)
        gelu(0)
        fetch_a(3)
        fetch_a(1)
        fetch_a(2)
        nc.scalar.activation(out=gelu_a_odd[:], in_=y_a_odd[:], func=GELU)
        gelu(2)
        put_a(0)
        put_a(3)
        put_b(1)
        put_b(0)
        put_a(2)
        put_a(1)
        put_b(3)
        put_b(2)
        w2_codes_first = placed([P, P], U32, "w2_codes_first", 0)
        nc.vector.tensor_copy(out=w2_codes_first[:], in_=w2_words_by_slot[:, :, 0])
        w2_codes = [w2_codes_first[:]] + [w2_codes_rest[:, t, :] for t in range(PACK - 1)]
        for u in range(3):
            idle_bank = psum.tile([P, S], F32, name="bank")
            mx(idle_bank[0:32, :], w2_codes_first[:, 0:32], w2_scale_mm[:, 0:32], w2_word_raw[:], w2_scale_mm[:])
        z_pairs = keep.tile([P, 2, S - CHUNK, 2], BF16, align_bytes=64)
        z_bf = [keep.tile([P, CHUNK, PACK], BF16, name=f"z_bf{c}", align_bytes=64) for c in range(CHUNKS)]
        pair_words = z_pairs[:].rearrange("p u n e -> p u (n e)").bitcast(U32)

        def round_first(t):
            nc.vector.tensor_copy(out=z_bf[0][:, :, t], in_=z[t][:, 0:CHUNK])

        def round_z(t, lo=CHUNK, hi=S):
            nc.vector.tensor_copy(out=z_pairs[:, t // 2, lo - CHUNK : hi - CHUNK, t % 2], in_=z[t][:, lo:hi])

        for t in (0, 3, 1):
            round_first(t)
            round_z(t)
        z_codes = keep.tile([P, S], U32, align_bytes=64)
        z_scales = keep.tile([P, S], U8, align_bytes=64)

        def weave(c, copy):
            copy(
                out=z_bf[c][:].rearrange("p n t -> p (n t)").bitcast(U32).rearrange("p (n u) -> p n u", u=2),
                in_=pair_words[:, :, CHUNK * (c - 1) : CHUNK * c].rearrange("p u n -> p n u"),
            )

        def quantise_z(c):
            cols = slice(CHUNK * c, CHUNK * (c + 1))
            nc.vector.quantize_mx(
                out=z_codes[:, cols].bitcast(FP8X4),
                scales=z_scales[:, cols],
                in_=z_bf[c][:].rearrange("p n t -> p (n t)"),
            )

        round_first(2)
        round_z(2, CHUNK, HALF)
        round_z(2, HALF, S)
        quantise_z(0)
        weave(1, nc.vector.tensor_copy)
        weave(2, nc.scalar.copy)
        weave(3, nc.scalar.copy)
        for c in range(1, CHUNKS):
            quantise_z(c)

        out_rows = out_0.rearrange("(p t) j -> p t j", t=PACK)
        out_words = out_1[0].rearrange("p c r -> p (c r)").bitcast(I32)
        o_codes = keep.tile([P, S], U32, align_bytes=64)
        o_scales = keep.tile([P, S], U8, align_bytes=64)
        o_bf = [keep.tile([P, CHUNK, PACK], BF16, name=f"o_bf{c}", align_bytes=64) for c in range(CHUNKS)]
        o_f32 = [keep.tile([P, PACK, HALF], F32, name=f"o_f32_{h}") for h in range(2)]

        def round_out(c, lo, hi, slots=slice(0, PACK), copy=nc.vector.tensor_copy):
            h, first = divmod(CHUNK * c, HALF)
            copy(
                out=o_bf[c][:, lo:hi, slots].rearrange("p (g i) t -> p g t i", i=4),
                in_=o_f32[h][:, slots, first + lo : first + hi].rearrange("p t (g i) -> p g t i", i=4),
            )

        def quantise_out(c, lo, hi):
            cols = slice(CHUNK * c + lo, CHUNK * c + hi)
            nc.vector.quantize_mx(
                out=o_codes[:, cols].bitcast(FP8X4),
                scales=o_scales[:, cols],
                in_=o_bf[c][:, lo:hi, :].rearrange("p n t -> p (n t)"),
            )

        last = CHUNKS - 1
        for c in range(CHUNKS):
            cols = slice(CHUNK * c, CHUNK * (c + 1))
            h, first = divmod(CHUNK * c, HALF)
            groups = ((0, 2), (2, 3), (3, 4))
            for lo, hi in groups:
                slots = slice(lo, hi)
                bank = psum.tile([P, S], F32, name="bank")
                for t in range(lo, hi):
                    w_cols = slice(P * t, P * (t + 1))
                    out_cols = slice(CHUNK * (t - lo), CHUNK * (t - lo + 1))
                    mx(bank[:, out_cols], w2_codes[t], w2_scale_mm[:, w_cols], z_codes[:, cols], z_scales[:, cols])
                copy = nc.vector.tensor_copy if lo == 2 and c < last else nc.scalar.copy
                copy(
                    out=o_f32[h][:, slots, first : first + CHUNK],
                    in_=bank[:, 0 : (hi - lo) * CHUNK].rearrange("p (t n) -> p t n", t=hi - lo),
                )
                if c == 0 and hi % 2 == 0:
                    pair = slice(hi - 2, hi)
                    nc.sync.dma_start(out=out_rows[:, pair, cols], in_=o_f32[0][:, pair, cols])
                if c == last and hi == 2:
                    round_out(c, 0, CHUNK, slots)
                    quantise_out(c - 1, 0, CHUNK)
            if c > 0:
                nc.sync.dma_start(out=out_rows[:, :, cols], in_=o_f32[h][:, :, first : first + CHUNK])
            if c < last:
                round_out(c, 0, CHUNK)
            else:
                round_out(c, 0, CHUNK // 2, slice(2, PACK))
                round_out(c, CHUNK // 2, CHUNK, slice(2, PACK), nc.scalar.copy)
            if 0 < c < last:
                quantise_out(c - 1, 0, CHUNK)
        early = CHUNK * last
        nc.sync.dma_start(out=out_words[:, 0:early], in_=o_codes[:, 0:early].bitcast(I32))
        quantise_out(last, 0, CHUNK // 2)
        quantise_out(last, CHUNK // 2, CHUNK)
        nc.sync.dma_start(out=out_words[:, early:S], in_=o_codes[:, early:S].bitcast(I32))
        for q in range(QUADS):
            queue = nc.scalar if q % 2 == 0 else nc.sync
            queue.dma_start(
                out=out_2[0, 4 * q : 4 * q + 4, :].bitcast(I32),
                in_=o_scales[32 * q : 32 * q + 4, :].bitcast(I32),
            )
